import numpy as np, ml_dtypes
CORES = [10,34,74,98]
N = 4
BF = ml_dtypes.bfloat16
def gentries(a):
    return np.ascontiguousarray(a.reshape(8, 16, -1).transpose(0, 2, 1)).reshape(8, -1)
def gtable(e):
    e = np.asarray(e); return np.ascontiguousarray(e.reshape(8, -1, 16).transpose(0, 2, 1)).reshape(128, -1).astype(np.int32)
C, K, A, V, S = 3072, 1024, 2, 3, 4
L = V * S
E = (V - 1) * S
def rock(rng, big=False):
    Q = C // 4; o = np.argsort(rng.random((N, 8, C)), axis=-1)
    a = np.where(rng.random((N, 8, 16, Q)) < 0.25, rng.integers(1, 3, (N, 8, 16, Q)), 0); a[:, :, 0] = rng.integers(0, 3, (N, 8, Q)); a[..., :Q // 16] = 0
    lv = [a]; pp = [rng.integers(0, Q // 16, (N, 8, Q))]
    for i in range(1, 4):
        j = rng.integers(0, Q, (N, 8, Q)); up = np.where(rng.random((N, 8, 16, Q)) < 0.15, rng.integers(1, 3, (N, 8, 16, Q)), 0); up[:, :, 0] = rng.integers(0, 3, (N, 8, Q))
        if big: up = up * rng.choice(np.array([1, 1, 2, 4]), (N, 8, 1, Q))
        lv.append(np.minimum(7, np.take_along_axis(lv[-1], j[:, :, None, :], 3) + up)); pp.append(j + (i - 1) * Q)
    fp = np.concatenate(lv, axis=3); pp = np.concatenate(pp, axis=2); inv = np.argsort(o, axis=-1)
    fm = np.ascontiguousarray(np.take_along_axis(fp, inv[:, :, None, :], 3)); nx = rng.integers(0, C, (N, 8, 16, C))
    nx[:, :, 0] = np.take_along_axis(o, np.take_along_axis(pp, inv, 2), 2)
    return fm, nx
def melts(rng):
    b = np.where(rng.random((N, 8, 16, K)) < 0.1, rng.integers(0, 4, (N, 8, 16, K)), rng.integers(4, 44, (N, 8, 16, K))); b[:, :, 0] = rng.integers(0, 16, (N, 8, K))
    w = np.where(rng.random((N, 8, 16, A * K)) < 0.5, rng.integers(0, 9, (N, 8, 16, A * K)), 0); w[:, :, 0] = rng.integers(0, 9, (N, 8, A * K))
    return b, w, rng.integers(0, C, (N, 8, K))
def link(fm, nx, g, a, form, row, after, partner):
    fm[:, g, :, a] = form; nx[:, g, row, a] = after; nx[:, g, 0, a] = partner
def mend(fm, nx, zs):
    low = np.take_along_axis(fm, nx[:, :, :1], 3)
    nx[:, :, 0] = np.where(np.any(low > fm, axis=2), np.array(zs).reshape(1, 8, 1), nx[:, :, 0])
def pack(fm, nx, w, b, m):
    return {"fm": np.ascontiguousarray(fm.reshape(N, 128, C)).astype(BF), "nx": np.ascontiguousarray(nx.reshape(N, 128, C)).astype(np.int32), "wl": np.ascontiguousarray(w.reshape(N, 128, A * K)).astype(BF),
            "b0": np.ascontiguousarray(b.reshape(N, 128, K)).astype(BF), "m0": np.stack([gtable(a) for a in m])}
def setup_inputs(rng):
    fm, nx = rock(rng); b, w, m = melts(rng)
    return pack(fm, nx, w, b, m)
def setup_inputs_spread(rng):
    fm, nx = rock(rng, True); b, w, m = melts(rng)
    b = np.minimum(255, (np.exp2(8 * rng.random((N, 8, 1, K))) * rng.random((N, 8, 16, K))).astype(np.int64))
    b[:, :, 0] = np.minimum(255, (np.exp2(8 * rng.random((N, 8, K)) * rng.random((N, 8, K))) - 1).astype(np.int64))
    w = np.minimum(255, (np.exp2(8 * rng.random((N, 8, 1, A * K))) * rng.random((N, 8, 16, A * K)) * rng.random((N, 8, 16, A * K))).astype(np.int64)) * (rng.random((N, 8, 1, A * K)) > 0.125)
    return pack(fm, nx, w, b, m)
def setup_inputs_ends(rng):
    full = rng.random((N, 8, 1, C)) < 0.3
    fm = 7 * (full | (rng.random((N, 8, 16, C)) < 0.3)).astype(np.int64)
    nx = np.where(rng.random((N, 8, 16, C)) < 0.75, (C - 1) * rng.integers(0, 2, (N, 8, 16, C)), rng.integers(0, C, (N, 8, 16, C))); nx[:, :, 0] = (C - 1) * rng.integers(0, 2, (N, 8, C))
    style = rng.integers(0, 4, (N, 8, 1, K)); rich = (np.arange(16) > 0).astype(np.int64).reshape(1, 1, 16, 1)
    b = 255 * np.where(style == 0, 0, np.where(style == 1, 1, np.where(style == 2, rng.integers(0, 2, (N, 8, 16, K)), rich)))
    w = 255 * rng.integers(0, 2, (N, 8, 16, A * K))
    m = np.where(rng.random((N, 8, K)) < 0.7, (C - 1) * rng.integers(0, 2, (N, 8, K)), rng.integers(0, C, (N, 8, K)))
    form = 7 * rich.reshape(16); zs = []
    for g in range(8):
        ch = [C - 1 - 2 * i for i in range(E - 1)] + [C - 2, 1]; z = 0; h = 1; half = 2
        idle = [3 + i for i in range((V - 3) * S)]
        if g % 2 == 1:
            ch = [C - 1 - a for a in ch]; z = C - 1; h = C - 2; half = C - 3; idle = [C - 1 - a for a in idle]
        for i in range(E): link(fm, nx, g, ch[i], form, 15, ch[i + 1], z)
        link(fm, nx, g, z, np.zeros(16, np.int64), 15, rng.integers(0, C, N), z)
        link(fm, nx, g, h, np.full(16, 7), 15, z, z)
        link(fm, nx, g, half, 7 * (np.arange(16) > 7), 15, ch[0], z)
        nx[:, g, 0, ch[E - 1]] = half; zs.append(z)
        way = idle + [ch[E - S]]
        for i in range(len(idle)): link(fm, nx, g, way[i], np.full(16, 7), 15, z, way[i + 1])
        pk = rng.permutation(K)
        ks = np.unique(np.concatenate([np.array([0, K // 2, K - 1]), pk[:K // 4]]))
        kc = np.setdiff1d(pk[K // 4:K // 4 + K // 16], ks); ka = np.concatenate([ks, kc])
        b[:, g, 0, ka] = 0; b[:, g, 1:, ka] = 255; m[:, g, ks] = ch[0]; m[:, g, kc] = way[0]
        for j in range(A):
            w[:, g, 0, j * K + ka] = 0; w[:, g, 1:, j * K + ka] = 255
    mend(fm, nx, zs)
    return pack(fm, nx, w, b, m)
def setup_inputs_corners(rng):
    fm, nx = rock(rng); b, w, m = melts(rng)
    u = rng.random(nx.shape); nx = np.where(u < 0.04, np.arange(C), np.where(u < 0.08, 0, np.where(u < 0.12, C - 1, nx)))
    kind = rng.integers(0, 3, (N, 8, 1, A * K)); w = np.where(kind == 0, 0, np.where(kind == 1, 255, rng.integers(0, 256, (N, 8, 16, A * K)))); w[:, :, 0] = rng.integers(0, 2, (N, 8, A * K))
    cls = rng.integers(0, 6, (N, 8, K)); cls[:, 7] = 4; cls[:, 7, 0] = 5; cls[:, 6] = 0; cls[:, 5] = 1; cls[:, :, K - 1] = np.arange(8) % 6
    rich = (np.arange(16) > 0).astype(np.int64).reshape(1, 1, 16, 1); c4 = cls[:, :, None, :]
    b = np.where(c4 == 0, 255, np.where(c4 == 1, 0, np.where(c4 == 2, b, 255 * rich)))
    m[:, 4] = rng.integers(0, C, (N, 1)); m[:, 5] = rng.integers(0, C, (N, 1)); m[:, 3, ::2] = 0; m[:, 3, 1::2] = C - 1; zs = []
    for g in range(8):
        nm = [int(a) for a in rng.permutation(C)[:L + 1]]; z = nm[L]; h = nm[L - 1]
        for i in range(L - 1): link(fm, nx, g, nm[i], rich.reshape(16), 15, nm[i + 1], z)
        link(fm, nx, g, h, 7 * (np.arange(16) == 0), 15, nm[0], z)
        link(fm, nx, g, z, np.zeros(16, np.int64), 15, rng.integers(0, C, N), z)
        zs.append(z); m[:, g] = np.where(cls[:, g] == 4, nm[0], np.where(cls[:, g] == 5, nm[1], m[:, g]))
    mend(fm, nx, zs)
    return pack(fm, nx, w, b, m)
def setup_inputs_calm(rng):
    fm, nx = rock(rng); b, w, m = melts(rng); w[:, :, 0] = rng.integers(0, 2, (N, 8, A * K)); zs = []
    part = rng.random((N, 8, K)); part[:, :, 0] = 0.0; part[:, :, K - 1] = 0.0
    still = rng.integers(20, 61, (N, 8, 16, K)); still[:, :, 0] = 0; still[:, :, 5] = 0
    b = np.where((part < 0.8)[:, :, None, :], still, b); r16 = np.arange(16)
    for g in range(8):
        j = g % 4; nm = [int(a) for a in rng.permutation(C)[:E + 3]]; h, q, z = nm[E], nm[E + 1], nm[E + 2]
        for i in range(E):
            if i < E - j: link(fm, nx, g, nm[i], 3 * (r16 == 5), 5, nm[i + 1], z)
            else: link(fm, nx, g, nm[i], ((r16 != 0) & (r16 != 5)).astype(np.int64), 15, nm[i + 1], z)
        link(fm, nx, g, h, 7 * (r16 == 0), 15, nm[0], q)
        link(fm, nx, g, q, 3 * (r16 == 0), 15, nm[0], z)
        link(fm, nx, g, z, np.zeros(16, np.int64), 15, rng.integers(0, C, N), z)
        zs.append(z); any_ = np.array(nm)[rng.integers(0, E + 1, (N, K))]
        m[:, g] = np.where(part[:, g] < 0.6, nm[0], np.where(part[:, g] < 0.8, any_, m[:, g]))
    mend(fm, nx, zs)
    return pack(fm, nx, w, b, m)
def check_inputs(d):
    bad = []
    for k, lo, hi in (("fm", 0, 7), ("nx", 0, C - 1), ("wl", 0, 255), ("b0", 0, 255), ("m0", 0, C - 1)):
        v = np.asarray(d[k]).astype(np.float64)
        if not (np.min(v) >= lo and np.max(v) <= hi): bad.append("range of " + k)
        if np.any(v != np.floor(v)): bad.append("whole numbers of " + k)
    fm = np.asarray(d["fm"]).astype(np.float32).reshape(N, 8, 16, C); p0 = np.clip(np.asarray(d["nx"]).astype(np.int64).reshape(N, 8, 16, C)[:, :, :1], 0, C - 1)
    if np.any(np.take_along_axis(fm, p0, 3) > fm): bad.append("partners in nx that are richer than their minerals in fm")
    return bad
def at(a, ix):
    return np.take_along_axis(a, ix[:, :, None, :], 3)
def one(a, ix):
    return np.take_along_axis(a, ix[:, :, None, :], 2)[:, :, 0]
def reference(fm, nx, wl, b0, m0):
    F = fm.astype(np.int64).reshape(N, 8, 16, C); X = nx.astype(np.int64).reshape(N, 8, 16, C); wall = wl.astype(np.int64).reshape(N, 8, 16, A * K)
    B = b0.astype(np.int64).reshape(N, 8, 16, K); m = np.stack([gentries(a) for a in m0]).astype(np.int64)
    lg = np.full((N, 8, L, K), -1, np.int64); n = np.zeros((N, 8, K), np.int64); c = np.full((N, 8, K), -1, np.int64)
    for v in range(V):
        if v > 0:
            B, m, lg, n, c = [np.roll(a, 1, axis=0) for a in (B, m, lg, n, c)]
            has = c >= 0; col = (one(lg, np.maximum(c, 0)) & (A - 1)) * K + np.arange(K)
            B = np.minimum(255, B + np.where(has[:, :, None, :], at(wall, col), 0))
            if v < V - 1:
                keep = np.ones((N, 8, A * K), np.int64); np.put_along_axis(keep, col, np.where(has, 0, 1), 2)
                wall = wall * keep[:, :, None, :]
        for s in range(S):
            f = at(F, m); short = B < f
            ok = ~np.any(short, axis=2); back = short[:, :, 0] & ~np.any(short[:, :, 1:], axis=2) & (c >= 0)
            B = B - np.where(ok[:, :, None, :], f, 0)
            low = B < f; p = np.where(np.any(low, axis=2), np.argmax(low, axis=2), 15)
            after = one(at(X, m), p)
            t = np.where(back, one(lg, np.maximum(c, 0)), m); pi = np.take_along_axis(X[:, :, 0], t, 2)
            B = B + np.where(back[:, :, None, :], at(F, t) - at(F, pi), 0)
            slot = np.where(ok, n, np.maximum(c, 0)); new = np.where(ok, m, np.where(back, pi, one(lg, slot)))
            np.put_along_axis(lg, slot[:, :, None, :], new[:, :, None, :], 2)
            c = np.where(ok, n, np.where(back, c - 1, c)); n = n + ok; m = np.where(back, m, after)
    return {"yb": B.reshape(N, 128, K).astype(np.float32), "yl": np.stack([gtable(a.reshape(8, L * K)) for a in lg]).astype(np.float32),
            "ym": np.stack([gtable(a) for a in m]).astype(np.float32), "yc": np.stack([gtable(a) for a in c]).astype(np.float32)}

@@ -1,0 +1,785 @@
+from concourse.mybir import AluOpType, ActivationFunctionType
+
+C = 3072
+CP = C + 16
+K = 1024
+H = 2
+KH = K // H
+JH = KH // 16
+NV, NS = 3, 4
+NL = NV * NS
+LW = NL * JH
+BW = KH + 3 * JH
+OFF = 2047.0
+NF32, NI32, NU16, NF16, NB16 = 560, 64, 96, 64, 80
+
+SCRATCH = {
+    "F": ("sbuf", [128, C], "bfloat16"), "F1": ("sbuf", [128, C], "bfloat16"), "F2": ("sbuf", [128, C], "bfloat16"),
+    "G": ("sbuf", [128, 2 * CP + 16], "bfloat16"), "NX": ("sbuf", [128, C], "int32"),
+    "W": ("sbuf", [128, 2 * K + 16], "bfloat16"), "B0": ("sbuf", [128, K], "bfloat16"), "M0": ("sbuf", [128, 64], "int32"),
+    "P1": ("sbuf", [128, 2, 6, 16], "int32"), "P2": ("sbuf", [128, 6, 32], "float32"), "P3": ("sbuf", [128, 6, 32], "float32"),
+    "PL": ("sbuf", [128, 192], "uint16"),
+    "ci": ("sbuf", [128, 16], "int32"), "cf": ("sbuf", [128, 16], "float32"),
+    "ix": ("sbuf", [128, 144], "float32"), "ig": ("sbuf", [128, 128], "float32"),
+    "t0": ("sbuf", [128, 128], "float32"), "t1": ("sbuf", [128, 128], "float32"), "t2": ("sbuf", [128, 128], "float32"),
+    "t3": ("sbuf", [128, 128], "float32"), "t4": ("sbuf", [128, 128], "float32"),
+    "EZ": ("sbuf", [128, 144], "bfloat16"), "ER": ("sbuf", [128, 144], "float16"),
+    "IB": ("sbuf", [128, 128], "bfloat16"), "IC": ("sbuf", [128, 128], "bfloat16"),
+    "NB": ("sbuf", [128, 128], "bfloat16"), "BC": ("sbuf", [128, K], "bfloat16"), "FG": ("sbuf", [128, K], "bfloat16"),
+    "IH": ("sbuf", [128, 128], "float16"), "L0": ("sbuf", [128, H * NS * JH], "float16"),
+    "M1": ("sbuf", [128, 128], "bfloat16"), "M2": ("sbuf", [128, 128], "bfloat16"),
+    "PLC": ("sbuf", [128, LW], "bfloat16"), "COFF": ("sbuf", [128, LW], "float16"), "CEMP": ("sbuf", [128, LW], "float16"),
+    "KI": ("sbuf", [128, 64], "float32"), "KJ": ("sbuf", [128, 64], "float32"),
+    "BI": ("sbuf", [128, 24], "float32"), "BO": ("sbuf", [128, 24], "uint16"),
+    "zf": ("sbuf", [128, JH], "float32"), "zb": ("sbuf", [128, JH], "bfloat16"),
+    "zh": ("sbuf", [128, JH], "float16"), "oh": ("sbuf", [128, JH], "float16"),
+    "lf": ("sbuf", [128, NF32 * JH], "float32"), "li": ("sbuf", [128, NI32 * JH], "int32"),
+    "lu": ("sbuf", [128, NU16 * JH], "uint16"), "lh": ("sbuf", [128, NF16 * JH], "float16"), "lb": ("sbuf", [128, NB16 * JH], "bfloat16"),
+    "S1": ("sbuf", [128, K], "bfloat16"), "S2": ("sbuf", [128, K], "bfloat16"), "XG": ("sbuf", [128, K], "float32"),
+    "GG": ("sbuf", [128, K], "bfloat16"), "Y": ("sbuf", [128, K], "float16"),
+    "XS": ("sbuf", [128, K], "float16"), "BA": ("sbuf", [128, K], "bfloat16"), "BB": ("sbuf", [128, K], "bfloat16"),
+    "MA": ("sbuf", [128, H * LW], "bfloat16"), "MB": ("sbuf", [128, H * LW], "bfloat16"),
+    "U": ("sbuf", [128, H * LW], "float16"), "R": ("sbuf", [128, H * LW], "float16"), "U2": ("sbuf", [128, H * LW], "float32"),
+    "SB": ("sbuf", [128, 2 * H * BW], "bfloat16"), "LB": ("sbuf", [128, 2 * H * BW], "bfloat16"), "N2": ("sbuf", [128, 128], "bfloat16"),
+    "SL": ("sbuf", [128, 2 * H * 16 * JH], "float16"), "LL": ("sbuf", [128, 2 * H * 16 * JH], "float16"),
+    "OB": ("sbuf", [128, K], "float32"), "OL": ("sbuf", [128, NL, 64], "float32"),
+    "OM": ("sbuf", [128, 64], "float32"), "OC": ("sbuf", [128, 64], "float32"),
+}
+for _h in range(H):
+    for _n in ("PP", "PB", "PG", "PS"):
+        SCRATCH["%s%d" % (_n, _h)] = ("psum", [128, 512], "float32")
+
+NDMA = 40
+SEMAPHORES = ["cv", "ca", "cp", "cg", "sent"] + ["d%d" % i for i in range(NDMA)] + ["r%d" % i for i in range(8 * H)]
+
+ALU = AluOpType
+ACT = ActivationFunctionType
+CY = 0.001
+PCY = 0.0005
+HOP = 0.25
+OWN = 0.07
+OPT = {"s1": "g", "s2": "a", "bv": "a", "gu": True, "gm": False, "lead": 3.5, "win": 0.2, "split": 2, "seed": 4639, "jit": 0.5,
+       "early": True, "lam": 30.0, "hold": 14.0, "late": True, "f2": 1.0, "rounds": 12000}
+
+
+def build(g, T, topo, core, rank):
+    ops = []
+    cur = [None]
+    cores = list(T.cores)
+    nxt = cores[(rank + 1) % len(cores)]
+    rid, pid, _se = topo.addr(nxt)
+    emask = topo.mask(core, nxt)
+    neng = len(topo.engines(cores[(rank - 1) % len(cores)], core))
+    nsend = len(topo.engines(core, nxt))
+    V, A, PE = g.vector, g.scalar, g.tensor
+
+    def add(eng, fn, cost, r=(), w=(), x=(), kind="c", lat=0.0, sem=None, cnt=0):
+        ops.append({"eng": eng, "fn": fn, "cost": cost, "r": list(r), "w": list(w), "x": list(x), "kind": kind,
+                    "lat": lat, "sem": sem, "cnt": cnt, "h": cur[0]})
+
+    used = {"lf": 0, "li": 0, "lu": 0, "lh": 0, "lb": 0}
+
+    def slot(pool):
+        i = used[pool]
+        used[pool] += 1
+        return (T[pool][:, i * JH:(i + 1) * JH], "%s%d" % (pool, i), i * JH)
+
+    def tt(out, a, b, op, n=JH, f=2.0, x=()):
+        add("v", lambda: V.tensor_tensor(out[0], a[0], b[0], op), max(64, n * f) * CY, [a[1], b[1]], [out[1]], x)
+
+    def ts(out, a, s1, o0, s2=None, o1=None, n=JH, f=1.0, x=(), r=()):
+        if o1 is None:
+            fn = lambda: V.tensor_scalar(out[0], a[0], s1, None, o0)
+        else:
+            fn = lambda: V.tensor_scalar(out[0], a[0], s1, s2, o0, o1)
+        add("v", fn, max(64, n * f) * CY, [a[1]] + list(r), [out[1]], x)
+
+    def cp(out, a, n=JH):
+        add("v", lambda: V.tensor_copy(out[0], a[0]), max(64, n) * CY, [a[1]], [out[1]])
+
+    def gtt(out, win, off, b, op, n):
+        add("v", lambda: V.tensor_tensor(out[0], win[0].indirect(off[0]), b[0], op), 0.06 + 1.56 * n * CY,
+            list(win[1]) + [off[1], b[1]], [out[1]])
+        ops[-1]["gn"] = n
+
+    def act(out, a, func, bias=0.0, scale=1.0, n=JH, x=()):
+        add("a", lambda: A.activation(out[0], a[0], func, bias=bias, scale=scale), max(64, n) * CY + 0.02, [a[1]], [out[1]], x)
+
+    def gact(out, win, off, func, bias, scale, n):
+        add("a", lambda: A.activation(out[0], win[0].indirect(off[0]), func, bias=bias, scale=scale), 0.08 + 1.56 * n * CY,
+            list(win[1]) + [off[1]], [out[1]])
+        ops[-1]["gn"] = n
+
+    def mm(items, r, w, bank, alone=False, cont=False, keep=False):
+        def fn():
+            last = None
+            for i, (o, l, rh, _n) in enumerate(items):
+                if alone:
+                    last = PE.matmul(o, l, rh, True, True)
+                else:
+                    last = PE.matmul(o, l, rh, (i == 0) and not cont, i == len(items) - 1 and not keep)
+            return last
+        add("p", fn, sum(max(64, it[3]) for it in items) * PCY + 0.05, r, w, [bank])
+
+    ndma = [0]
+
+    def dma(q, out, in_, r, w, nbytes):
+        s = "d%d" % ndma[0]
+        ndma[0] += 1
+        e = {"s": g.sync, "a": g.scalar}[q]
+        add(q, lambda: e.dma_start(out, in_), 0.06, r, w, kind="d", lat=2.0, sem=s, cnt=16)
+        ops[-1]["bytes"] = nbytes
+
+    def gop(fn, n, w):
+        add("g", fn, 0.13 + 2 * n * CY, [], w)
+
+    NFP = 2
+    fw = C // NFP
+    dma("a", T.M0[:], T.m0[:], [], ["M0"], 128 * 256)
+    for gr in range(8):
+        q, hh = gr // 2, gr % 2
+        if gr == 1:
+            dma("s", T.F[:, 0:fw], T.fm[:, 0:fw], [], ["F0"], 128 * fw * 2)
+        dma("as"[hh], T.P1[32 * q:32 * q + 32, hh], T.nx[16 * gr, :], [], ["P1_%d" % gr], C * 4)
+    dma("s", T.F[:, fw:C], T.fm[:, fw:C], [], ["F1"], 128 * fw * 2)
+    for h in range(H):
+        dma("a", T.B0[:, h * KH:(h + 1) * KH], T.b0[:, h * KH:(h + 1) * KH], [], ["B0%d" % h], 128 * KH * 2)
+    dma("s", T.NX[:, 0:C // 2], T.nx[:, 0:C // 2], [], ["NX0"], 128 * C * 2)
+    dma("a", T.NX[:, C // 2:C], T.nx[:, C // 2:C], [], ["NX1"], 128 * C * 2)
+    dma("s", T.W[:, 0:2 * K], T.wl[:], [], ["W"], 128 * 2 * K * 2)
+    FT = ["F%d" % i for i in range(NFP)]
+
+    gop(lambda: g.iota(T.ci[:, 0:1], [[0, 1]], 0, 1), 1, ["ci0"])
+    gop(lambda: g.iota(T.ix[:], [[1, 144]], 0, 0, allow_small_or_imprecise_dtypes=True), 144, ["ix"])
+    gop(lambda: g.iota(T.ig[:], [[16, 8], [0, 16]], 0, 0, allow_small_or_imprecise_dtypes=True), 128, ["ig"])
+    gop(lambda: g.iota(T.PLC[:], [[1, NL], [0, JH]], 1, 0, allow_small_or_imprecise_dtypes=True), LW, ["PLC"])
+    gop(lambda: g.iota(T.KI[:], [[16, 64]], 0, 0, allow_small_or_imprecise_dtypes=True), 64, ["KI"])
+    gop(lambda: g.iota(T.BI[:], [[0, 12], [16, 2]], 0, 0, allow_small_or_imprecise_dtypes=True), 24, ["BI"])
+
+    def ci(i):
+        return (T.ci[:, i:i + 1], "ci%d" % i)
+
+    def cf(i):
+        return (T.cf[:, i:i + 1], "cf%d" % i)
+
+    def whole(name):
+        return (T[name][:], name)
+
+    ts(ci(1), ci(0), 15, ALU.bitwise_and)
+    ts(ci(2), ci(0), 112, ALU.bitwise_and)
+    cp(cf(0), ci(0))
+    cp(cf(1), ci(1))
+    cp(cf(2), ci(2))
+    ts(cf(3), cf(2), 15.0, ALU.add)
+    ts(cf(4), cf(1), 0.0, ALU.is_gt, 2.0 * CP, ALU.mult)
+    ts(cf(5), cf(4), 2.0 * CP, ALU.add)
+    ts(cf(6), cf(1), 15.0, ALU.is_equal, 328.0, ALU.mult)
+    ts(cf(7), cf(6), -128.0, ALU.add)
+    ts(cf(8), cf(1), 15.0, ALU.is_equal, -0.5, ALU.mult)
+    for q, o in ((9, 0.0), (11, 128.0)) + (((14, -128.0),) if "t" in OPT["s1"] else ()):
+        ts(cf(13), cf(1), 15.0, ALU.is_equal, 1000.0, ALU.mult)
+        ts(cf(q + 1), cf(13), -o, ALU.add)
+        ts(cf(q), cf(q + 1), 256.0, ALU.mult, -128.0, ALU.add)
+    ixs = (T.ix[:, 0:128], "ix")
+    ts(whole("EZ"), whole("ix"), cf(3)[0], ALU.is_equal, cf(5)[0], ALU.mult, n=144, r=["cf3", "cf5"])
+    ts(whole("IC"), ixs, cf(0)[0], ALU.is_equal, -1.0 * CP, ALU.mult, n=128, r=["cf0"])
+    ts(whole("t0"), whole("ig"), cf(2)[0], ALU.is_equal, n=128, r=["cf2"])
+    ts(whole("t1"), ixs, cf(0)[0], ALU.is_equal, n=128, r=["cf0"])
+    ts(whole("t2"), ixs, cf(0)[0], ALU.is_gt, n=128, r=["cf0"])
+    ts(whole("t3"), whole("t1"), 16.0, ALU.mult, -1.0, ALU.add, n=128)
+    ts(whole("t4"), whole("t2"), -14.0, ALU.mult, n=128)
+    tt(whole("t3"), whole("t3"), whole("t4"), ALU.add, n=128)
+    tt(whole("M1"), whole("t3"), whole("t0"), ALU.mult, n=128)
+    tt(whole("t4"), whole("t1"), whole("t2"), ALU.subtract, n=128)
+    ts(whole("t2"), whole("t4"), cf(8)[0], ALU.add, n=128, r=["cf8"])
+    tt(whole("M2"), whole("t2"), whole("t0"), ALU.mult, n=128)
+    ts(whole("ER"), whole("ix"), cf(3)[0], ALU.is_equal, 4096.0, ALU.mult, n=144, r=["cf3"])
+    cp(whole("IB"), whole("t1"), 128)
+    cp(whole("IH"), whole("t1"), 128)
+    ts(whole("NB"), whole("t1"), -1.0, ALU.mult, n=128)
+    ts(whole("N2"), whole("t1"), -2.0, ALU.mult, n=128)
+    ts(whole("COFF"), whole("PLC"), 0.0, ALU.mult, OFF, ALU.add, n=LW, f=0.5)
+    ts(whole("CEMP"), whole("PLC"), 0.0, ALU.mult, -OFF - 1.0, ALU.add, n=LW, f=0.5)
+    ts(whole("KJ"), whole("KI"), cf(1)[0], ALU.add, n=64, r=["cf1"])
+    ts(whole("BO"), whole("BI"), cf(1)[0], ALU.add, n=24, r=["cf1"])
+    add("v", lambda: V.memset(T.zf[:], 0.0), 64 * CY, [], ["zf"])
+    add("v", lambda: V.memset(T.zb[:], 0.0), 64 * CY, [], ["zb"])
+    ts(whole("oh"), whole("zf"), 1.0, ALU.add)
+    add("v", lambda: V.memset(T.G[:, C:CP], 0.0), 64 * CY, [], ["Gz0"])
+    add("v", lambda: V.memset(T.G[:, CP + C:2 * CP + 16], 0.0), 64 * CY, [], ["Gz1"])
+    add("v", lambda: V.memset(T.W[:, 2 * K:2 * K + 16], 0.0), 64 * CY, [], ["Wz"])
+    for v in range(2):
+        for h in range(H):
+            o = (v * H + h) * 16 * JH
+            wv = NS * (v + 1)
+            cp((T.LL[:, o + (4 + wv) * JH:o + 16 * JH], "LX%de" % (v * H + h)), (T.CEMP[:, 0:(NL - wv) * JH], "CEMP"), 128)
+
+    for i in range(NFP):
+        sl = slice(i * fw, (i + 1) * fw)
+        ts((T.G[:, sl], "GN%d" % i), (T.F[:, sl], "F%d" % i), -1.0, ALU.mult, n=fw, f=0.5)
+        if "g" in OPT["s1"] or "t" in OPT["s1"]:
+            act((T.F1[:, sl], "F1_%d" % i), (T.F[:, sl], "F%d" % i), ACT.Identity, bias=-128.0, n=fw)
+        if "g" in OPT["s2"]:
+            ts((T.F2[:, sl], "F2_%d" % i), (T.F[:, sl], "F%d" % i), 2.0, ALU.mult, cf(7)[0], ALU.add, n=fw, f=0.5, r=["cf7"])
+    for hh in range(2):
+        add("v", lambda hh=hh: V.tensor_copy(T.P2[:, :, 16 * hh:16 * hh + 16], T.P1[:, hh]), 96 * CY,
+            ["P1_%d" % (2 * q + hh) for q in range(4)], ["P2_%d" % hh])
+    for b in range(6):
+        add("v", lambda b=b: V.transpose(T.P3[:, b, :], T.P2[:, b, :]), 64 * CY, ["P2_0", "P2_1"], ["P3_%d" % b])
+        cp((T.PL[:, b::6], "PL%d" % b), (T.P3[:, b, :], "P3_%d" % b))
+    GN = ["GN%d" % i for i in range(NFP)]
+    NDP = 6
+    dw = C // NDP
+    for i in range(NDP):
+        add("v", lambda i=i: V.tensor_tensor(T.G[:, CP + i * dw:CP + (i + 1) * dw],
+                                             T.G[:, 0:C].indirect(T.PL[:, i * dw // 16:(i + 1) * dw // 16]),
+                                             T.F[:, i * dw:(i + 1) * dw], ALU.add),
+            0.06 + 1.56 * dw * CY, GN + FT + ["PL%d" % b for b in range(6)], ["GD%d" % i])
+    winF = (T.F[:], FT)
+    winF1 = (T.F1[:], ["F1_%d" % i for i in range(NFP)])
+    winF2 = (T.F2[:], ["F2_%d" % i for i in range(NFP)])
+    winG0 = (T.G[:, 0:CP], GN + ["Gz0"])
+    winG = (T.G[:], GN + ["Gz0", "Gz1"] + ["GD%d" % i for i in range(NDP)])
+    winX = (T.NX[:], ["NX0", "NX1"])
+    winW = (T.W[:], ["W", "Wz"])
+
+    def big(name, h, w=KH):
+        return (T[name][:, h * KH:h * KH + w], "%s%d" % (name, h))
+
+    def wide(name, h, blocks):
+        return (T[name][:, h * LW:h * LW + blocks * JH], "%s%d" % (name, h))
+
+    def spread(bank, col, src, blocks, one="IH"):
+        mm([(T[bank][:, col + s * JH:col + (s + 1) * JH], T[one][:], src[0], JH) for s in range(blocks)],
+           [one, src[1]], [bank + "w"], bank, alone=True)
+
+    def mask(h, st, blocks, name):
+        ps = "PS%d" % h
+        mk = wide(name, h, blocks)
+        if OPT["gm"]:
+            gtt(mk, (st["c1"][0], [st["c1"][1]]), (T.BO[:, 0:2 * blocks], "BO"), (T.PLC[:, 0:blocks * JH], "PLC"), ALU.is_equal, blocks * JH)
+            return mk
+        spread(ps, 128, st["c1"], blocks, "IB")
+        tt(mk, (T[ps][:, 128:128 + blocks * JH], ps + "w"), (T.PLC[:, 0:blocks * JH], "PLC"), ALU.is_equal, n=blocks * JH, f=1.0, x=[ps])
+        return mk
+
+    def first(h):
+        st = {}
+        m0 = (T.M0[:, h * JH:(h + 1) * JH], "M0")
+        st["m16"] = slot("lu")
+        cp(st["m16"], m0)
+        st["m"] = m0
+        st["B"] = big("B0", h)
+        st["e"] = whole("zf")
+        st["tn"] = whole("zf")
+        st["c1"] = whole("zf")
+        st["n1"] = whole("oh")
+        st["has"] = whole("zb")
+        st["M"] = None
+        st["L"] = ("L0", h * NS * JH, "L0%d" % h)
+        cp((T.L0[:, h * NS * JH:(h + 1) * NS * JH], "L0%d" % h), (T.CEMP[:, 0:NS * JH], "CEMP"), 64)
+        return st
+
+    def arrive(v, h, old):
+        st = {}
+        k = (v - 1) * H + h
+        o = k * 16 * JH
+        wv = NS * v
+        ll = "LL%d" % k
+
+        def part(i):
+            return (T.LL[:, o + i * JH:o + (i + 1) * JH], ll)
+        st["m16"] = slot("lu")
+        ts(st["m16"], part(0), OFF, ALU.add)
+        st["m"] = slot("lf")
+        ts(st["m"], part(0), OFF, ALU.add)
+        st["tn"] = part(1)
+        lj = ("LJ%d" if OPT["late"] else "LB%d") % k
+        st["c1"] = (T.LB[:, k * BW + KH + JH:k * BW + KH + 2 * JH], lj)
+        st["n1"] = (T.LB[:, k * BW + KH + 2 * JH:(k + 1) * BW], lj)
+        st["e"] = slot("lf")
+        tt(st["e"], part(1), part(0), ALU.subtract)
+        st["has"] = slot("lb")
+        act(st["has"], st["c1"], ACT.Sign)
+        o3 = (T.LB[:, k * BW + KH:k * BW + KH + JH], lj)
+        st["wall"] = o3
+        if v > 1:
+            d = slot("lf")
+            tt(d, o3, old["wall"], ALU.is_equal)
+            ez = slot("lf")
+            ts(ez, d, 2.0 * K, ALU.mult)
+            o4 = slot("lf")
+            tt(o4, o3, ez, ALU.max)
+            o3 = o4
+        o2, o16 = slot("lf"), slot("lu")
+        tt(o2, o3, (T.KJ[:, h * JH:(h + 1) * JH], "KJ"), ALU.add)
+        ts(o16, o2, 2.0 * K, ALU.min)
+        bs = big("BB", h)
+        lb = (T.LB[:, k * BW:k * BW + KH], "LB%d" % k)
+        if OPT["late"]:
+            gact(bs, winW, o16, ACT.Copy, 0.0, 1.0, KH)
+            st["lb"], st["wg"] = lb, bs
+            bs = big("XS", h)
+            tt(bs, st["wg"], lb, ALU.add, n=KH, f=1.5)
+        else:
+            gtt(bs, winW, o16, lb, ALU.add, KH)
+        st["B"] = big("BA", h)
+        ts(st["B"], bs, 127.0, ALU.min, n=KH, f=0.5)
+        st["L"] = ("LL", o + 4 * JH, "LX%d" % k)
+        st["M"] = mask(h, st, wv, "MA")
+        return st
+
+    def send(k, part, src, dst, r, w, nbytes):
+        s = "r%d" % (4 * k + part)
+        add("g", lambda: g.remote_dma(dst, src, T.sem[s], T.sem.sent, pid, rid, emask), 0.6, r, ["fly" + w], kind="s")
+        add("x", None, 0.0, ["fly" + w], [w], kind="r", lat=2.5 + nbytes / 40e3, sem=s, cnt=neng)
+
+    def step(i, h, st):
+        v, s = divmod(i, NS)
+        leave = s == NS - 1 and i < NL - 1
+        last = i == NL - 1
+        pp, pb, pg, ps = "PP%d" % h, "PB%d" % h, "PG%d" % h, "PS%d" % h
+        k_ = v * H + h
+        so = k_ * 16 * JH
+
+        def spart(j):
+            return (T.SL[:, so + j * JH:so + (j + 1) * JH], "SL%d_%d" % (k_, j))
+        nw = {"wall": st.get("wall")}
+        B, m = st.get("B"), st["m"]
+        s1, s2 = big("S1", h), big("S2", h)
+        pbw = (T[pb][:], pb + "w")
+        ppw = (T[pp][:], pp + "w")
+        way1 = "v" if "lb" in st else OPT["s1"][i % len(OPT["s1"])]
+        way2 = OPT["s2"][i % len(OPT["s2"])]
+        if way2 == "g" and (i == 0 or "lb" in st):
+            way2 = "a"
+        fg = big("FG", h)
+        low = way1 == "t" and i > 0
+        if way1 != "g" or way2 != "g":
+            gact(fg, winF1 if low else winF, st["m16"], ACT.Copy, 0.0, 1.0, KH)
+
+        def less(bank, bw, lhs):
+            if "lb" in st:
+                mm([(bw[0], T.IB[:], st["wg"][0], KH)], ["IB", st["wg"][1]], [bw[1]], bank, keep=True)
+                mm([(bw[0], T[lhs][:], fg[0], KH)], [lhs, fg[1], bw[1]], [bw[1]], bank, cont=True, keep=True)
+                mm([(bw[0], T.IB[:], st["lb"][0], KH)], ["IB", st["lb"][1], bw[1]], [bw[1]], bank, cont=True)
+            else:
+                mm([(bw[0], T.IB[:], B[0], KH)], ["IB", B[1]], [bw[1]], bank, keep=True)
+                mm([(bw[0], T[lhs][:], fg[0], KH)], [lhs, fg[1], bw[1]], [bw[1]], bank, cont=True)
+        if way1 == "g":
+            gtt(s1, winF if i == 0 else winF1, st["m16"], B, ALU.is_gt, KH)
+        elif way1 == "t":
+            tt(s1, fg, B, ALU.is_gt, n=KH, f=OPT["f2"])
+        else:
+            less(pb, pbw, "NB")
+            ts(s1, pbw, 0.0 if i == 0 else -128.0, ALU.is_lt, n=KH, x=[pb])
+        q = 9 if i == 0 else 14 if low else 11
+        if way2 == "g":
+            gtt(s2, winF2, st["m16"], B, ALU.is_gt, KH)
+        else:
+            less(pp, ppw, "N2")
+            if way2 == "a":
+                add("a", lambda: A.activation(s2[0], ppw[0], ACT.Sigmoid, bias=cf(q)[0], scale=-256.0),
+                    KH * CY + 0.02 + (1.3 if i + h == 0 else 0), [ppw[1], cf(q)[1]], [s2[1]], [pp])
+            else:
+                ts(s2, ppw, cf(q + 1)[0], ALU.is_lt, n=KH, x=[pp], r=[cf(q + 1)[1]])
+        z = (T[ps][:, 0:JH], ps + "z")
+        mm([(z[0], T.IC[:], st["has"][0], JH)] +
+           [(z[0], T.EZ[:, 15 - r:143 - r], T.S1[:, h * KH + r:(h + 1) * KH:16], JH) for r in range(16)],
+           ["IC", "EZ", st["has"][1], s1[1]], [z[1]], ps)
+        mm([(T[pp][:], T.M1[:], s1[0], KH), (T[pp][:], T.M2[:], s2[0], KH)], ["M1", "M2", s1[1], s2[1]], [pp + "w"], pp)
+        b, k = slot("lf"), slot("lf")
+        ts(b, z, float(CP), ALU.is_equal, x=[ps])
+        ts(k, z, 0.0, ALU.max, 2.0 * CP, ALU.min, x=[ps])
+        be, ix, ig = slot("lf"), slot("lf"), slot("lf")
+        ix16, ig16 = slot("lu"), slot("lu")
+        if i == 0:
+            ix, ix16, be = m, st["m16"], whole("zf")
+        else:
+            tt(be, b, st["e"], ALU.mult)
+            tt(ix, m, be, ALU.add)
+            cp(ix16, ix)
+        tt(ig, ix, k, ALU.add)
+        ts(ig16, ig, float(C if i == 0 else 2 * CP), ALU.min)
+        xg, gg, y = big("XG", h), big("GG", h), big("Y", h)
+        ys = []
+        pw = KH // OPT["split"]
+        for a in range(0, KH, pw):
+            xa = (T.XG[:, h * KH + a:h * KH + a + pw], "XG%d_%d" % (h, a))
+            ya = (T.Y[:, h * KH + a:h * KH + a + pw], "Y%d_%d" % (h, a))
+            o16 = ix16[2] + a // 16
+            gact(xa, winX, (T.lu[:, o16:o16 + pw // 16], ix16[1]), ACT.Identity, -0.375, 1.0 / 4096, pw)
+            tt(ya, (T[pp][:, a:a + pw], pp + "w"), xa, ALU.min, n=pw, f=1.0, x=[pp])
+            ys.append(ya[1])
+        if leave:
+            nb = (T.SB[:, k_ * BW:k_ * BW + KH], "SB%d" % k_)
+        else:
+            nb = big("BC" if B[1].startswith("BA") else "BA", h)
+        nw["B"] = nb
+        if 0 < i < NL - 1 and OPT["bv"][i % len(OPT["bv"])] == "v":
+            gtt(nb, winG, ig16, B, ALU.add, KH)
+        else:
+            gact(gg, winG0 if i == 0 else winG, ig16, ACT.Copy, 0.0, 1.0, KH)
+            mm([(pbw[0], T.IB[:], B[0], KH)], ["IB", B[1]], [pbw[1]], pb, keep=True)
+            mm([(pbw[0], T.IB[:], gg[0], KH)], ["IB", gg[1], pbw[1]], [pbw[1]], pb, cont=True)
+            if last:
+                ob = big("OB", h)
+                act(ob, pbw, ACT.Identity, bias=128.0, n=KH, x=[pb])
+                dma("s", T.yb[:, h * KH:(h + 1) * KH], ob[0], [ob[1]], [], 128 * KH * 4)
+            else:
+                act(nb, pbw, ACT.Identity, bias=-128.0 if i == 0 else 0.0, n=KH, x=[pb])
+        cb, nk = slot("lf"), slot("lf")
+        c1 = (T.SB[:, k_ * BW + KH + JH:k_ * BW + KH + 2 * JH], "SC%d" % k_) if leave else slot("lb")
+        tt(cb, st["c1"], b, ALU.subtract)
+        tt(nk, st["n1"], k, ALU.subtract)
+        tt(c1, cb, nk, ALU.max)
+        nw["c1"] = c1
+        if last:
+            ts((T.OC[:, h * JH:(h + 1) * JH], "OC%d" % h), c1, -1.0, ALU.add)
+        else:
+            ok = slot("lf")
+            act(ok, k, ACT.Relu, bias=1.0, scale=-1.0)
+            n1 = (T.SB[:, k_ * BW + KH + 2 * JH:(k_ + 1) * BW], "SN%d" % k_) if leave else slot("lb")
+            tt(n1, st["n1"], ok, ALU.add)
+            nw["n1"] = n1
+            if not leave:
+                nw["has"] = slot("lb")
+                act(nw["has"], c1, ACT.Sign)
+        x = slot("lf")
+        tt(x, m, k, ALU.subtract)
+        mk = mask(h, nw, i + 1, "MB" if (st["M"] is None or st["M"][1].startswith("MA")) else "MA")
+        nw["M"] = mk
+        if last:
+            okm = slot("lf")
+            ts(okm, x, 1.0, ALU.add, 0.0, ALU.max)
+            u2 = wide("U2", h, NL)
+            gtt(u2, (okm[0], [okm[1]]), whole("BO"), mk, ALU.mult, LW)
+        L = pg + "w"
+        tn = st["tn"]
+
+        lbuf, lo, ltok = st["L"]
+        nw["L"] = st["L"]
+        lsb = (T[lbuf][:, lo:lo + (i + 1) * JH], ltok)
+
+        def take(extra):
+            rr = wide("R", h, i + 1)
+            if extra or i == 0:
+                tt(rr, lsb, mk, ALU.mult, n=(i + 1) * JH, f=1.5)
+            else:
+                tt(rr, (T[pg][:, 0:(i + 1) * JH], L), mk, ALU.mult, n=(i + 1) * JH, f=1.0, x=[pg])
+            tsum = (T[ps][:, 2 * JH:3 * JH], ps + "t")
+            mm([(tsum[0], T.IH[:], T.COFF[:, 0:JH], JH)] + [(tsum[0], T.IH[:], e_[0], JH) for e_ in extra] +
+               [(tsum[0], T.IH[:], T.R[:, h * LW + s_ * JH:h * LW + (s_ + 1) * JH], JH) for s_ in range(i + 1)],
+               ["IH", "COFF", rr[1]] + [e_[1] for e_ in extra], [tsum[1]], ps)
+            t = slot("lf")
+            tt(t, tsum, x, ALU.max, f=1.0, x=[ps])
+            return rr, t
+        early = leave or (OPT["early"] and not last and i > 0)
+        if early:
+            stay, stt, tn = slot("lf"), slot("lh"), slot("lf")
+            act(stay, k, ACT.Relu, bias=1.0 - 2.0 * CP)
+            tt(stt, stay, st["tn"], ALU.mult)
+            tt(tn, st["tn"], stt, ALU.subtract)
+            rr, t = take([stt])
+        if leave:
+            ti, j_, nz = slot("li"), slot("li"), slot("lf")
+            ts(ti, t, float(K), ALU.mult)
+            ts(j_, ti, K, ALU.bitwise_and)
+            ts(nz, c1, 0.5, ALU.is_lt, 2.0 * K, ALU.mult)
+            jw = (T.SB[:, k_ * BW + KH:k_ * BW + KH + JH], "SJ%d" % k_)
+            tt(jw, j_, nz, ALU.max)
+            if OPT["late"]:
+                send(k_, 3, T.SB[:, k_ * BW + KH:(k_ + 1) * BW], T.LB[:, k_ * BW + KH:(k_ + 1) * BW], [jw[1], c1[1], n1[1]], "LJ%d" % k_, 128 * 3 * JH * 2)
+                send(k_, 0, nb[0], T.LB[:, k_ * BW:k_ * BW + KH], [nb[1]], "LB%d" % k_, 128 * KH * 2)
+            else:
+                send(k_, 0, T.SB[:, k_ * BW:(k_ + 1) * BW], T.LB[:, k_ * BW:(k_ + 1) * BW], [nb[1], jw[1], c1[1], n1[1]], "LB%d" % k_, 128 * BW * 2)
+            ts(spart(1), t, -OFF, ALU.add)
+        rs = (T[ps][:, JH:2 * JH], ps + "r")
+        mm([(rs[0], T.ER[:, 15 - r:143 - r], T.Y[:, h * KH + r:(h + 1) * KH:16], JH) for r in range(16)],
+           ["ER"] + ys, [rs[1]], ps)
+        ri, r_ = slot("li"), slot("li")
+        ts(ri, rs, 8388608.0 - 512.0, ALU.add, x=[ps])
+        ts(r_, ri, 4095, ALU.bitwise_and)
+        if i == 0:
+            mn = r_
+        else:
+            yy, by = slot("lf"), slot("lf")
+            mn = (T.OM[:, h * JH:(h + 1) * JH], "OM%d" % h) if last else slot("lf")
+            tt(yy, r_, m, ALU.subtract)
+            tt(by, b, yy, ALU.mult)
+            tt(mn, r_, by, ALU.subtract)
+        nw["m"] = mn
+        if leave:
+            ts(spart(0), mn, -OFF, ALU.add)
+            send(k_, 1, T.SL[:, so:so + 2 * JH], T.LL[:, so:so + 2 * JH], ["SL%d_%d" % (k_, j) for j in range(2)], "LL%d" % k_, 128 * 2 * JH * 2)
+        elif not last:
+            nw["m16"] = slot("lu")
+            cp(nw["m16"], mn)
+        if i > 0:
+            w_, vn = slot("lf"), slot("lf" if OPT["gu"] else "lh")
+            tt(w_, tn, be, ALU.subtract)
+            tt(vn, w_, by, ALU.add)
+            u = wide("U", h, i)
+            mo = (T[st["M"][1][:2]][:, h * LW:h * LW + i * JH], st["M"][1])
+            if OPT["gu"]:
+                gtt(u, (vn[0], [vn[1]]), (T.BO[:, 0:2 * i], "BO"), mo, ALU.mult, i * JH)
+            else:
+                spread(pp, 0, vn, i)
+                tt(u, (T[pp][:, 0:i * JH], pp + "w"), mo, ALU.mult, n=i * JH, f=1.0, x=[pp])
+            items = [(T[pg][:, 0:(i + 1) * JH], T.IH[:], lsb[0], (i + 1) * JH)]
+            if last:
+                items.append((T[pg][:, 0:LW], T.IH[:], T.COFF[:], LW))
+            mm(items, ["IH", "COFF", ltok, ltok + "e"], [L], pg, keep=True)
+            mm([(T[pg][:, 0:i * JH], T.IH[:], u[0], i * JH)], ["IH", u[1], L], [L], pg, cont=True)
+        if last:
+            add("v", lambda: V.tensor_tensor(T.OL[:, :, h * JH:(h + 1) * JH], T[pg][:, 0:LW], u2[0], ALU.add), LW * CY,
+                [L, u2[1]], ["OL%d" % h], [pg])
+            return nw
+        if not early:
+            rr, t = take([])
+        if leave:
+            lx = (T.SL[:, so + 4 * JH:so + (5 + i) * JH], "SL%d_4" % k_)
+            tt(lx, (T[pg][:, 0:(i + 1) * JH], L), rr, ALU.subtract, n=(i + 1) * JH, f=1.0, x=[pg])
+            send(k_, 2, lx[0], T.LL[:, so + 4 * JH:so + (5 + i) * JH], [lx[1]], "LX%d" % k_, 128 * (1 + i) * JH * 2)
+        else:
+            if i == 0:
+                tt(lsb, lsb, rr, ALU.subtract)
+            else:
+                tt(lsb, (T[pg][:, 0:(i + 1) * JH], L), rr, ALU.subtract, n=(i + 1) * JH, f=1.0, x=[pg])
+            nw["tn"] = slot("lf")
+            act(nw["tn"], t, ACT.Identity, bias=-OFF)
+            nw["e"] = slot("lf")
+            tt(nw["e"], t, mn, ALU.subtract)
+        return nw
+
+    sts = []
+    for h in range(H):
+        cur[0] = h
+        sts.append(first(h))
+    for i in range(NL):
+        for h in range(H):
+            cur[0] = h
+            if i > 0 and i % NS == 0:
+                sts[h] = arrive(i // NS, h, sts[h])
+            sts[h] = step(i, h, sts[h])
+    dma("s", T.ym[:], T.OM[:], ["OM0", "OM1"], [], 128 * 256)
+    dma("a", T.yc[:], T.OC[:], ["OC0", "OC1"], [], 128 * 256)
+    dma("s", T.yl[:], T.OL[:], ["OL0", "OL1"], [], 128 * 768 * 4)
+    return ops, nsend * len([op for op in ops if op["kind"] == "s"])
+
+
+def depend(ops):
+    lastw, readers, lastx = {}, {}, {}
+    for i, op in enumerate(ops):
+        pre = {}
+
+        def edge(j, data):
+            if j == i:
+                return
+            pj = ops[j]
+            need = pj["eng"] != op["eng"] or pj["kind"] in ("d", "r") or (data and op["eng"] != "p")
+            if pj["kind"] == "s":
+                need = False
+            pre[j] = pre.get(j, False) or need
+        for n in op["r"]:
+            if n in lastw:
+                edge(lastw[n], True)
+        for n in op["w"]:
+            if n in lastw:
+                edge(lastw[n], True)
+            for j in readers.get(n, []):
+                edge(j, True)
+        for n in op["x"]:
+            if n in lastx:
+                edge(lastx[n], False)
+            lastx[n] = i
+        for n in op["r"]:
+            readers.setdefault(n, []).append(i)
+        for n in op["w"]:
+            lastw[n] = i
+            readers[n] = []
+        op["pre"] = pre
+
+
+def order(ops):
+    n = len(ops)
+    succ = [[] for _ in range(n)]
+    for i, op in enumerate(ops):
+        for j in op["pre"]:
+            succ[j].append(i)
+
+    def gap(j, i):
+        if not ops[i]["pre"][j]:
+            return ops[j]["lat"]
+        return ops[j]["lat"] + (OWN if ops[j]["eng"] == ops[i]["eng"] else HOP)
+    prio = [0.0] * n
+    for i in range(n - 1, -1, -1):
+        d = ops[i].get("bytes", 0) / 250e3
+        prio[i] = ops[i]["cost"] + d + max([ops[i]["lat"]] + [gap(i, s) + prio[s] for s in succ[i]])
+    x = OPT["seed"] * 7919 + 1
+    for i in range(n):
+        x = (x * 1103515245 + 12345) % 2147483648
+        prio[i] += OPT["jit"] * x / 2147483648.0
+        if ops[i]["h"] == 0:
+            prio[i] += OPT["lead"]
+    left = [len(op["pre"]) for op in ops]
+    rdy = [0.0] * n
+    for i in range(n):
+        if ops[i]["w"] == ["XG1_0"]:
+            rdy[i] = OPT["hold"]
+            break
+    ready = [i for i in range(n) if left[i] == 0]
+    free = {}
+    dfree = [0.0]
+    seq = []
+    end = 0.0
+    while ready:
+        st = [max(rdy[i], free.get(ops[i]["eng"], 0.0)) for i in ready]
+        t0 = min(st)
+        e0 = ops[ready[st.index(t0)]]["eng"]
+        cand = [i for i, s in zip(ready, st) if ops[i]["eng"] == e0 and s <= t0 + OPT["win"]]
+        if ops[cand[0]]["kind"] == "d" and not ops[cand[0]]["r"]:
+            i = min(cand)
+        else:
+            i = max(cand, key=lambda q: prio[q] - OPT["lam"] * max(0.0, rdy[q] - t0))
+        s = max(rdy[i], free.get(e0, 0.0))
+        f = s + ops[i]["cost"]
+        free[e0] = f
+        if ops[i]["kind"] == "d":
+            dfree[0] = max(dfree[0], f) + ops[i]["bytes"] / 250e3
+            f = dfree[0]
+        ops[i]["t"] = (s, f)
+        end = max(end, f + ops[i]["lat"])
+        ready.remove(i)
+        seq.append(i)
+        for q in succ[i]:
+            rdy[q] = max(rdy[q], f + gap(i, q))
+            left[q] -= 1
+            if left[q] == 0:
+                ready.append(q)
+    return seq, end
+
+
+def polish(ops, seq, rounds, paces):
+    n = len(ops)
+    tabs = []
+    for gr, pc, hop, own, net in paces:
+        c = [o["cost"] * pc if o["eng"] == "p" else 0.07 + o["gn"] * gr * CY if o.get("gn") else o["cost"] for o in ops]
+        pr = [[(j, ops[j]["lat"] * (net if ops[j]["kind"] == "r" else 1.0) +
+                ((own if ops[j]["eng"] == o["eng"] else hop) if need else 0.0)) for j, need in o["pre"].items()] for o in ops]
+        tabs.append((c, pr))
+    eng = [o["eng"] for o in ops]
+    dm = [o.get("bytes", 0) / 250e3 for o in ops]
+    lat = [o["lat"] for o in ops]
+
+    def run(sq, tab, trace=False):
+        c, pr = tab
+        fin = [0.0] * n
+        why = [-1] * n
+        free = {}
+        dfree = 0.0
+        end, last = 0.0, -1
+        for i in sq:
+            s, w = free.get(eng[i], (0.0, -1))
+            if w >= 0:
+                w = -2 - w
+            for j, l in pr[i]:
+                t = fin[j] + l
+                if t > s:
+                    s, w = t, j
+            f = s + c[i]
+            free[eng[i]] = (f, i)
+            if dm[i]:
+                dfree = max(dfree, f) + dm[i]
+                f = dfree
+            fin[i] = f
+            why[i] = w
+            if f + lat[i] > end:
+                end, last = f + lat[i], i
+        if not trace:
+            return end
+        pairs = []
+        while last != -1:
+            w = why[last]
+            if w <= -2:
+                w = -2 - w
+                if w not in ops[last]["pre"] and not dm[w]:
+                    pairs.append((w, last))
+            last = w
+        return pairs
+    best = sum(run(seq, t) for t in tabs)
+    x = 1
+    pairs = []
+    for _ in range(rounds):
+        x = (x * 1103515245 + 12345) % 2147483648
+        if not pairs:
+            pairs = run(seq, tabs[(x >> 8) % len(tabs)], True)
+            if not pairs:
+                continue
+        a, b = pairs.pop((x >> 8) % len(pairs))
+        pa, pb = seq.index(a), seq.index(b)
+        if pa > pb:
+            continue
+        need = {b}
+        for q in range(pb - 1, pa - 1, -1):
+            k = seq[q]
+            if any(k in ops[m]["pre"] for m in need) or (eng[k] != eng[a] and any(eng[m] == eng[k] for m in need)):
+                need.add(k)
+        if a in need:
+            continue
+        mid = seq[pa:pb + 1]
+        new = seq[:pa] + [k for k in mid if k in need] + [k for k in mid if k not in need] + seq[pb + 1:]
+        t = sum(run(new, tb) for tb in tabs)
+        if t <= best + 1e-9:
+            if t < best - 1e-9:
+                pairs = []
+            best, seq = t, new
+    return seq
+
+
+PACES = [(1.56, 1.0, 0.15, 0.07, 1.0), (1.3, 1.2, 0.3, 0.1, 1.3), (1.9, 0.9, 0.2, 0.05, 1.0)]
+ORDER = {}
+
+
+def rank_program(g, core, T, topo):
+    rank = T.rank_of(core)
+    if rank is None:
+        return
+    ops, sent = build(g, T, topo, core, rank)
+    depend(ops)
+    if len(ops) not in ORDER:
+        ORDER[len(ops)] = polish(ops, order(ops)[0], OPT["rounds"], PACES)
+    seq = ORDER[len(ops)]
+    queue = {"v": g.vector, "a": g.scalar, "p": g.tensor, "g": g, "s": g.sync}
+    count = {}
+    for i in seq:
+        op = ops[i]
+        if op["kind"] == "c":
+            op["sem"] = "c" + op["eng"]
+            count[op["sem"]] = count.get(op["sem"], 0) + 1
+            op["cnt"] = count[op["sem"]]
+        elif op["kind"] in ("d", "r"):
+            count[op["sem"]] = op["cnt"]
+    seen = {}
+    for i in seq:
+        op = ops[i]
+        if op["kind"] == "r":
+            continue
+        q = queue[op["eng"]]
+        want = {}
+        for j, need in op["pre"].items():
+            if need:
+                want[ops[j]["sem"]] = max(want.get(ops[j]["sem"], 0), ops[j]["cnt"])
+        for s, c in want.items():
+            if seen.get((op["eng"], s), 0) < c:
+                q.wait_ge(T.sem[s], c)
+                seen[(op["eng"], s)] = c
+        ins = op["fn"]()
+        if op["kind"] == "c":
+            ins.then_inc(T.sem[op["sem"]], 1)
+        elif op["kind"] == "d":
+            ins.then_inc(T.sem[op["sem"]], 16)
+    count["sent"] = sent
+    for s, c in count.items():
+        if max([seen.get((e, s), 0) for e in queue]) < c:
+            g.wait_ge(T.sem[s], c)

@@ -37,6 +37,7 @@ SCRATCH = {
     "lu": ("sbuf", [128, NU16 * JH], "uint16"), "lh": ("sbuf", [128, NF16 * JH], "float16"), "lb": ("sbuf", [128, NB16 * JH], "bfloat16"),
     "S1": ("sbuf", [128, K], "bfloat16"), "S2": ("sbuf", [128, K], "bfloat16"), "XG": ("sbuf", [128, K], "float32"),
     "GG": ("sbuf", [128, K], "bfloat16"), "Y": ("sbuf", [128, K], "float16"),
+    "SG": ("sbuf", [128, 2 * K], "bfloat16"), "LG": ("sbuf", [128, 2 * K], "bfloat16"), "X2": ("sbuf", [128, K], "float16"),
     "XS": ("sbuf", [128, K], "float16"), "BA": ("sbuf", [128, K], "bfloat16"), "BB": ("sbuf", [128, K], "bfloat16"),
     "MA": ("sbuf", [128, H * LW], "bfloat16"), "MB": ("sbuf", [128, H * LW], "bfloat16"),
     "U": ("sbuf", [128, H * LW], "float16"), "R": ("sbuf", [128, H * LW], "float16"), "U2": ("sbuf", [128, H * LW], "float32"),
@@ -50,21 +51,21 @@ for _h in range(H):
         SCRATCH["%s%d" % (_n, _h)] = ("psum", [128, 512], "float32")
 
 NDMA = 40
-SEMAPHORES = ["cv", "ca", "cp", "cg", "sent"] + ["d%d" % i for i in range(NDMA)] + ["r%d" % i for i in range(8 * H)]
+SEMAPHORES = ["cv", "ca", "cp", "cg", "sent"] + ["d%d" % i for i in range(NDMA)] + ["r%d" % i for i in range(10 * H)]
 
 ALU = AluOpType
 ACT = ActivationFunctionType
 CY = 0.001
 PCY = 0.0005
-HOP = 0.25
-OWN = 0.07
-OPT = {"s1": "g", "s2": "a", "bv": "a", "gu": True, "gm": False, "lead": 3.5, "win": 0.2, "split": 2, "seed": 4639, "jit": 0.5,
-       "early": True, "lam": 30.0, "hold": 14.0, "late": True, "f2": 1.0, "rounds": 12000}
+HOP = 0.3
+OWN = 0.08
+OPT = {"s1": "t", "s2": "a", "bv": "a", "gu": True, "gm": False, "lead": 3.0, "win": 0.3, "split": 2, "seed": 1790, "jit": 0.5,
+       "early": False, "lam": 30.0, "hold": 13.0, "late": 3, "f2": 1.0, "cut": 192, "turn": 11, "lead2": 0.0, "ahead": True, "both": False, "dl": 1.5, "rounds": 26000}
 
 
 def build(g, T, topo, core, rank):
     ops = []
-    cur = [None]
+    cur = [None, 0]
     cores = list(T.cores)
     nxt = cores[(rank + 1) % len(cores)]
     rid, pid, _se = topo.addr(nxt)
@@ -75,7 +76,7 @@ def build(g, T, topo, core, rank):
 
     def add(eng, fn, cost, r=(), w=(), x=(), kind="c", lat=0.0, sem=None, cnt=0):
         ops.append({"eng": eng, "fn": fn, "cost": cost, "r": list(r), "w": list(w), "x": list(x), "kind": kind,
-                    "lat": lat, "sem": sem, "cnt": cnt, "h": cur[0]})
+                    "lat": lat, "sem": sem, "cnt": cnt, "h": cur[0], "i": cur[1]})
 
     used = {"lf": 0, "li": 0, "lu": 0, "lh": 0, "lb": 0}
 
@@ -126,8 +127,11 @@ def build(g, T, topo, core, rank):
     def dma(q, out, in_, r, w, nbytes):
         s = "d%d" % ndma[0]
         ndma[0] += 1
-        e = {"s": g.sync, "a": g.scalar}[q]
-        add(q, lambda: e.dma_start(out, in_), 0.06, r, w, kind="d", lat=2.0, sem=s, cnt=16)
+        if q == "g":
+            add(q, lambda: g.dma_start(out, in_, accum_op=ALU.add), 0.6, r, w, kind="d", lat=OPT["dl"], sem=s, cnt=16)
+        else:
+            e = {"s": g.sync, "a": g.scalar}[q]
+            add(q, lambda: e.dma_start(out, in_), 0.06, r, w, kind="d", lat=2.0, sem=s, cnt=16)
         ops[-1]["bytes"] = nbytes
 
     def gop(fn, n, w):
@@ -146,7 +150,7 @@ def build(g, T, topo, core, rank):
         dma("a", T.B0[:, h * KH:(h + 1) * KH], T.b0[:, h * KH:(h + 1) * KH], [], ["B0%d" % h], 128 * KH * 2)
     dma("s", T.NX[:, 0:C // 2], T.nx[:, 0:C // 2], [], ["NX0"], 128 * C * 2)
     dma("a", T.NX[:, C // 2:C], T.nx[:, C // 2:C], [], ["NX1"], 128 * C * 2)
-    dma("s", T.W[:, 0:2 * K], T.wl[:], [], ["W"], 128 * 2 * K * 2)
+    dma("s", T.W[:, 0:2 * K], T.wl[:], ["NX0", "NX1"], ["W"], 128 * 2 * K * 2)
     FT = ["F%d" % i for i in range(NFP)]
 
     gop(lambda: g.iota(T.ci[:, 0:1], [[0, 1]], 0, 1), 1, ["ci0"])
@@ -176,7 +180,7 @@ def build(g, T, topo, core, rank):
     ts(cf(6), cf(1), 15.0, ALU.is_equal, 328.0, ALU.mult)
     ts(cf(7), cf(6), -128.0, ALU.add)
     ts(cf(8), cf(1), 15.0, ALU.is_equal, -0.5, ALU.mult)
-    for q, o in ((9, 0.0), (11, 128.0)) + (((14, -128.0),) if "t" in OPT["s1"] else ()):
+    for q, o in ((9, 0.0), (11, 128.0)) + (((14, -128.0),) if "t" in OPT["s1"] or "h" in OPT["s1"] else ()):
         ts(cf(13), cf(1), 15.0, ALU.is_equal, 1000.0, ALU.mult)
         ts(cf(q + 1), cf(13), -o, ALU.add)
         ts(cf(q), cf(q + 1), 256.0, ALU.mult, -128.0, ALU.add)
@@ -217,7 +221,7 @@ def build(g, T, topo, core, rank):
     for i in range(NFP):
         sl = slice(i * fw, (i + 1) * fw)
         ts((T.G[:, sl], "GN%d" % i), (T.F[:, sl], "F%d" % i), -1.0, ALU.mult, n=fw, f=0.5)
-        if "g" in OPT["s1"] or "t" in OPT["s1"]:
+        if OPT["s1"] != "v":
             act((T.F1[:, sl], "F1_%d" % i), (T.F[:, sl], "F%d" % i), ACT.Identity, bias=-128.0, n=fw)
         if "g" in OPT["s2"]:
             ts((T.F2[:, sl], "F2_%d" % i), (T.F[:, sl], "F%d" % i), 2.0, ALU.mult, cf(7)[0], ALU.add, n=fw, f=0.5, r=["cf7"])
@@ -244,7 +248,7 @@ def build(g, T, topo, core, rank):
     winW = (T.W[:], ["W", "Wz"])
 
     def big(name, h, w=KH):
-        return (T[name][:, h * KH:h * KH + w], "%s%d" % (name, h))
+        return (T[name][:, h * KH:h * KH + w], "%s%d" % (name, h), (name, h * KH))
 
     def wide(name, h, blocks):
         return (T[name][:, h * LW:h * LW + blocks * JH], "%s%d" % (name, h))
@@ -316,13 +320,25 @@ def build(g, T, topo, core, rank):
         ts(o16, o2, 2.0 * K, ALU.min)
         bs = big("BB", h)
         lb = (T.LB[:, k * BW:k * BW + KH], "LB%d" % k)
-        if OPT["late"]:
+        if OPT["late"] == 3:
+            tt(bs, lb, (T.LG[:, k * KH:(k + 1) * KH], "LG%d" % k), ALU.add, n=KH, f=OPT["f2"])
+            st["raw"] = big("XS", h)
+            gtt(st["raw"], winW, o16, bs, ALU.add, KH)
+            bs = st["raw"]
+        elif OPT["late"]:
             gact(bs, winW, o16, ACT.Copy, 0.0, 1.0, KH)
             st["lb"], st["wg"] = lb, bs
             bs = big("XS", h)
-            tt(bs, st["wg"], lb, ALU.add, n=KH, f=1.5)
+            tt(bs, st["wg"], lb, ALU.add, n=KH, f=OPT["f2"])
+            if OPT["ahead"]:
+                st["lb"], st["wg"] = (T.LG[:, k * KH:(k + 1) * KH], "LG%d" % k), bs
+                bs = big("X2", h)
+                tt(bs, st["wg"], st["lb"], ALU.add, n=KH, f=OPT["f2"])
         else:
             gtt(bs, winW, o16, lb, ALU.add, KH)
+        if OPT["late"] == 2:
+            del st["lb"]
+            st["raw"] = bs
         st["B"] = big("BA", h)
         ts(st["B"], bs, 127.0, ALU.min, n=KH, f=0.5)
         st["L"] = ("LL", o + 4 * JH, "LX%d" % k)
@@ -330,7 +346,7 @@ def build(g, T, topo, core, rank):
         return st
 
     def send(k, part, src, dst, r, w, nbytes):
-        s = "r%d" % (4 * k + part)
+        s = "r%d" % (5 * k + part)
         add("g", lambda: g.remote_dma(dst, src, T.sem[s], T.sem.sent, pid, rid, emask), 0.6, r, ["fly" + w], kind="s")
         add("x", None, 0.0, ["fly" + w], [w], kind="r", lat=2.5 + nbytes / 40e3, sem=s, cnt=neng)
 
@@ -354,22 +370,41 @@ def build(g, T, topo, core, rank):
         if way2 == "g" and (i == 0 or "lb" in st):
             way2 = "a"
         fg = big("FG", h)
-        low = way1 == "t" and i > 0
-        if way1 != "g" or way2 != "g":
+        low = way1 in "th" and i > 0
+        cut = OPT["cut"]
+        if way1 == "h":
+            o16 = st["m16"][2]
+            fgb = (T.FG[:, h * KH + cut:(h + 1) * KH], "FGb%d" % h)
+            gact(fgb, winF1 if low else winF, (T.lu[:, o16 + cut // 16:o16 + JH], st["m16"][1]), ACT.Copy, 0.0, 1.0, KH - cut)
+            add("a", lambda: A.activation(T.FG[:, h * KH:h * KH + cut], (winF1 if low else winF)[0].indirect(T.lu[:, o16:o16 + cut // 16]), ACT.Copy),
+                0.08 + 1.56 * cut * CY, list((winF1 if low else winF)[1]) + [st["m16"][1], fgb[1]], [fg[1]])
+            ops[-1]["gn"] = cut
+        elif way1 != "g" or way2 != "g":
             gact(fg, winF1 if low else winF, st["m16"], ACT.Copy, 0.0, 1.0, KH)
 
         def less(bank, bw, lhs):
             if "lb" in st:
-                mm([(bw[0], T.IB[:], st["wg"][0], KH)], ["IB", st["wg"][1]], [bw[1]], bank, keep=True)
+                one = "IH" if OPT["ahead"] else "IB"
+                mm([(bw[0], T[one][:], st["wg"][0], KH)], [one, st["wg"][1]], [bw[1]], bank, keep=True)
                 mm([(bw[0], T[lhs][:], fg[0], KH)], [lhs, fg[1], bw[1]], [bw[1]], bank, cont=True, keep=True)
                 mm([(bw[0], T.IB[:], st["lb"][0], KH)], ["IB", st["lb"][1], bw[1]], [bw[1]], bank, cont=True)
             else:
-                mm([(bw[0], T.IB[:], B[0], KH)], ["IB", B[1]], [bw[1]], bank, keep=True)
-                mm([(bw[0], T[lhs][:], fg[0], KH)], [lhs, fg[1], bw[1]], [bw[1]], bank, cont=True)
+                one = "IH" if "raw" in st else "IB"
+                mm([(bw[0], T[one][:], Bc[0], KH)], [one, Bc[1]], [bw[1]], bank, keep=True)
+                mm([(bw[0], T[lhs][:], fg[0], KH)], [lhs, fg[1], "FGb%d" % h, bw[1]], [bw[1]], bank, cont=True)
+        Bc = st.get("raw", B)
         if way1 == "g":
-            gtt(s1, winF if i == 0 else winF1, st["m16"], B, ALU.is_gt, KH)
+            gtt(s1, winF if i == 0 else winF1, st["m16"], Bc, ALU.is_gt, KH)
+        elif way1 == "h":
+            bo = Bc[2]
+            s1a = (T.S1[:, h * KH:h * KH + cut], "S1a%d" % h)
+            add("v", lambda: V.tensor_tensor(s1a[0], (winF1 if low else winF)[0].indirect(T.lu[:, o16:o16 + cut // 16]), T[bo[0]][:, bo[1]:bo[1] + cut], ALU.is_gt),
+                0.06 + 1.56 * cut * CY, list((winF1 if low else winF)[1]) + [st["m16"][1], Bc[1]], [s1a[1], s1[1]])
+            ops[-1]["gn"] = cut
+            add("v", lambda: V.tensor_tensor(T.S1[:, h * KH + cut:(h + 1) * KH], fgb[0], T[bo[0]][:, bo[1] + cut:bo[1] + KH], ALU.is_gt),
+                (KH - cut) * CY, [fgb[1], Bc[1]], ["S1b%d" % h])
         elif way1 == "t":
-            tt(s1, fg, B, ALU.is_gt, n=KH, f=OPT["f2"])
+            tt(s1, fg, Bc, ALU.is_gt, n=KH, f=OPT["f2"])
         else:
             less(pb, pbw, "NB")
             ts(s1, pbw, 0.0 if i == 0 else -128.0, ALU.is_lt, n=KH, x=[pb])
@@ -386,8 +421,8 @@ def build(g, T, topo, core, rank):
         z = (T[ps][:, 0:JH], ps + "z")
         mm([(z[0], T.IC[:], st["has"][0], JH)] +
            [(z[0], T.EZ[:, 15 - r:143 - r], T.S1[:, h * KH + r:(h + 1) * KH:16], JH) for r in range(16)],
-           ["IC", "EZ", st["has"][1], s1[1]], [z[1]], ps)
-        mm([(T[pp][:], T.M1[:], s1[0], KH), (T[pp][:], T.M2[:], s2[0], KH)], ["M1", "M2", s1[1], s2[1]], [pp + "w"], pp)
+           ["IC", "EZ", st["has"][1], s1[1], "S1b%d" % h], [z[1]], ps)
+        mm([(T[pp][:], T.M1[:], s1[0], KH), (T[pp][:], T.M2[:], s2[0], KH)], ["M1", "M2", s1[1], "S1b%d" % h, s2[1]], [pp + "w"], pp)
         b, k = slot("lf"), slot("lf")
         ts(b, z, float(CP), ALU.is_equal, x=[ps])
         ts(k, z, 0.0, ALU.max, 2.0 * CP, ALU.min, x=[ps])
@@ -398,26 +433,40 @@ def build(g, T, topo, core, rank):
         else:
             tt(be, b, st["e"], ALU.mult)
             tt(ix, m, be, ALU.add)
-            cp(ix16, ix)
+            if not OPT["both"]:
+                cp(ix16, ix)
         tt(ig, ix, k, ALU.add)
-        ts(ig16, ig, float(C if i == 0 else 2 * CP), ALU.min)
+        if i > 0 and OPT["both"]:
+            add("v", lambda: V.tensor_scalar(T.lu[:, ix16[2]:ix16[2] + 2 * JH], T.lf[:, ix[2]:ix[2] + 2 * JH], 2.0 * CP, None, ALU.min),
+                64 * CY, [ix[1], ig[1]], [ix16[1], ig16[1]])
+        else:
+            ts(ig16, ig, float(C if i == 0 else 2 * CP), ALU.min)
         xg, gg, y = big("XG", h), big("GG", h), big("Y", h)
         ys = []
         pw = KH // OPT["split"]
         for a in range(0, KH, pw):
             xa = (T.XG[:, h * KH + a:h * KH + a + pw], "XG%d_%d" % (h, a))
             ya = (T.Y[:, h * KH + a:h * KH + a + pw], "Y%d_%d" % (h, a))
-            o16 = ix16[2] + a // 16
-            gact(xa, winX, (T.lu[:, o16:o16 + pw // 16], ix16[1]), ACT.Identity, -0.375, 1.0 / 4096, pw)
+            ox = ix16[2] + a // 16
+            gact(xa, winX, (T.lu[:, ox:ox + pw // 16], ix16[1]), ACT.Identity, -0.375, 1.0 / 4096, pw)
             tt(ya, (T[pp][:, a:a + pw], pp + "w"), xa, ALU.min, n=pw, f=1.0, x=[pp])
             ys.append(ya[1])
-        if leave:
-            nb = (T.SB[:, k_ * BW:k_ * BW + KH], "SB%d" % k_)
+        ahead = OPT["ahead"] and s == NS - 2 and v < NV - 1
+        if leave or ahead:
+            nb = (T.SB[:, k_ * BW:k_ * BW + KH], "SB%d" % k_, ("SB", k_ * BW))
         else:
             nb = big("BC" if B[1].startswith("BA") else "BA", h)
         nw["B"] = nb
-        if 0 < i < NL - 1 and OPT["bv"][i % len(OPT["bv"])] == "v":
+        if leave and OPT["ahead"]:
+            sg = (T.SG[:, k_ * KH:(k_ + 1) * KH], "SG%d" % k_)
+            gact(sg, winG, ig16, ACT.Copy, 0.0, 1.0, KH)
+            send(k_, 4, sg[0], T.LG[:, k_ * KH:(k_ + 1) * KH], [sg[1]], "LG%d" % k_, 128 * KH * 2)
+        elif 0 < i < NL - 1 and OPT["bv"][i % len(OPT["bv"])] == "v":
             gtt(nb, winG, ig16, B, ALU.add, KH)
+        elif i > 0 and s < NS - 1 and not ahead and OPT["bv"][i % len(OPT["bv"])] == "d":
+            gact(gg, winG, ig16, ACT.Copy, 0.0, 1.0, KH)
+            dma("g", B[0], gg[0], [gg[1], B[1]], [B[1]], 2 * 128 * KH * 2)
+            nw["B"] = B
         else:
             gact(gg, winG0 if i == 0 else winG, ig16, ACT.Copy, 0.0, 1.0, KH)
             mm([(pbw[0], T.IB[:], B[0], KH)], ["IB", B[1]], [pbw[1]], pb, keep=True)
@@ -428,6 +477,8 @@ def build(g, T, topo, core, rank):
                 dma("s", T.yb[:, h * KH:(h + 1) * KH], ob[0], [ob[1]], [], 128 * KH * 4)
             else:
                 act(nb, pbw, ACT.Identity, bias=-128.0 if i == 0 else 0.0, n=KH, x=[pb])
+        if ahead:
+            send(k_, 0, nb[0], T.LB[:, k_ * BW:k_ * BW + KH], [nb[1]], "LB%d" % k_, 128 * KH * 2)
         cb, nk = slot("lf"), slot("lf")
         c1 = (T.SB[:, k_ * BW + KH + JH:k_ * BW + KH + 2 * JH], "SC%d" % k_) if leave else slot("lb")
         tt(cb, st["c1"], b, ALU.subtract)
@@ -464,7 +515,7 @@ def build(g, T, topo, core, rank):
         def take(extra):
             rr = wide("R", h, i + 1)
             if extra or i == 0:
-                tt(rr, lsb, mk, ALU.mult, n=(i + 1) * JH, f=1.5)
+                tt(rr, lsb, mk, ALU.mult, n=(i + 1) * JH, f=OPT["f2"])
             else:
                 tt(rr, (T[pg][:, 0:(i + 1) * JH], L), mk, ALU.mult, n=(i + 1) * JH, f=1.0, x=[pg])
             tsum = (T[ps][:, 2 * JH:3 * JH], ps + "t")
@@ -490,7 +541,8 @@ def build(g, T, topo, core, rank):
             tt(jw, j_, nz, ALU.max)
             if OPT["late"]:
                 send(k_, 3, T.SB[:, k_ * BW + KH:(k_ + 1) * BW], T.LB[:, k_ * BW + KH:(k_ + 1) * BW], [jw[1], c1[1], n1[1]], "LJ%d" % k_, 128 * 3 * JH * 2)
-                send(k_, 0, nb[0], T.LB[:, k_ * BW:k_ * BW + KH], [nb[1]], "LB%d" % k_, 128 * KH * 2)
+                if not OPT["ahead"]:
+                    send(k_, 0, nb[0], T.LB[:, k_ * BW:k_ * BW + KH], [nb[1]], "LB%d" % k_, 128 * KH * 2)
             else:
                 send(k_, 0, T.SB[:, k_ * BW:(k_ + 1) * BW], T.LB[:, k_ * BW:(k_ + 1) * BW], [nb[1], jw[1], c1[1], n1[1]], "LB%d" % k_, 128 * BW * 2)
             ts(spart(1), t, -OFF, ALU.add)
@@ -515,6 +567,26 @@ def build(g, T, topo, core, rank):
         elif not last:
             nw["m16"] = slot("lu")
             cp(nw["m16"], mn)
+        if last:
+            w_ = slot("lf")
+            tt(w_, tn, be, ALU.subtract)
+            u = wide("U", h, i)
+            mo = (T[st["M"][1][:2]][:, h * LW:h * LW + i * JH], st["M"][1])
+            gtt(u, (w_[0], [w_[1]]), (T.BO[:, 0:2 * i], "BO"), mo, ALU.mult, i * JH)
+            mm([(T[pg][:, 0:LW], T.IH[:], lsb[0], LW), (T[pg][:, 0:LW], T.IH[:], T.COFF[:], LW), (T[pg][:, 0:i * JH], T.IH[:], u[0], i * JH)],
+               ["IH", "COFF", ltok, ltok + "e", u[1]], [L], pg)
+            tt((T[pg][:, 0:LW], L), (T[pg][:, 0:LW], L), u2, ALU.add, n=LW, f=1.0, x=[pg])
+            hp = NL // 2
+            for a in (0, hp):
+                e_ = min(a + hp, i)
+                u3 = (T.U2[:, h * LW + a * JH:h * LW + e_ * JH], "U3%d%d" % (h, a))
+                add("v", lambda a=a, e_=e_, u3=u3: V.tensor_tensor(u3[0], by[0].indirect(T.BO[:, 0:2 * (e_ - a)]),
+                                                                  T[mo[1][:2]][:, h * LW + a * JH:h * LW + e_ * JH], ALU.mult),
+                    0.06 + 1.56 * (e_ - a) * JH * CY, [by[1], "BO", mo[1], L], [u3[1]])
+                add("v", lambda a=a, e_=e_, u3=u3: V.tensor_tensor(T.OL[:, a:e_, h * JH:(h + 1) * JH], T[pg][:, a * JH:e_ * JH], u3[0], ALU.add),
+                    (e_ - a) * JH * CY, [L, u3[1]], ["OL%d%d" % (h, a)], [pg])
+            add("v", lambda: V.tensor_copy(T.OL[:, i, h * JH:(h + 1) * JH], T[pg][:, i * JH:LW]), 64 * CY, [L], ["OLz%d" % h], [pg])
+            return nw
         if i > 0:
             w_, vn = slot("lf"), slot("lf" if OPT["gu"] else "lh")
             tt(w_, tn, be, ALU.subtract)
@@ -527,14 +599,8 @@ def build(g, T, topo, core, rank):
                 spread(pp, 0, vn, i)
                 tt(u, (T[pp][:, 0:i * JH], pp + "w"), mo, ALU.mult, n=i * JH, f=1.0, x=[pp])
             items = [(T[pg][:, 0:(i + 1) * JH], T.IH[:], lsb[0], (i + 1) * JH)]
-            if last:
-                items.append((T[pg][:, 0:LW], T.IH[:], T.COFF[:], LW))
-            mm(items, ["IH", "COFF", ltok, ltok + "e"], [L], pg, keep=True)
+            mm(items, ["IH", ltok, ltok + "e"], [L], pg, keep=True)
             mm([(T[pg][:, 0:i * JH], T.IH[:], u[0], i * JH)], ["IH", u[1], L], [L], pg, cont=True)
-        if last:
-            add("v", lambda: V.tensor_tensor(T.OL[:, :, h * JH:(h + 1) * JH], T[pg][:, 0:LW], u2[0], ALU.add), LW * CY,
-                [L, u2[1]], ["OL%d" % h], [pg])
-            return nw
         if not early:
             rr, t = take([])
         if leave:
@@ -558,13 +624,14 @@ def build(g, T, topo, core, rank):
         sts.append(first(h))
     for i in range(NL):
         for h in range(H):
-            cur[0] = h
+            cur[0], cur[1] = h, i
             if i > 0 and i % NS == 0:
                 sts[h] = arrive(i // NS, h, sts[h])
             sts[h] = step(i, h, sts[h])
     dma("s", T.ym[:], T.OM[:], ["OM0", "OM1"], [], 128 * 256)
     dma("a", T.yc[:], T.OC[:], ["OC0", "OC1"], [], 128 * 256)
-    dma("s", T.yl[:], T.OL[:], ["OL0", "OL1"], [], 128 * 768 * 4)
+    dma("s", T.yl[:, 0:384], T.OL[:, 0:6], ["OL00", "OL10"], [], 128 * 384 * 4)
+    dma("a", T.yl[:, 384:768], T.OL[:, 6:12], ["OL06", "OL16", "OLz0", "OLz1"], [], 128 * 384 * 4)
     return ops, nsend * len([op for op in ops if op["kind"] == "s"])
 
 
@@ -621,7 +688,7 @@ def order(ops):
         x = (x * 1103515245 + 12345) % 2147483648
         prio[i] += OPT["jit"] * x / 2147483648.0
         if ops[i]["h"] == 0:
-            prio[i] += OPT["lead"]
+            prio[i] += OPT["lead"] if ops[i]["i"] < OPT["turn"] else OPT["lead2"]
     left = [len(op["pre"]) for op in ops]
     rdy = [0.0] * n
     for i in range(n):
@@ -737,7 +804,7 @@ def polish(ops, seq, rounds, paces):
     return seq
 
 
-PACES = [(1.56, 1.0, 0.15, 0.07, 1.0), (1.3, 1.2, 0.3, 0.1, 1.3), (1.9, 0.9, 0.2, 0.05, 1.0)]
+PACES = [(1.56, 1.0, 0.27, 0.09, 1.0), (1.3, 1.1, 0.33, 0.12, 1.3), (1.9, 0.9, 0.18, 0.07, 1.0)]
 ORDER = {}
 
 

@@ -9,40 +9,45 @@ JH = KH // 16
 NV, NS = 3, 4
 NL = NV * NS
 LW = NL * JH
-BW = KH + 3 * JH
-OFF = 2047.0
-NF32, NI32, NU16, NF16, NB16 = 560, 64, 96, 64, 80
+OFF = 2032.0
+TOP = OFF + CP
+BIG = 8192.0
+NF32, NI32, NU16, NF16 = 400, 72, 100, 200
 
 SCRATCH = {
-    "F": ("sbuf", [128, C], "bfloat16"), "F1": ("sbuf", [128, C], "bfloat16"), "F2": ("sbuf", [128, C], "bfloat16"),
-    "G": ("sbuf", [128, 2 * CP + 16], "bfloat16"), "NX": ("sbuf", [128, C], "int32"),
+    "G": ("sbuf", [128, CP + C], "bfloat16"), "R": ("sbuf", [128, C], "bfloat16"), "LN": ("sbuf", [128, C], "float32"),
+    "NX": ("sbuf", [128, 2 * C], "int32"), "F": ("sbuf", [128, C], "bfloat16"),
     "W": ("sbuf", [128, 2 * K + 16], "bfloat16"), "B0": ("sbuf", [128, K], "bfloat16"), "M0": ("sbuf", [128, 64], "int32"),
     "P1": ("sbuf", [128, 2, 6, 16], "int32"), "P2": ("sbuf", [128, 6, 32], "float32"), "P3": ("sbuf", [128, 6, 32], "float32"),
     "PL": ("sbuf", [128, 192], "uint16"),
-    "ci": ("sbuf", [128, 16], "int32"), "cf": ("sbuf", [128, 16], "float32"),
+    "ci": ("sbuf", [128, 16], "int32"), "cf": ("sbuf", [128, 16], "float32"), "cb": ("sbuf", [128, 16], "bfloat16"),
     "ix": ("sbuf", [128, 144], "float32"), "ig": ("sbuf", [128, 128], "float32"),
     "t0": ("sbuf", [128, 128], "float32"), "t1": ("sbuf", [128, 128], "float32"), "t2": ("sbuf", [128, 128], "float32"),
-    "t3": ("sbuf", [128, 128], "float32"), "t4": ("sbuf", [128, 128], "float32"),
-    "EZ": ("sbuf", [128, 144], "bfloat16"), "ER": ("sbuf", [128, 144], "float16"),
-    "IB": ("sbuf", [128, 128], "bfloat16"), "IC": ("sbuf", [128, 128], "bfloat16"),
-    "NB": ("sbuf", [128, 128], "bfloat16"), "BC": ("sbuf", [128, K], "bfloat16"), "FG": ("sbuf", [128, K], "bfloat16"),
-    "IH": ("sbuf", [128, 128], "float16"), "L0": ("sbuf", [128, H * NS * JH], "float16"),
-    "M1": ("sbuf", [128, 128], "bfloat16"), "M2": ("sbuf", [128, 128], "bfloat16"),
-    "PLC": ("sbuf", [128, LW], "bfloat16"), "COFF": ("sbuf", [128, LW], "float16"), "CEMP": ("sbuf", [128, LW], "float16"),
+    "t3": ("sbuf", [128, 128], "float32"), "t4": ("sbuf", [128, 128], "float32"), "t5": ("sbuf", [128, 128], "float32"),
+    "EZ": ("sbuf", [128, 144], "bfloat16"), "ER": ("sbuf", [128, 144], "float16"), "EP": ("sbuf", [128, 144], "float16"),
+    "IB": ("sbuf", [128, 128], "bfloat16"), "IH": ("sbuf", [128, 128], "float16"), "NH": ("sbuf", [128, 128], "float16"),
+    "I5": ("sbuf", [128, 128], "float16"), "IP": ("sbuf", [128, 128], "float16"), "I8": ("sbuf", [128, 128], "float16"),
+    "IK": ("sbuf", [128, 128], "float16"),
+    "M1": ("sbuf", [128, 128], "bfloat16"), "M2": ("sbuf", [128, 128], "bfloat16"), "M3": ("sbuf", [128, 128], "bfloat16"),
+    "L0": ("sbuf", [128, H * NS * JH], "float16"),
+    "PLC": ("sbuf", [128, LW], "float16"), "COFF": ("sbuf", [128, LW], "float16"), "CEMP": ("sbuf", [128, LW], "float16"),
     "KI": ("sbuf", [128, 64], "float32"), "KJ": ("sbuf", [128, 64], "float32"),
     "BI": ("sbuf", [128, 24], "float32"), "BO": ("sbuf", [128, 24], "uint16"),
-    "zf": ("sbuf", [128, JH], "float32"), "zb": ("sbuf", [128, JH], "bfloat16"),
-    "zh": ("sbuf", [128, JH], "float16"), "oh": ("sbuf", [128, JH], "float16"),
+    "oh": ("sbuf", [128, JH], "float16"), "mh": ("sbuf", [128, JH], "float16"),
     "lf": ("sbuf", [128, NF32 * JH], "float32"), "li": ("sbuf", [128, NI32 * JH], "int32"),
-    "lu": ("sbuf", [128, NU16 * JH], "uint16"), "lh": ("sbuf", [128, NF16 * JH], "float16"), "lb": ("sbuf", [128, NB16 * JH], "bfloat16"),
-    "S1": ("sbuf", [128, K], "bfloat16"), "S2": ("sbuf", [128, K], "bfloat16"), "XG": ("sbuf", [128, K], "float32"),
-    "GG": ("sbuf", [128, K], "bfloat16"), "Y": ("sbuf", [128, K], "float16"),
-    "SG": ("sbuf", [128, 2 * K], "bfloat16"), "LG": ("sbuf", [128, 2 * K], "bfloat16"), "X2": ("sbuf", [128, K], "float16"),
-    "XS": ("sbuf", [128, K], "float16"), "BA": ("sbuf", [128, K], "bfloat16"), "BB": ("sbuf", [128, K], "bfloat16"),
-    "MA": ("sbuf", [128, H * LW], "bfloat16"), "MB": ("sbuf", [128, H * LW], "bfloat16"),
-    "U": ("sbuf", [128, H * LW], "float16"), "R": ("sbuf", [128, H * LW], "float16"), "U2": ("sbuf", [128, H * LW], "float32"),
-    "SB": ("sbuf", [128, 2 * H * BW], "bfloat16"), "LB": ("sbuf", [128, 2 * H * BW], "bfloat16"), "N2": ("sbuf", [128, 128], "bfloat16"),
-    "SL": ("sbuf", [128, 2 * H * 16 * JH], "float16"), "LL": ("sbuf", [128, 2 * H * 16 * JH], "float16"),
+    "lu": ("sbuf", [128, NU16 * JH], "uint16"), "lh": ("sbuf", [128, NF16 * JH], "float16"),
+    "Q": ("sbuf", [128, K], "float16"), "S1": ("sbuf", [128, K], "bfloat16"), "S2": ("sbuf", [128, K], "bfloat16"),
+    "XG": ("sbuf", [128, K], "float32"), "PN": ("sbuf", [128, K], "float16"),
+    "GG": ("sbuf", [128, K], "float16"), "Y": ("sbuf", [128, K], "float16"),
+    "BA": ("sbuf", [128, K], "float16"), "BB": ("sbuf", [128, K], "float16"), "BC": ("sbuf", [128, K], "float16"),
+    "XS": ("sbuf", [128, K], "float16"),
+    "MA": ("sbuf", [128, H * LW], "float16"), "MB": ("sbuf", [128, H * LW], "float16"), "MD": ("sbuf", [128, H * LW], "float16"),
+    "U": ("sbuf", [128, H * LW], "float16"), "RR": ("sbuf", [128, H * LW], "float16"), "U2": ("sbuf", [128, H * LW], "float16"),
+    "SB": ("sbuf", [128, 2 * K], "float16"), "LB": ("sbuf", [128, 2 * K], "float16"),
+    "SG": ("sbuf", [128, 2 * K], "float16"), "LG": ("sbuf", [128, 2 * K], "float16"),
+    "SJ": ("sbuf", [128, 2 * H * 4 * JH], "float16"), "LJ": ("sbuf", [128, 2 * H * 4 * JH], "float16"),
+    "LM": ("sbuf", [128, 2 * H * JH], "uint16"),
+    "SL": ("sbuf", [128, 2 * H * LW], "float16"), "LL": ("sbuf", [128, 2 * H * LW], "float16"),
     "OB": ("sbuf", [128, K], "float32"), "OL": ("sbuf", [128, NL, 64], "float32"),
     "OM": ("sbuf", [128, 64], "float32"), "OC": ("sbuf", [128, 64], "float32"),
 }
@@ -50,7 +55,7 @@ for _h in range(H):
     for _n in ("PP", "PB", "PG", "PS"):
         SCRATCH["%s%d" % (_n, _h)] = ("psum", [128, 512], "float32")
 
-NDMA = 40
+NDMA = 44
 SEMAPHORES = ["cv", "ca", "cp", "cg", "sent"] + ["d%d" % i for i in range(NDMA)] + ["r%d" % i for i in range(10 * H)]
 
 ALU = AluOpType
@@ -59,8 +64,9 @@ CY = 0.001
 PCY = 0.0005
 HOP = 0.3
 OWN = 0.08
-OPT = {"s1": "t", "s2": "a", "bv": "a", "gu": True, "gm": False, "lead": 3.0, "win": 0.3, "split": 2, "seed": 1790, "jit": 0.5,
-       "early": False, "lam": 30.0, "hold": 13.0, "late": 3, "f2": 1.0, "cut": 192, "turn": 11, "lead2": 0.0, "ahead": True, "both": False, "dl": 1.5, "rounds": 26000}
+OPT = {"xm": "p", "bv": "a", "s2": "a", "mk": "v", "lu": "v", "cen": "v", "gu": "g", "fb": "v", "late": 6, "np": 2, "pf": True, "link": 40e3,
+       "split": 2, "lead": 3.0, "lead2": 0.0, "turn": 11, "win": 0.3, "lam": 30.0, "hold": 13.0, "seed": 1790, "jit": 1.0,
+       "rounds": 20000, "pace": (1.56, 0.95, 0.35, 0.12, 1.1), "sweeps": 600, "again": 6}
 
 
 def build(g, T, topo, core, rank):
@@ -74,16 +80,22 @@ def build(g, T, topo, core, rank):
     nsend = len(topo.engines(core, nxt))
     V, A, PE = g.vector, g.scalar, g.tensor
 
+    def way(name, i):
+        return OPT[name][i % len(OPT[name])]
+
     def add(eng, fn, cost, r=(), w=(), x=(), kind="c", lat=0.0, sem=None, cnt=0):
         ops.append({"eng": eng, "fn": fn, "cost": cost, "r": list(r), "w": list(w), "x": list(x), "kind": kind,
                     "lat": lat, "sem": sem, "cnt": cnt, "h": cur[0], "i": cur[1]})
 
-    used = {"lf": 0, "li": 0, "lu": 0, "lh": 0, "lb": 0}
+    used = {"lf": 0, "li": 0, "lu": 0, "lh": 0}
 
     def slot(pool):
         i = used[pool]
         used[pool] += 1
-        return (T[pool][:, i * JH:(i + 1) * JH], "%s%d" % (pool, i), i * JH)
+        return (T[pool][:, i * JH:(i + 1) * JH], "%s%d" % (pool, i), pool, i * JH)
+
+    def pair(a):
+        return T[a[2]][:, a[3]:a[3] + 2 * JH]
 
     def tt(out, a, b, op, n=JH, f=2.0, x=()):
         add("v", lambda: V.tensor_tensor(out[0], a[0], b[0], op), max(64, n * f) * CY, [a[1], b[1]], [out[1]], x)
@@ -103,8 +115,9 @@ def build(g, T, topo, core, rank):
             list(win[1]) + [off[1], b[1]], [out[1]])
         ops[-1]["gn"] = n
 
-    def act(out, a, func, bias=0.0, scale=1.0, n=JH, x=()):
-        add("a", lambda: A.activation(out[0], a[0], func, bias=bias, scale=scale), max(64, n) * CY + 0.02, [a[1]], [out[1]], x)
+    def act(out, a, func, bias=0.0, scale=1.0, n=JH, x=(), r=(), more=0.0):
+        add("a", lambda: A.activation(out[0], a[0], func, bias=bias, scale=scale), max(64, n) * CY + 0.02 + more,
+            [a[1]] + list(r), [out[1]], x)
 
     def gact(out, win, off, func, bias, scale, n):
         add("a", lambda: A.activation(out[0], win[0].indirect(off[0]), func, bias=bias, scale=scale), 0.08 + 1.56 * n * CY,
@@ -127,11 +140,8 @@ def build(g, T, topo, core, rank):
     def dma(q, out, in_, r, w, nbytes):
         s = "d%d" % ndma[0]
         ndma[0] += 1
-        if q == "g":
-            add(q, lambda: g.dma_start(out, in_, accum_op=ALU.add), 0.6, r, w, kind="d", lat=OPT["dl"], sem=s, cnt=16)
-        else:
-            e = {"s": g.sync, "a": g.scalar}[q]
-            add(q, lambda: e.dma_start(out, in_), 0.06, r, w, kind="d", lat=2.0, sem=s, cnt=16)
+        e = {"s": g.sync, "a": g.scalar}[q]
+        add(q, lambda: e.dma_start(out, in_), 0.06, r, w, kind="d", lat=2.0, sem=s, cnt=16)
         ops[-1]["bytes"] = nbytes
 
     def gop(fn, n, w):
@@ -143,22 +153,26 @@ def build(g, T, topo, core, rank):
     for gr in range(8):
         q, hh = gr // 2, gr % 2
         if gr == 1:
-            dma("s", T.F[:, 0:fw], T.fm[:, 0:fw], [], ["F0"], 128 * fw * 2)
+            dma("s", T.G[:, 16:16 + fw], T.fm[:, 0:fw], [], ["F0"], 128 * fw * 2)
         dma("as"[hh], T.P1[32 * q:32 * q + 32, hh], T.nx[16 * gr, :], [], ["P1_%d" % gr], C * 4)
-    dma("s", T.F[:, fw:C], T.fm[:, fw:C], [], ["F1"], 128 * fw * 2)
+    dma("s", T.G[:, 16 + fw:CP], T.fm[:, fw:C], [], ["F1"], 128 * fw * 2)
     for h in range(H):
         dma("a", T.B0[:, h * KH:(h + 1) * KH], T.b0[:, h * KH:(h + 1) * KH], [], ["B0%d" % h], 128 * KH * 2)
     dma("s", T.NX[:, 0:C // 2], T.nx[:, 0:C // 2], [], ["NX0"], 128 * C * 2)
     dma("a", T.NX[:, C // 2:C], T.nx[:, C // 2:C], [], ["NX1"], 128 * C * 2)
-    dma("s", T.W[:, 0:2 * K], T.wl[:], ["NX0", "NX1"], ["W"], 128 * 2 * K * 2)
     FT = ["F%d" % i for i in range(NFP)]
 
     gop(lambda: g.iota(T.ci[:, 0:1], [[0, 1]], 0, 1), 1, ["ci0"])
     gop(lambda: g.iota(T.ix[:], [[1, 144]], 0, 0, allow_small_or_imprecise_dtypes=True), 144, ["ix"])
     gop(lambda: g.iota(T.ig[:], [[16, 8], [0, 16]], 0, 0, allow_small_or_imprecise_dtypes=True), 128, ["ig"])
-    gop(lambda: g.iota(T.PLC[:], [[1, NL], [0, JH]], 1, 0, allow_small_or_imprecise_dtypes=True), LW, ["PLC"])
+    gop(lambda: g.iota(T.LN[:, 0:LW], [[1, NL], [0, JH]], 1, 0, allow_small_or_imprecise_dtypes=True), LW, ["LN0"])
     gop(lambda: g.iota(T.KI[:], [[16, 64]], 0, 0, allow_small_or_imprecise_dtypes=True), 64, ["KI"])
     gop(lambda: g.iota(T.BI[:], [[0, 12], [16, 2]], 0, 0, allow_small_or_imprecise_dtypes=True), 24, ["BI"])
+    if "s" in OPT["xm"]:
+        gop(lambda: g.iota(T.NX[:, C:2 * C], [[0, C]], 0, 0), C, ["NXz"])
+    for gr in range(8 if "s" in OPT["xm"] else 0):
+        dma("s", T.NX[16 * gr:16 * gr + 1, C:2 * C], T.nx[16 * gr:16 * gr + 1, :], ["NXz"], ["NXp%d" % gr], C * 4)
+    dma("s", T.W[:, 0:2 * K], T.wl[:], ["NX0", "NX1"], ["W"], 128 * 2 * K * 2)
 
     def ci(i):
         return (T.ci[:, i:i + 1], "ci%d" % i)
@@ -175,96 +189,113 @@ def build(g, T, topo, core, rank):
     cp(cf(1), ci(1))
     cp(cf(2), ci(2))
     ts(cf(3), cf(2), 15.0, ALU.add)
-    ts(cf(4), cf(1), 0.0, ALU.is_gt, 2.0 * CP, ALU.mult)
-    ts(cf(5), cf(4), 2.0 * CP, ALU.add)
-    ts(cf(6), cf(1), 15.0, ALU.is_equal, 328.0, ALU.mult)
-    ts(cf(7), cf(6), -128.0, ALU.add)
-    ts(cf(8), cf(1), 15.0, ALU.is_equal, -0.5, ALU.mult)
-    for q, o in ((9, 0.0), (11, 128.0)) + (((14, -128.0),) if "t" in OPT["s1"] or "h" in OPT["s1"] else ()):
-        ts(cf(13), cf(1), 15.0, ALU.is_equal, 1000.0, ALU.mult)
-        ts(cf(q + 1), cf(13), -o, ALU.add)
-        ts(cf(q), cf(q + 1), 256.0, ALU.mult, -128.0, ALU.add)
+    ts(cf(4), cf(1), 0.0, ALU.is_gt, 3.0 * BIG, ALU.mult)
+    ts(cf(5), cf(4), -BIG, ALU.add)
+    ts(cf(6), cf(1), 15.0, ALU.is_equal)
+    ts(cf(7), cf(6), -1000.0, ALU.mult)
+    ts(cf(8), cf(6), 32768.0, ALU.mult, 2.0, ALU.add)
+    thr = (T.cb[:, 0:1], "cb0")
+    cp(thr, cf(8))
+    nthr = (T.cb[:, 1:2], "cb1")
+    ts(nthr, cf(8), -1.0, ALU.mult)
+    ts(cf(9), cf(1), 0.0, ALU.is_equal)
     ixs = (T.ix[:, 0:128], "ix")
     ts(whole("EZ"), whole("ix"), cf(3)[0], ALU.is_equal, cf(5)[0], ALU.mult, n=144, r=["cf3", "cf5"])
-    ts(whole("IC"), ixs, cf(0)[0], ALU.is_equal, -1.0 * CP, ALU.mult, n=128, r=["cf0"])
     ts(whole("t0"), whole("ig"), cf(2)[0], ALU.is_equal, n=128, r=["cf2"])
     ts(whole("t1"), ixs, cf(0)[0], ALU.is_equal, n=128, r=["cf0"])
     ts(whole("t2"), ixs, cf(0)[0], ALU.is_gt, n=128, r=["cf0"])
-    ts(whole("t3"), whole("t1"), 16.0, ALU.mult, -1.0, ALU.add, n=128)
-    ts(whole("t4"), whole("t2"), -14.0, ALU.mult, n=128)
+    ts(whole("t3"), whole("t1"), 32.0, ALU.mult, -2.0, ALU.add, n=128)
+    ts(whole("t4"), whole("t2"), -28.0, ALU.mult, n=128)
     tt(whole("t3"), whole("t3"), whole("t4"), ALU.add, n=128)
     tt(whole("M1"), whole("t3"), whole("t0"), ALU.mult, n=128)
     tt(whole("t4"), whole("t1"), whole("t2"), ALU.subtract, n=128)
-    ts(whole("t2"), whole("t4"), cf(8)[0], ALU.add, n=128, r=["cf8"])
+    ts(whole("t2"), whole("t4"), 2.0, ALU.mult, cf(6)[0], ALU.subtract, n=128, r=["cf6"])
     tt(whole("M2"), whole("t2"), whole("t0"), ALU.mult, n=128)
+    if "a" in OPT["s2"]:
+        tt(whole("t5"), whole("ig"), ixs, ALU.subtract, n=128)
+        ts(whole("t5"), whole("t5"), cf(6)[0], ALU.mult, n=128, r=["cf6"])
+        tt(whole("t5"), whole("t5"), whole("t4"), ALU.add, n=128)
+        tt(whole("M3"), whole("t5"), whole("t0"), ALU.mult, n=128)
     ts(whole("ER"), whole("ix"), cf(3)[0], ALU.is_equal, 4096.0, ALU.mult, n=144, r=["cf3"])
+    ts(whole("EP"), whole("ix"), cf(3)[0], ALU.is_equal, cf(9)[0], ALU.mult, n=144, r=["cf3", "cf9"])
     cp(whole("IB"), whole("t1"), 128)
     cp(whole("IH"), whole("t1"), 128)
-    ts(whole("NB"), whole("t1"), -1.0, ALU.mult, n=128)
-    ts(whole("N2"), whole("t1"), -2.0, ALU.mult, n=128)
+    for name, val in (("NH", -1.0), ("I5", TOP), ("IP", -1.0 * CP), ("I8", BIG), ("IK", OFF + 1.0)):
+        ts(whole(name), whole("IH"), val, ALU.mult, n=128, f=0.5)
+    cp(whole("PLC"), (T.LN[:, 0:LW], "LN0"), LW)
     ts(whole("COFF"), whole("PLC"), 0.0, ALU.mult, OFF, ALU.add, n=LW, f=0.5)
     ts(whole("CEMP"), whole("PLC"), 0.0, ALU.mult, -OFF - 1.0, ALU.add, n=LW, f=0.5)
     ts(whole("KJ"), whole("KI"), cf(1)[0], ALU.add, n=64, r=["cf1"])
     ts(whole("BO"), whole("BI"), cf(1)[0], ALU.add, n=24, r=["cf1"])
-    add("v", lambda: V.memset(T.zf[:], 0.0), 64 * CY, [], ["zf"])
-    add("v", lambda: V.memset(T.zb[:], 0.0), 64 * CY, [], ["zb"])
-    ts(whole("oh"), whole("zf"), 1.0, ALU.add)
-    add("v", lambda: V.memset(T.G[:, C:CP], 0.0), 64 * CY, [], ["Gz0"])
-    add("v", lambda: V.memset(T.G[:, CP + C:2 * CP + 16], 0.0), 64 * CY, [], ["Gz1"])
+    ts(whole("oh"), (T.PLC[:, 0:JH], "PLC"), 1.0, ALU.mult)
+    ts(whole("mh"), (T.PLC[:, 0:JH], "PLC"), -1.0, ALU.mult)
+    add("v", lambda: V.memset(T.G[:, 0:16], 0.0), 64 * CY, [], ["Gz"])
     add("v", lambda: V.memset(T.W[:, 2 * K:2 * K + 16], 0.0), 64 * CY, [], ["Wz"])
     for v in range(2):
         for h in range(H):
-            o = (v * H + h) * 16 * JH
+            o = (v * H + h) * LW
             wv = NS * (v + 1)
-            cp((T.LL[:, o + (4 + wv) * JH:o + 16 * JH], "LX%de" % (v * H + h)), (T.CEMP[:, 0:(NL - wv) * JH], "CEMP"), 128)
+            cp((T.LL[:, o + wv * JH:o + LW], "LX%de" % (v * H + h)), (T.CEMP[:, 0:(NL - wv) * JH], "CEMP"), 128)
 
-    for i in range(NFP):
-        sl = slice(i * fw, (i + 1) * fw)
-        ts((T.G[:, sl], "GN%d" % i), (T.F[:, sl], "F%d" % i), -1.0, ALU.mult, n=fw, f=0.5)
-        if OPT["s1"] != "v":
-            act((T.F1[:, sl], "F1_%d" % i), (T.F[:, sl], "F%d" % i), ACT.Identity, bias=-128.0, n=fw)
-        if "g" in OPT["s2"]:
-            ts((T.F2[:, sl], "F2_%d" % i), (T.F[:, sl], "F%d" % i), 2.0, ALU.mult, cf(7)[0], ALU.add, n=fw, f=0.5, r=["cf7"])
+    NRP = 4
+    rw = C // NRP
+    for i in range(NRP):
+        act((T.LN[:, i * rw:(i + 1) * rw], "LN%d" % i), (T.G[:, 16 + i * rw:16 + (i + 1) * rw], "F%d" % (i * NFP // NRP)), ACT.Ln,
+            bias=0.05, n=rw, more=1.3 if i == 0 else 0.0, r=["LN%d" % (i - 1)] if i else [])
+    for i in range(NRP):
+        act((T.R[:, i * rw:(i + 1) * rw], "R%d" % i), (T.LN[:, i * rw:(i + 1) * rw], "LN%d" % i), ACT.Exp, scale=-1.0, n=rw,
+            more=1.5 if i == 0 else 0.0, r=["LN%d" % (NRP - 1)] + (["R%d" % (i - 1)] if i else []))
     for hh in range(2):
         add("v", lambda hh=hh: V.tensor_copy(T.P2[:, :, 16 * hh:16 * hh + 16], T.P1[:, hh]), 96 * CY,
             ["P1_%d" % (2 * q + hh) for q in range(4)], ["P2_%d" % hh])
     for b in range(6):
         add("v", lambda b=b: V.transpose(T.P3[:, b, :], T.P2[:, b, :]), 64 * CY, ["P2_0", "P2_1"], ["P3_%d" % b])
         cp((T.PL[:, b::6], "PL%d" % b), (T.P3[:, b, :], "P3_%d" % b))
-    GN = ["GN%d" % i for i in range(NFP)]
     NDP = 6
     dw = C // NDP
     for i in range(NDP):
+        add("g", lambda i=i: g.affine_select(T.F[:, i * dw:(i + 1) * dw], T.G[:, 16 + i * dw:16 + (i + 1) * dw], [[0, dw]], ALU.is_ge, 0.0, 0, 0),
+            0.17 + 2 * dw * CY, ["F%d" % (i * NFP // NDP)], ["FC%d" % i])
         add("v", lambda i=i: V.tensor_tensor(T.G[:, CP + i * dw:CP + (i + 1) * dw],
-                                             T.G[:, 0:C].indirect(T.PL[:, i * dw // 16:(i + 1) * dw // 16]),
-                                             T.F[:, i * dw:(i + 1) * dw], ALU.add),
-            0.06 + 1.56 * dw * CY, GN + FT + ["PL%d" % b for b in range(6)], ["GD%d" % i])
-    winF = (T.F[:], FT)
-    winF1 = (T.F1[:], ["F1_%d" % i for i in range(NFP)])
-    winF2 = (T.F2[:], ["F2_%d" % i for i in range(NFP)])
-    winG0 = (T.G[:, 0:CP], GN + ["Gz0"])
-    winG = (T.G[:], GN + ["Gz0", "Gz1"] + ["GD%d" % i for i in range(NDP)])
-    winX = (T.NX[:], ["NX0", "NX1"])
+                                             T.G[:, 16:CP].indirect(T.PL[:, i * dw // 16:(i + 1) * dw // 16]),
+                                             T.F[:, i * dw:(i + 1) * dw], ALU.subtract),
+            0.06 + 1.56 * dw * CY, FT + ["FC%d" % i] + ["PL%d" % b for b in range(6)], ["GD%d" % i])
+        ops[-1]["gn"] = dw
+    winF = (T.G[:, 16:CP], FT)
+    winR = (T.R[:], ["R%d" % i for i in range(NRP)])
+    winG0 = (T.G[:, 0:CP], FT + ["Gz"])
+    winG = (T.G[:], FT + ["Gz"] + ["GD%d" % i for i in range(NDP)])
+    winX = (T.NX[:, 0:C], ["NX0", "NX1"])
+    winX2 = (T.NX[:], ["NX0", "NX1"] + ["NXp%d" % i for i in range(8)])
     winW = (T.W[:], ["W", "Wz"])
 
     def big(name, h, w=KH):
-        return (T[name][:, h * KH:h * KH + w], "%s%d" % (name, h), (name, h * KH))
+        return (T[name][:, h * KH:h * KH + w], "%s%d" % (name, h))
 
     def wide(name, h, blocks):
         return (T[name][:, h * LW:h * LW + blocks * JH], "%s%d" % (name, h))
 
-    def spread(bank, col, src, blocks, one="IH"):
-        mm([(T[bank][:, col + s * JH:col + (s + 1) * JH], T[one][:], src[0], JH) for s in range(blocks)],
-           [one, src[1]], [bank + "w"], bank, alone=True)
+    def spread(bank, col, src, blocks, less=False):
+        items = [(T[bank][:, col + s * JH:col + (s + 1) * JH], T.IH[:], src[0], JH) for s in range(blocks)]
+        if less:
+            items = [(T[bank][:, col:col + blocks * JH], T.NH[:], T.PLC[:, 0:blocks * JH], blocks * JH)] + items
+        mm(items, ["IH", "NH", "PLC", src[1]], [bank + "w"], bank, alone=not less)
 
-    def mask(h, st, blocks, name):
-        ps = "PS%d" % h
+    def mask(h, c1, blocks, name, how):
+        ps = "PP%d" % h
         mk = wide(name, h, blocks)
-        if OPT["gm"]:
-            gtt(mk, (st["c1"][0], [st["c1"][1]]), (T.BO[:, 0:2 * blocks], "BO"), (T.PLC[:, 0:blocks * JH], "PLC"), ALU.is_equal, blocks * JH)
-            return mk
-        spread(ps, 128, st["c1"], blocks, "IB")
-        tt(mk, (T[ps][:, 128:128 + blocks * JH], ps + "w"), (T.PLC[:, 0:blocks * JH], "PLC"), ALU.is_equal, n=blocks * JH, f=1.0, x=[ps])
+        n = blocks * JH
+        pw = (T[ps][:, 0:n], ps + "w")
+        spread(ps, 0, c1, blocks, how != "v")
+        if how == "v":
+            tt(mk, pw, (T.PLC[:, 0:n], "PLC"), ALU.is_equal, n=n, f=1.0, x=[ps])
+        else:
+            md = wide("MD", h, blocks)
+            act(md, pw, ACT.Abs, n=n, x=[ps])
+            if how == "a":
+                act(mk, md, ACT.Relu, bias=1.0, scale=-1.0, n=n)
+            else:
+                ts(mk, md, 0.5, ALU.is_lt, n=n, f=0.5)
         return mk
 
     def first(h):
@@ -272,46 +303,31 @@ def build(g, T, topo, core, rank):
         m0 = (T.M0[:, h * JH:(h + 1) * JH], "M0")
         st["m16"] = slot("lu")
         cp(st["m16"], m0)
-        st["m"] = m0
+        st["m"] = slot("lf")
+        ts(st["m"], m0, float(CP), ALU.add)
         st["B"] = big("B0", h)
-        st["e"] = whole("zf")
-        st["tn"] = whole("zf")
-        st["c1"] = whole("zf")
-        st["n1"] = whole("oh")
-        st["has"] = whole("zb")
-        st["M"] = None
         st["L"] = ("L0", h * NS * JH, "L0%d" % h)
-        cp((T.L0[:, h * NS * JH:(h + 1) * NS * JH], "L0%d" % h), (T.CEMP[:, 0:NS * JH], "CEMP"), 64)
+        cp((T.L0[:, (h * NS + 1) * JH:(h + 1) * NS * JH], "L0%de" % h), (T.CEMP[:, 0:(NS - 1) * JH], "CEMP"), 64)
         return st
 
     def arrive(v, h, old):
-        st = {}
+        st = {"low": True}
         k = (v - 1) * H + h
-        o = k * 16 * JH
-        wv = NS * v
-        ll = "LL%d" % k
+        st["m16"] = (T.LM[:, k * JH:(k + 1) * JH], "LM%d" % k, "LM", k * JH)
+        st["m"] = slot("lf")
+        ts(st["m"], st["m16"], float(CP), ALU.add)
 
         def part(i):
-            return (T.LL[:, o + i * JH:o + (i + 1) * JH], ll)
-        st["m16"] = slot("lu")
-        ts(st["m16"], part(0), OFF, ALU.add)
-        st["m"] = slot("lf")
-        ts(st["m"], part(0), OFF, ALU.add)
-        st["tn"] = part(1)
-        lj = ("LJ%d" if OPT["late"] else "LB%d") % k
-        st["c1"] = (T.LB[:, k * BW + KH + JH:k * BW + KH + 2 * JH], lj)
-        st["n1"] = (T.LB[:, k * BW + KH + 2 * JH:(k + 1) * BW], lj)
-        st["e"] = slot("lf")
-        tt(st["e"], part(1), part(0), ALU.subtract)
-        st["has"] = slot("lb")
-        act(st["has"], st["c1"], ACT.Sign)
-        o3 = (T.LB[:, k * BW + KH:k * BW + KH + JH], lj)
+            o = (4 * k + i) * JH
+            return (T.LJ[:, o:o + JH], "LJ%d" % k, "LJ", o)
+        st["c1"], st["n1"], st["t"] = part(1), part(2), part(3)
+        o3 = part(0)
         st["wall"] = o3
         if v > 1:
             d = slot("lf")
             tt(d, o3, old["wall"], ALU.is_equal)
             ez = slot("lf")
-            ts(ez, d, 2.0 * K, ALU.mult)
+            act(ez, d, ACT.Copy, scale=2.0 * K)
             o4 = slot("lf")
             tt(o4, o3, ez, ALU.max)
             o3 = o4
@@ -319,303 +335,328 @@ def build(g, T, topo, core, rank):
         tt(o2, o3, (T.KJ[:, h * JH:(h + 1) * JH], "KJ"), ALU.add)
         ts(o16, o2, 2.0 * K, ALU.min)
         bs = big("BB", h)
-        lb = (T.LB[:, k * BW:k * BW + KH], "LB%d" % k)
-        if OPT["late"] == 3:
-            tt(bs, lb, (T.LG[:, k * KH:(k + 1) * KH], "LG%d" % k), ALU.add, n=KH, f=OPT["f2"])
-            st["raw"] = big("XS", h)
-            gtt(st["raw"], winW, o16, bs, ALU.add, KH)
-            bs = st["raw"]
-        elif OPT["late"]:
-            gact(bs, winW, o16, ACT.Copy, 0.0, 1.0, KH)
-            st["lb"], st["wg"] = lb, bs
-            bs = big("XS", h)
-            tt(bs, st["wg"], lb, ALU.add, n=KH, f=OPT["f2"])
-            if OPT["ahead"]:
-                st["lb"], st["wg"] = (T.LG[:, k * KH:(k + 1) * KH], "LG%d" % k), bs
-                bs = big("X2", h)
-                tt(bs, st["wg"], st["lb"], ALU.add, n=KH, f=OPT["f2"])
+        lb = (T.LB[:, k * KH:(k + 1) * KH], "LB%d" % k)
+        lg = (T.LG[:, k * KH:(k + 1) * KH], "LG%d" % k)
+        st["raw"] = big("XS", h)
+        if OPT["late"] >= 5:
+            npc = OPT["np"]
+            pw = KH // npc
+            if OPT["late"] == 6:
+                gact(bs, winW, o16, ACT.Copy, 0.0, 1.0, KH)
+            for a in range(npc):
+                ra = (T.XS[:, h * KH + a * pw:h * KH + (a + 1) * pw], "XS%d_%d" % (h, a))
+                la = (T.LB[:, k * KH + a * pw:k * KH + (a + 1) * pw], "LB%d_%d" % (k, a))
+                if OPT["late"] == 6:
+                    tt(ra, (T.BB[:, h * KH + a * pw:h * KH + (a + 1) * pw], bs[1]), la, ALU.subtract, n=pw, f=1.0)
+                else:
+                    gtt(ra, winW, (T.lu[:, o16[3] + a * pw // 16:o16[3] + (a + 1) * pw // 16], o16[1]), la, ALU.subtract, pw)
+            st["cut"] = npc
+            st["raw"] = (st["raw"][0], "XS%d_0" % h)
+        elif OPT["late"] == 3:
+            tt(bs, lb, lg, ALU.add, n=KH, f=1.0)
+            gtt(st["raw"], winW, o16, bs, ALU.subtract, KH)
         else:
-            gtt(bs, winW, o16, lb, ALU.add, KH)
-        if OPT["late"] == 2:
-            del st["lb"]
-            st["raw"] = bs
+            gtt(bs, winW, o16, lb, ALU.subtract, KH)
+            tt(st["raw"], bs, lg, ALU.subtract, n=KH, f=1.0)
         st["B"] = big("BA", h)
-        ts(st["B"], bs, 127.0, ALU.min, n=KH, f=0.5)
-        st["L"] = ("LL", o + 4 * JH, "LX%d" % k)
-        st["M"] = mask(h, st, wv, "MA")
+        ts(st["B"], st["raw"], -1.0, ALU.mult, -255.5, ALU.max, n=KH, f=0.5, r=["XS%d_%d" % (h, a) for a in range(st.get("cut", 0))])
+        st["L"] = ("LL", k * LW, "LX%d" % k)
+        st["M"] = mask(h, st["c1"], NS * v, "MA", way("mk", NS * v))
         return st
 
     def send(k, part, src, dst, r, w, nbytes):
         s = "r%d" % (5 * k + part)
         add("g", lambda: g.remote_dma(dst, src, T.sem[s], T.sem.sent, pid, rid, emask), 0.6, r, ["fly" + w], kind="s")
-        add("x", None, 0.0, ["fly" + w], [w], kind="r", lat=2.5 + nbytes / 40e3, sem=s, cnt=neng)
+        add("x", None, nbytes / OPT["link"], ["fly" + w], [w], kind="r", lat=2.5, sem=s, cnt=neng)
 
     def step(i, h, st):
-        v, s = divmod(i, NS)
+        v_, s = divmod(i, NS)
         leave = s == NS - 1 and i < NL - 1
+        ahead = s == NS - 2 and v_ < NV - 1 and OPT["late"] < 5
+        fetch = leave and OPT["pf"]
         last = i == NL - 1
+        par = i > 0 and way("xm", i) == "p"
+        low = TOP if st.get("low") else 0.0
         pp, pb, pg, ps = "PP%d" % h, "PB%d" % h, "PG%d" % h, "PS%d" % h
-        k_ = v * H + h
-        so = k_ * 16 * JH
+        k_ = v_ * H + h
 
         def spart(j):
-            return (T.SL[:, so + j * JH:so + (j + 1) * JH], "SL%d_%d" % (k_, j))
-        nw = {"wall": st.get("wall")}
-        B, m = st.get("B"), st["m"]
-        s1, s2 = big("S1", h), big("S2", h)
+            o = (4 * k_ + j) * JH
+            return (T.SJ[:, o:o + JH], "SJ%d_%d" % (k_, j), "SJ", o)
+        nw = {"wall": st.get("wall"), "L": st["L"]}
+        B, m, m16 = st["B"], st["m"], st["m16"]
+        s1, s2, qq = big("S1", h), big("S2", h), big("Q", h)
         pbw = (T[pb][:], pb + "w")
-        ppw = (T[pp][:], pp + "w")
-        way1 = "v" if "lb" in st else OPT["s1"][i % len(OPT["s1"])]
-        way2 = OPT["s2"][i % len(OPT["s2"])]
-        if way2 == "g" and (i == 0 or "lb" in st):
-            way2 = "a"
-        fg = big("FG", h)
-        low = way1 in "th" and i > 0
-        cut = OPT["cut"]
-        if way1 == "h":
-            o16 = st["m16"][2]
-            fgb = (T.FG[:, h * KH + cut:(h + 1) * KH], "FGb%d" % h)
-            gact(fgb, winF1 if low else winF, (T.lu[:, o16 + cut // 16:o16 + JH], st["m16"][1]), ACT.Copy, 0.0, 1.0, KH - cut)
-            add("a", lambda: A.activation(T.FG[:, h * KH:h * KH + cut], (winF1 if low else winF)[0].indirect(T.lu[:, o16:o16 + cut // 16]), ACT.Copy),
-                0.08 + 1.56 * cut * CY, list((winF1 if low else winF)[1]) + [st["m16"][1], fgb[1]], [fg[1]])
-            ops[-1]["gn"] = cut
-        elif way1 != "g" or way2 != "g":
-            gact(fg, winF1 if low else winF, st["m16"], ACT.Copy, 0.0, 1.0, KH)
-
-        def less(bank, bw, lhs):
-            if "lb" in st:
-                one = "IH" if OPT["ahead"] else "IB"
-                mm([(bw[0], T[one][:], st["wg"][0], KH)], [one, st["wg"][1]], [bw[1]], bank, keep=True)
-                mm([(bw[0], T[lhs][:], fg[0], KH)], [lhs, fg[1], bw[1]], [bw[1]], bank, cont=True, keep=True)
-                mm([(bw[0], T.IB[:], st["lb"][0], KH)], ["IB", st["lb"][1], bw[1]], [bw[1]], bank, cont=True)
-            else:
-                one = "IH" if "raw" in st else "IB"
-                mm([(bw[0], T[one][:], Bc[0], KH)], [one, Bc[1]], [bw[1]], bank, keep=True)
-                mm([(bw[0], T[lhs][:], fg[0], KH)], [lhs, fg[1], "FGb%d" % h, bw[1]], [bw[1]], bank, cont=True)
-        Bc = st.get("raw", B)
-        if way1 == "g":
-            gtt(s1, winF if i == 0 else winF1, st["m16"], Bc, ALU.is_gt, KH)
-        elif way1 == "h":
-            bo = Bc[2]
-            s1a = (T.S1[:, h * KH:h * KH + cut], "S1a%d" % h)
-            add("v", lambda: V.tensor_tensor(s1a[0], (winF1 if low else winF)[0].indirect(T.lu[:, o16:o16 + cut // 16]), T[bo[0]][:, bo[1]:bo[1] + cut], ALU.is_gt),
-                0.06 + 1.56 * cut * CY, list((winF1 if low else winF)[1]) + [st["m16"][1], Bc[1]], [s1a[1], s1[1]])
-            ops[-1]["gn"] = cut
-            add("v", lambda: V.tensor_tensor(T.S1[:, h * KH + cut:(h + 1) * KH], fgb[0], T[bo[0]][:, bo[1] + cut:bo[1] + KH], ALU.is_gt),
-                (KH - cut) * CY, [fgb[1], Bc[1]], ["S1b%d" % h])
-        elif way1 == "t":
-            tt(s1, fg, Bc, ALU.is_gt, n=KH, f=OPT["f2"])
-        else:
-            less(pb, pbw, "NB")
-            ts(s1, pbw, 0.0 if i == 0 else -128.0, ALU.is_lt, n=KH, x=[pb])
-        q = 9 if i == 0 else 14 if low else 11
-        if way2 == "g":
-            gtt(s2, winF2, st["m16"], B, ALU.is_gt, KH)
-        else:
-            less(pp, ppw, "N2")
-            if way2 == "a":
-                add("a", lambda: A.activation(s2[0], ppw[0], ACT.Sigmoid, bias=cf(q)[0], scale=-256.0),
-                    KH * CY + 0.02 + (1.3 if i + h == 0 else 0), [ppw[1], cf(q)[1]], [s2[1]], [pp])
-            else:
-                ts(s2, ppw, cf(q + 1)[0], ALU.is_lt, n=KH, x=[pp], r=[cf(q + 1)[1]])
-        z = (T[ps][:, 0:JH], ps + "z")
-        mm([(z[0], T.IC[:], st["has"][0], JH)] +
-           [(z[0], T.EZ[:, 15 - r:143 - r], T.S1[:, h * KH + r:(h + 1) * KH:16], JH) for r in range(16)],
-           ["IC", "EZ", st["has"][1], s1[1], "S1b%d" % h], [z[1]], ps)
-        mm([(T[pp][:], T.M1[:], s1[0], KH), (T[pp][:], T.M2[:], s2[0], KH)], ["M1", "M2", s1[1], "S1b%d" % h, s2[1]], [pp + "w"], pp)
-        b, k = slot("lf"), slot("lf")
-        ts(b, z, float(CP), ALU.is_equal, x=[ps])
-        ts(k, z, 0.0, ALU.max, 2.0 * CP, ALU.min, x=[ps])
-        be, ix, ig = slot("lf"), slot("lf"), slot("lf")
-        ix16, ig16 = slot("lu"), slot("lu")
+        m2 = "M2"
         if i == 0:
-            ix, ix16, be = m, st["m16"], whole("zf")
+            gtt(s1, winF, m16, B, ALU.is_gt, KH)
+            ts(qq, B, 0.5, ALU.mult, cf(7)[0], ALU.add, n=KH, f=0.5, r=["cf7"])
+            gtt(s2, winF, m16, qq, ALU.is_gt, KH)
         else:
-            tt(be, b, st["e"], ALU.mult)
-            tt(ix, m, be, ALU.add)
-            if not OPT["both"]:
-                cp(ix16, ix)
-        tt(ig, ix, k, ALU.add)
-        if i > 0 and OPT["both"]:
-            add("v", lambda: V.tensor_scalar(T.lu[:, ix16[2]:ix16[2] + 2 * JH], T.lf[:, ix[2]:ix[2] + 2 * JH], 2.0 * CP, None, ALU.min),
-                64 * CY, [ix[1], ig[1]], [ix16[1], ig16[1]])
+            q2 = qq[1] + "b"
+            if st.get("cut", 1) > 1:
+                pw = KH // 2
+                for a in range(2):
+                    o = h * KH + a * pw
+                    gtt((T.Q[:, o:o + pw], q2 if a else qq[1]), winR, (T.LM[:, m16[3] + a * pw // 16:m16[3] + (a + 1) * pw // 16], m16[1]),
+                        (T.XS[:, o:o + pw], "XS%d_%d" % (h, a)), ALU.mult, pw)
+            else:
+                gtt(qq, winR, m16, st.get("raw", B), ALU.mult, KH)
+                ops[-1]["w"].append(q2)
+            up = "raw" in st
+            ts(s1, qq, 1.0 if up else -1.0, ALU.is_lt if up else ALU.is_gt, n=KH, f=0.5, r=[q2])
+            if way("s2", i) == "v":
+                th = thr if up else nthr
+                ts(s2, qq, th[0], ALU.is_lt if up else ALU.is_gt, n=KH, f=0.5, r=[th[1], q2])
+            else:
+                act(s2, qq, ACT.Sign, bias=cf(8)[0], scale=-1.0 if up else 1.0, n=KH, r=["cf8", q2])
+                m2 = "M3"
+        if par:
+            t16, pn = slot("lu"), big("PN", h)
+            ts(t16, st["t"], low - CP, ALU.add)
+            gact(pn, winX, t16, ACT.Identity, -OFF, 1.0, KH)
+            pr = (T[pg][:, LW:LW + JH], pg + "p")
+            mm([(pr[0], T.I8[:], T.mh[:], JH)] +
+               [(pr[0], T.EP[:, 15 - r:143 - r], T.PN[:, h * KH + r:(h + 1) * KH:16], JH) for r in range(16)],
+               ["I8", "mh", "EP", pn[1]], [pr[1]], pg, keep=True)
+        if fetch:
+            lbuf, lo, ltok = st["L"]
+            ru, nh = wide("U2", h, i - 1), slot("lh")
+            mn_ = st["M"][1]
+            tt(ru, (T[lbuf][:, lo:lo + (i - 1) * JH], ltok), (T[mn_[:2]][:, h * LW + JH:h * LW + i * JH], mn_), ALU.mult, n=(i - 1) * JH, f=1.0)
+            ts(nh, st["c1"], 1.5, ALU.is_lt, -1.0, ALU.mult)
+            tm = (T[pb][:, 0:JH], pb + "w")
+            mm([(tm[0], T.I8[:], T.mh[:], JH), (tm[0], T.I5[:], nh[0], JH)] +
+               [(tm[0], T.IH[:], T.U2[:, h * LW + s_ * JH:h * LW + (s_ + 1) * JH], JH) for s_ in range(i - 1)],
+               ["I8", "I5", "IH", "mh", nh[1], ru[1]], [tm[1]], pb, keep=True)
+        if last:
+            mk = mask(h, st["n1"], NL, "MB" if st["M"][1].startswith("MA") else "MA", way("mk", i))
+        z = (T[ps][:, 0:JH], ps + "z")
+        base = i > 0 and not low
+        mm(([(z[0], T.I5[:], T.oh[:], JH)] if base else []) +
+           [(z[0], T.EZ[:, 15 - r:143 - r], T.S1[:, h * KH + r:(h + 1) * KH:16], JH) for r in range(16)],
+           ["I5", "oh", "EZ", s1[1]], [z[1]], ps)
+        mm([(T[pp][:], T.M1[:], s1[0], KH), (T[pp][:], T[m2][:], s2[0], KH)], ["M1", m2, s1[1], s2[1]], [pp + "w"], pp)
+        b, nok = slot("lh"), slot("lh")
+        x, ix16, ig16 = slot("lf"), m16, slot("lu")
+        if i > 0:
+            v = slot("lf")
+            tt(v, st["t"], z, ALU.subtract, f=1.0, x=[ps])
+            if not par:
+                ix, ix16 = slot("lf"), slot("lu")
+                tt(ix, v, m, ALU.max)
+                ts(ix16, ix, -1.0 * CP, ALU.add)
+        ts(nok, z, TOP if base else 0.0, ALU.not_equal, BIG, ALU.mult, x=[ps])
+        tt(x, m, nok, ALU.subtract)
+        if i > 0:
+            ig = slot("lf")
+            tt(ig, v, x, ALU.max)
+            ts(ig16, ig, -1.0 * C, ALU.add)
+            if way("fb", i) == "v":
+                ts(b, v, CP + C - 0.5, ALU.is_gt)
+            else:
+                sg = slot("lf")
+                act(sg, v, ACT.Sign, bias=0.5 - CP - C)
+                act(b, sg, ACT.Relu)
         else:
-            ts(ig16, ig, float(C if i == 0 else 2 * CP), ALU.min)
-        xg, gg, y = big("XG", h), big("GG", h), big("Y", h)
+            ts(ig16, x, -1.0 * C, ALU.add)
         ys = []
-        pw = KH // OPT["split"]
+        pw = KH // (1 if par else OPT["split"])
         for a in range(0, KH, pw):
             xa = (T.XG[:, h * KH + a:h * KH + a + pw], "XG%d_%d" % (h, a))
             ya = (T.Y[:, h * KH + a:h * KH + a + pw], "Y%d_%d" % (h, a))
-            ox = ix16[2] + a // 16
-            gact(xa, winX, (T.lu[:, ox:ox + pw // 16], ix16[1]), ACT.Identity, -0.375, 1.0 / 4096, pw)
+            ox = ix16[3] + a // 16
+            gact(xa, winX if par or i == 0 else winX2, (T[ix16[2]][:, ox:ox + pw // 16], ix16[1]), ACT.Identity, -0.375, 1.0 / 4096, pw)
+            if par:
+                ops[-1]["w"] += ["XG%d_%d" % (h, KH // 2)]
             tt(ya, (T[pp][:, a:a + pw], pp + "w"), xa, ALU.min, n=pw, f=1.0, x=[pp])
+            if par:
+                ops[-1]["r"] += ["XG%d_%d" % (h, KH // 2)]
+                ops[-1]["w"] += ["Y%d_%d" % (h, KH // 2)]
+                ys.append("Y%d_%d" % (h, KH // 2))
             ys.append(ya[1])
-        ahead = OPT["ahead"] and s == NS - 2 and v < NV - 1
-        if leave or ahead:
-            nb = (T.SB[:, k_ * BW:k_ * BW + KH], "SB%d" % k_, ("SB", k_ * BW))
+        gg = big("GG", h)
+        if leave and OPT["late"] >= 5:
+            pw = KH // OPT["np"]
+            for a in range(OPT["np"]):
+                o = k_ * KH + a * pw
+                sb = (T.SB[:, o:o + pw], "SB%d_%d" % (k_, a))
+                gtt(sb, winG, (T.lu[:, ig16[3] + a * pw // 16:ig16[3] + (a + 1) * pw // 16], ig16[1]),
+                    (T[B[1][:2]][:, h * KH + a * pw:h * KH + (a + 1) * pw], B[1]), ALU.add, pw)
+                send(k_, 4 * a, sb[0], T.LB[:, o:o + pw], [sb[1]], "LB%d_%d" % (k_, a), 128 * pw * 2)
+        elif leave:
+            sg_ = (T.SG[:, k_ * KH:(k_ + 1) * KH], "SG%d" % k_)
+            gact(sg_, winG, ig16, ACT.Copy, 0.0, 1.0, KH)
+            send(k_, 4, sg_[0], T.LG[:, k_ * KH:(k_ + 1) * KH], [sg_[1]], "LG%d" % k_, 128 * KH * 2)
         else:
-            nb = big("BC" if B[1].startswith("BA") else "BA", h)
-        nw["B"] = nb
-        if leave and OPT["ahead"]:
-            sg = (T.SG[:, k_ * KH:(k_ + 1) * KH], "SG%d" % k_)
-            gact(sg, winG, ig16, ACT.Copy, 0.0, 1.0, KH)
-            send(k_, 4, sg[0], T.LG[:, k_ * KH:(k_ + 1) * KH], [sg[1]], "LG%d" % k_, 128 * KH * 2)
-        elif 0 < i < NL - 1 and OPT["bv"][i % len(OPT["bv"])] == "v":
-            gtt(nb, winG, ig16, B, ALU.add, KH)
-        elif i > 0 and s < NS - 1 and not ahead and OPT["bv"][i % len(OPT["bv"])] == "d":
-            gact(gg, winG, ig16, ACT.Copy, 0.0, 1.0, KH)
-            dma("g", B[0], gg[0], [gg[1], B[1]], [B[1]], 2 * 128 * KH * 2)
-            nw["B"] = B
-        else:
-            gact(gg, winG0 if i == 0 else winG, ig16, ACT.Copy, 0.0, 1.0, KH)
-            mm([(pbw[0], T.IB[:], B[0], KH)], ["IB", B[1]], [pbw[1]], pb, keep=True)
-            mm([(pbw[0], T.IB[:], gg[0], KH)], ["IB", gg[1], pbw[1]], [pbw[1]], pb, cont=True)
-            if last:
-                ob = big("OB", h)
-                act(ob, pbw, ACT.Identity, bias=128.0, n=KH, x=[pb])
-                dma("s", T.yb[:, h * KH:(h + 1) * KH], ob[0], [ob[1]], [], 128 * KH * 4)
+            if ahead:
+                nb = (T.SB[:, k_ * KH:(k_ + 1) * KH], "SB%d" % k_)
             else:
-                act(nb, pbw, ACT.Identity, bias=-128.0 if i == 0 else 0.0, n=KH, x=[pb])
-        if ahead:
-            send(k_, 0, nb[0], T.LB[:, k_ * BW:k_ * BW + KH], [nb[1]], "LB%d" % k_, 128 * KH * 2)
-        cb, nk = slot("lf"), slot("lf")
-        c1 = (T.SB[:, k_ * BW + KH + JH:k_ * BW + KH + 2 * JH], "SC%d" % k_) if leave else slot("lb")
-        tt(cb, st["c1"], b, ALU.subtract)
-        tt(nk, st["n1"], k, ALU.subtract)
-        tt(c1, cb, nk, ALU.max)
-        nw["c1"] = c1
-        if last:
-            ts((T.OC[:, h * JH:(h + 1) * JH], "OC%d" % h), c1, -1.0, ALU.add)
-        else:
-            ok = slot("lf")
-            act(ok, k, ACT.Relu, bias=1.0, scale=-1.0)
-            n1 = (T.SB[:, k_ * BW + KH + 2 * JH:(k_ + 1) * BW], "SN%d" % k_) if leave else slot("lb")
-            tt(n1, st["n1"], ok, ALU.add)
-            nw["n1"] = n1
-            if not leave:
-                nw["has"] = slot("lb")
-                act(nw["has"], c1, ACT.Sign)
-        x = slot("lf")
-        tt(x, m, k, ALU.subtract)
-        mk = mask(h, nw, i + 1, "MB" if (st["M"] is None or st["M"][1].startswith("MA")) else "MA")
-        nw["M"] = mk
-        if last:
-            okm = slot("lf")
-            ts(okm, x, 1.0, ALU.add, 0.0, ALU.max)
-            u2 = wide("U2", h, NL)
-            gtt(u2, (okm[0], [okm[1]]), whole("BO"), mk, ALU.mult, LW)
-        L = pg + "w"
-        tn = st["tn"]
-
+                nb = big("BC" if B[1].startswith("BA") else "BA", h)
+            nw["B"] = nb
+            how = way("bv", i) if 0 < i < NL - 1 else "a"
+            if how == "g":
+                gtt(nb, winG, ig16, B, ALU.add, KH)
+            else:
+                gact(gg, winG0 if i == 0 else winG, ig16, ACT.Copy, 0.0, -1.0 if i == 0 else 1.0, KH)
+            if how == "v":
+                tt(nb, B, gg, ALU.add, n=KH, f=1.0)
+            elif how == "a":
+                one = "IB" if i == 0 else "IH"
+                mm([(pbw[0], T[one][:], B[0], KH)], [one, B[1]], [pbw[1]], pb, keep=True)
+                mm([(pbw[0], T.IH[:], gg[0], KH)], ["IH", gg[1], pbw[1]], [pbw[1]], pb, cont=True)
+                if last:
+                    ob = big("OB", h)
+                    act(ob, pbw, ACT.Identity, bias=-0.5, scale=-1.0, n=KH, x=[pb])
+                    dma("s", T.yb[:, h * KH:(h + 1) * KH], ob[0], [ob[1]], [], 128 * KH * 4)
+                elif i == 0:
+                    act(nb, pbw, ACT.Identity, bias=-0.5, scale=-1.0, n=KH, x=[pb])
+                else:
+                    act(nb, pbw, ACT.Copy, n=KH, x=[pb])
+            if ahead:
+                send(k_, 0, nb[0], T.LB[:, k_ * KH:(k_ + 1) * KH], [nb[1]], "LB%d" % k_, 128 * KH * 2)
+        c1, n1 = (spart(1), spart(2)) if leave else (slot("lh"), slot("lh"))
+        nw["c1"], nw["n1"] = c1, n1
         lbuf, lo, ltok = st["L"]
-        nw["L"] = st["L"]
         lsb = (T[lbuf][:, lo:lo + (i + 1) * JH], ltok)
-
-        def take(extra):
-            rr = wide("R", h, i + 1)
-            if extra or i == 0:
-                tt(rr, lsb, mk, ALU.mult, n=(i + 1) * JH, f=OPT["f2"])
-            else:
-                tt(rr, (T[pg][:, 0:(i + 1) * JH], L), mk, ALU.mult, n=(i + 1) * JH, f=1.0, x=[pg])
-            tsum = (T[ps][:, 2 * JH:3 * JH], ps + "t")
-            mm([(tsum[0], T.IH[:], T.COFF[:, 0:JH], JH)] + [(tsum[0], T.IH[:], e_[0], JH) for e_ in extra] +
-               [(tsum[0], T.IH[:], T.R[:, h * LW + s_ * JH:h * LW + (s_ + 1) * JH], JH) for s_ in range(i + 1)],
-               ["IH", "COFF", rr[1]] + [e_[1] for e_ in extra], [tsum[1]], ps)
-            t = slot("lf")
-            tt(t, tsum, x, ALU.max, f=1.0, x=[ps])
-            return rr, t
-        early = leave or (OPT["early"] and not last and i > 0)
-        if early:
-            stay, stt, tn = slot("lf"), slot("lh"), slot("lf")
-            act(stay, k, ACT.Relu, bias=1.0 - 2.0 * CP)
-            tt(stt, stay, st["tn"], ALU.mult)
-            tt(tn, st["tn"], stt, ALU.subtract)
-            rr, t = take([stt])
-        if leave:
-            ti, j_, nz = slot("li"), slot("li"), slot("lf")
-            ts(ti, t, float(K), ALU.mult)
-            ts(j_, ti, K, ALU.bitwise_and)
-            ts(nz, c1, 0.5, ALU.is_lt, 2.0 * K, ALU.mult)
-            jw = (T.SB[:, k_ * BW + KH:k_ * BW + KH + JH], "SJ%d" % k_)
-            tt(jw, j_, nz, ALU.max)
-            if OPT["late"]:
-                send(k_, 3, T.SB[:, k_ * BW + KH:(k_ + 1) * BW], T.LB[:, k_ * BW + KH:(k_ + 1) * BW], [jw[1], c1[1], n1[1]], "LJ%d" % k_, 128 * 3 * JH * 2)
-                if not OPT["ahead"]:
-                    send(k_, 0, nb[0], T.LB[:, k_ * BW:k_ * BW + KH], [nb[1]], "LB%d" % k_, 128 * KH * 2)
-            else:
-                send(k_, 0, T.SB[:, k_ * BW:(k_ + 1) * BW], T.LB[:, k_ * BW:(k_ + 1) * BW], [nb[1], jw[1], c1[1], n1[1]], "LB%d" % k_, 128 * BW * 2)
-            ts(spart(1), t, -OFF, ALU.add)
-        rs = (T[ps][:, JH:2 * JH], ps + "r")
-        mm([(rs[0], T.ER[:, 15 - r:143 - r], T.Y[:, h * KH + r:(h + 1) * KH:16], JH) for r in range(16)],
-           ["ER"] + ys, [rs[1]], ps)
-        ri, r_ = slot("li"), slot("li")
-        ts(ri, rs, 8388608.0 - 512.0, ALU.add, x=[ps])
-        ts(r_, ri, 4095, ALU.bitwise_and)
         if i == 0:
-            mn = r_
+            act(c1, nok, ACT.Relu, bias=1.0, scale=-1.0)
+            act(n1, c1, ACT.Identity, bias=1.0)
+            act(lsb, c1, ACT.Identity, bias=-OFF - 1.0, scale=OFF + 1.0)
+            nw["M"], nw["t"] = c1, x
         else:
-            yy, by = slot("lf"), slot("lf")
-            mn = (T.OM[:, h * JH:(h + 1) * JH], "OM%d" % h) if last else slot("lf")
-            tt(yy, r_, m, ALU.subtract)
-            tt(by, b, yy, ALU.mult)
-            tt(mn, r_, by, ALU.subtract)
-        nw["m"] = mn
-        if leave:
-            ts(spart(0), mn, -OFF, ALU.add)
-            send(k_, 1, T.SL[:, so:so + 2 * JH], T.LL[:, so:so + 2 * JH], ["SL%d_%d" % (k_, j) for j in range(2)], "LL%d" % k_, 128 * 2 * JH * 2)
-        elif not last:
-            nw["m16"] = slot("lu")
-            cp(nw["m16"], mn)
-        if last:
-            w_ = slot("lf")
-            tt(w_, tn, be, ALU.subtract)
+            cb, nk = slot("lh"), slot("lh")
+            add("v", lambda: V.tensor_tensor(pair(cb), pair(st["c1"]), pair(b), ALU.subtract), 64 * CY,
+                [st["c1"][1], st["n1"][1], b[1], nok[1]], [cb[1], nk[1]])
+            tt(c1, cb, nk, ALU.max)
+            if last:
+                act((T.OC[:, h * JH:(h + 1) * JH], "OC%d" % h), c1, ACT.Identity, bias=-1.0)
+            else:
+                ok, has = slot("lh"), slot("lh")
+                act(ok, nok, ACT.Relu, bias=1.0, scale=-1.0)
+                tt(n1, st["n1"], ok, ALU.add)
+                if not fetch:
+                    act(has, c1, ACT.Sign)
+            mb, bb, tb = slot("lf"), slot("lf"), slot("lf")
+            tt(mb, b, m, ALU.mult)
+            if par:
+                act(bb, b, ACT.Identity, bias=low - TOP, scale=-BIG)
+            else:
+                act(bb, b, ACT.Identity, bias=low - CP, scale=BIG)
+            tt(tb, st["t"], bb, ALU.add)
+            mo = st["M"]
+            if not last:
+                mk = mask(h, c1, i + 1, "MB" if mo[1].startswith("MA") else "MA", way("mk", i))
+            nw["M"] = mk
+        L = pg + "w"
+        n_ = (i + 1) * JH
+
+        def put(vn):
             u = wide("U", h, i)
-            mo = (T[st["M"][1][:2]][:, h * LW:h * LW + i * JH], st["M"][1])
-            gtt(u, (w_[0], [w_[1]]), (T.BO[:, 0:2 * i], "BO"), mo, ALU.mult, i * JH)
-            mm([(T[pg][:, 0:LW], T.IH[:], lsb[0], LW), (T[pg][:, 0:LW], T.IH[:], T.COFF[:], LW), (T[pg][:, 0:i * JH], T.IH[:], u[0], i * JH)],
-               ["IH", "COFF", ltok, ltok + "e", u[1]], [L], pg)
-            tt((T[pg][:, 0:LW], L), (T[pg][:, 0:LW], L), u2, ALU.add, n=LW, f=1.0, x=[pg])
-            hp = NL // 2
-            for a in (0, hp):
-                e_ = min(a + hp, i)
-                u3 = (T.U2[:, h * LW + a * JH:h * LW + e_ * JH], "U3%d%d" % (h, a))
-                add("v", lambda a=a, e_=e_, u3=u3: V.tensor_tensor(u3[0], by[0].indirect(T.BO[:, 0:2 * (e_ - a)]),
-                                                                  T[mo[1][:2]][:, h * LW + a * JH:h * LW + e_ * JH], ALU.mult),
-                    0.06 + 1.56 * (e_ - a) * JH * CY, [by[1], "BO", mo[1], L], [u3[1]])
-                add("v", lambda a=a, e_=e_, u3=u3: V.tensor_tensor(T.OL[:, a:e_, h * JH:(h + 1) * JH], T[pg][:, a * JH:e_ * JH], u3[0], ALU.add),
-                    (e_ - a) * JH * CY, [L, u3[1]], ["OL%d%d" % (h, a)], [pg])
-            add("v", lambda: V.tensor_copy(T.OL[:, i, h * JH:(h + 1) * JH], T[pg][:, i * JH:LW]), 64 * CY, [L], ["OLz%d" % h], [pg])
-            return nw
-        if i > 0:
-            w_, vn = slot("lf"), slot("lf" if OPT["gu"] else "lh")
-            tt(w_, tn, be, ALU.subtract)
-            tt(vn, w_, by, ALU.add)
-            u = wide("U", h, i)
-            mo = (T[st["M"][1][:2]][:, h * LW:h * LW + i * JH], st["M"][1])
-            if OPT["gu"]:
+            if way("gu", i) == "g":
                 gtt(u, (vn[0], [vn[1]]), (T.BO[:, 0:2 * i], "BO"), mo, ALU.mult, i * JH)
             else:
                 spread(pp, 0, vn, i)
                 tt(u, (T[pp][:, 0:i * JH], pp + "w"), mo, ALU.mult, n=i * JH, f=1.0, x=[pp])
-            items = [(T[pg][:, 0:(i + 1) * JH], T.IH[:], lsb[0], (i + 1) * JH)]
-            mm(items, ["IH", ltok, ltok + "e"], [L], pg, keep=True)
+            return u
+
+        def log(vn):
+            u = put(vn)
+            lw = T[pg][:, 0:n_]
+            mm([(lw, T.IH[:], lsb[0], n_)], ["IH", ltok, ltok + "e"], [L], pg, keep=True)
             mm([(T[pg][:, 0:i * JH], T.IH[:], u[0], i * JH)], ["IH", u[1], L], [L], pg, cont=True)
-        if not early:
-            rr, t = take([])
-        if leave:
-            lx = (T.SL[:, so + 4 * JH:so + (5 + i) * JH], "SL%d_4" % k_)
-            tt(lx, (T[pg][:, 0:(i + 1) * JH], L), rr, ALU.subtract, n=(i + 1) * JH, f=1.0, x=[pg])
-            send(k_, 2, lx[0], T.LL[:, so + 4 * JH:so + (5 + i) * JH], [lx[1]], "LX%d" % k_, 128 * (1 + i) * JH * 2)
-        else:
-            if i == 0:
-                tt(lsb, lsb, rr, ALU.subtract)
+            rr = wide("RR", h, i + 1)
+            tt(rr, (lw, L), mk, ALU.mult, n=n_, f=1.0, x=[pg])
+            return u, rr
+
+        def take(u, rr):
+            if not fetch:
+                tsum = (T[pg][:, LW + JH:LW + 2 * JH], pg + "t")
+                mm([(tsum[0], T.I5[:], has[0], JH)] +
+                   [(tsum[0], T.IH[:], T.RR[:, h * LW + s_ * JH:h * LW + (s_ + 1) * JH], JH) for s_ in range(i + 1)],
+                   ["IH", "I5", rr[1], has[1]], [tsum[1]], pg)
+                t = slot("lf")
+                tt(t, tsum, x, ALU.max, f=1.0, x=[pg])
+                nw["t"] = t
+            lw = T[pg][:, 0:n_]
+            lx = (T.SL[:, k_ * LW:k_ * LW + n_], "SL%d" % k_) if leave else lsb
+            if way("lu", i) == "v":
+                tt(lx, (lw, L), rr, ALU.subtract, n=n_, f=1.0, x=[pg])
             else:
-                tt(lsb, (T[pg][:, 0:(i + 1) * JH], L), rr, ALU.subtract, n=(i + 1) * JH, f=1.0, x=[pg])
-            nw["tn"] = slot("lf")
-            act(nw["tn"], t, ACT.Identity, bias=-OFF)
-            nw["e"] = slot("lf")
-            tt(nw["e"], t, mn, ALU.subtract)
+                mm([(lw, T.IH[:], lsb[0], n_), (T[pg][:, 0:i * JH], T.IH[:], u[0], i * JH), (lw, T.NH[:], rr[0], n_)],
+                   ["IH", "NH", ltok, ltok + "e", u[1], rr[1]], [L], pg)
+                act(lx, (lw, L), ACT.Copy, n=n_, x=[pg])
+            if leave:
+                if not fetch:
+                    act(spart(3), t, ACT.Identity, bias=-TOP)
+                    wall(t, 0.0)
+                send(k_, 2, lx[0], T.LL[:, k_ * LW:k_ * LW + n_], [lx[1]], "LX%d" % k_, 128 * n_ * 2)
+
+        def wall(t, up):
+            ti, j_, nz = slot("li"), slot("li"), slot("lf")
+            ts(ti, t, up, ALU.add, float(K), ALU.mult)
+            ts(j_, ti, K, ALU.bitwise_and)
+            act(nz, c1, ACT.Relu, bias=2.0 * K, scale=-2.0 * K)
+            tt(spart(0), j_, nz, ALU.max)
+            o = 4 * k_ * JH
+            send(k_, 3, T.SJ[:, o:o + 4 * JH], T.LJ[:, o:o + 4 * JH], [spart(j)[1] for j in range(4)], "LJ%d" % k_, 128 * 4 * JH * 2)
+
+        if fetch:
+            mm([(tm[0], T.I8[:], b[0], JH)], ["I8", b[1], tm[1]], [tm[1]], pb, cont=True)
+            okb, xc, t2, t3 = slot("lf"), slot("lf"), slot("lf"), slot("lf")
+            act(okb, nok, ACT.Relu, bias=BIG, scale=-1.0)
+            act(xc, x, ACT.Identity, bias=-TOP)
+            tt(t2, tb, okb, ALU.subtract)
+            tt(t3, t2, xc, ALU.max)
+            tt(spart(3), tm, t3, ALU.max, f=1.0, x=[pb])
+            wall(spart(3), TOP)
+        if par:
+            mm([(pr[0], T.I8[:], b[0], JH)], ["I8", b[1], pr[1]], [pr[1]], pg, cont=True)
+            vn = slot("lf" if way("gu", i) == "g" else "lh")
+            tt(vn, pr, tb, ALU.max, f=1.0, x=[pg])
+            if last:
+                mc = slot("lf")
+                ts(mc, x, -TOP, ALU.add, -OFF - 1.0, ALU.max)
+                u = put(vn)
+                u2 = wide("U2", h, NL)
+                gtt(u2, (mc[0], [mc[1]]), whole("BO"), mk, ALU.mult, LW)
+                lw = T[pg][:, 0:LW]
+                mm([(lw, T.IH[:], lsb[0], LW), (lw, T.IH[:], T.COFF[:], LW), (lw, T.IK[:], mk[0], LW)],
+                   ["IH", "IK", "COFF", ltok, ltok + "e", mk[1]], [L], pg, keep=True)
+                mm([(T[pg][:, 0:i * JH], T.IH[:], u[0], i * JH), (lw, T.IH[:], u2[0], LW)], ["IH", u[1], u2[1], L], [L], pg, cont=True)
+                act((T.OL[:, :, h * JH:(h + 1) * JH], "OL%d" % h), (lw, L), ACT.Copy, n=LW, x=[pg])
+            else:
+                u, rr = log(vn)
+        rs = (T[ps][:, JH:2 * JH], ps + "r")
+        mm(([(rs[0], T.IP[:], b[0], JH)] if i > 0 else []) +
+           [(rs[0], T.ER[:, 15 - r:143 - r], T.Y[:, h * KH + r:(h + 1) * KH:16], JH) for r in range(16)],
+           ["ER", "IP"] + ys + ([b[1]] if i > 0 else []), [rs[1]], ps)
+        ri, r_ = slot("li"), slot("li")
+        ts(ri, rs, 16777216.0 - BIG + CP - 2560.0, ALU.add, x=[ps])
+        ts(r_, ri, 8191, ALU.bitwise_and)
+        if i == 0:
+            mn = r_
+        else:
+            mn = slot("lf")
+            tt(mn, r_, mb, ALU.max)
+        nw["m"] = mn
+        if last:
+            ts((T.OM[:, h * JH:(h + 1) * JH], "OM%d" % h), mn, -1.0 * CP, ALU.add)
+            return nw
+        nw["m16"] = slot("lu")
+        ts(nw["m16"], mn, -1.0 * CP, ALU.add)
+        if leave:
+            send(k_, 1, nw["m16"][0], T.LM[:, k_ * JH:(k_ + 1) * JH], [nw["m16"][1]], "LM%d" % k_, 128 * JH * 2)
+        if i > 0 and not par:
+            vn, vc = slot("lf"), slot("lf" if way("gu", i) == "g" else "lh")
+            tt(vn, r_, tb, ALU.min)
+            if way("cen", i) == "v":
+                ts(vc, vn, -OFF, ALU.add)
+            else:
+                act(vc, vn, ACT.Identity, bias=-OFF)
+            u, rr = log(vc)
+        if i > 0:
+            take(u, rr)
         return nw
 
     sts = []
@@ -630,8 +671,8 @@ def build(g, T, topo, core, rank):
             sts[h] = step(i, h, sts[h])
     dma("s", T.ym[:], T.OM[:], ["OM0", "OM1"], [], 128 * 256)
     dma("a", T.yc[:], T.OC[:], ["OC0", "OC1"], [], 128 * 256)
-    dma("s", T.yl[:, 0:384], T.OL[:, 0:6], ["OL00", "OL10"], [], 128 * 384 * 4)
-    dma("a", T.yl[:, 384:768], T.OL[:, 6:12], ["OL06", "OL16", "OLz0", "OLz1"], [], 128 * 384 * 4)
+    dma("s", T.yl[:, 0:384], T.OL[:, 0:6], ["OL0", "OL1"], [], 128 * 384 * 4)
+    dma("a", T.yl[:, 384:768], T.OL[:, 6:12], ["OL0", "OL1"], [], 128 * 384 * 4)
     return ops, nsend * len([op for op in ops if op["kind"] == "s"])
 
 
@@ -727,11 +768,133 @@ def order(ops):
     return seq, end
 
 
+def clear(a, b, s, d):
+    lo, hi = 0, len(b)
+    while lo < hi:
+        mid = (lo + hi) // 2
+        if b[mid] <= s:
+            lo = mid + 1
+        else:
+            hi = mid
+    while lo < len(a) and a[lo] < s + d - 1e-9:
+        s = max(s, b[lo])
+        lo += 1
+    return s, lo
+
+
+def justify(ops, paces):
+    n = len(ops)
+    gr, pc, hop, own, net = OPT["pace"]
+    c = costs(ops, gr, pc)
+    res = ["D" if o["kind"] == "d" else o["eng"] for o in ops]
+    dur = [c[i] + o.get("bytes", 0) / 250e3 for i, o in enumerate(ops)]
+    pre = [[(j, ops[j]["lat"] * (net if ops[j]["kind"] == "r" else 1.0) + ((own if ops[j]["eng"] == o["eng"] else hop) if need else 0.0))
+            for j, need in o["pre"].items()] for o in ops]
+    suc = [[] for _ in range(n)]
+    for i in range(n):
+        for j, l in pre[i]:
+            suc[j].append((i, l))
+    tail = [o["lat"] if o["kind"] == "d" else 0.0 for o in ops]
+
+    def sweep(seq, edges, first):
+        st, fin, span = [0.0] * n, [0.0] * n, {}
+        for i in seq:
+            s = first[i]
+            for j, l in edges[i]:
+                if fin[j] + l > s:
+                    s = fin[j] + l
+            if dur[i] > 0:
+                a, b = span.setdefault(res[i], ([], []))
+                s, k = clear(a, b, s, dur[i])
+                a.insert(k, s)
+                b.insert(k, s + dur[i])
+            st[i], fin[i] = s, s + dur[i]
+        return st, fin
+
+    def topo_sort(key, edges, back):
+        k2 = list(key)
+        for i in (range(n - 1, -1, -1) if back else range(n)):
+            for j, _l in edges[i]:
+                if k2[j] >= k2[i]:
+                    k2[i] = k2[j] + 1e-7
+        return sorted(range(n), key=lambda i: k2[i])
+    far = [0.0] * n
+    for i in range(n - 1, -1, -1):
+        far[i] = dur[i] + max([tail[i]] + [l + far[s] for s, l in suc[i]])
+    key = [-far[i] - (OPT["lead"] if ops[i]["h"] == 0 else 0.0) for i in range(n)]
+    zero = [0.0] * n
+    loads = [i for i, o in enumerate(ops) if o["kind"] == "d" and not o["pre"]]
+    lands = [i for i, o in enumerate(ops) if o["kind"] == "r"]
+    x = OPT["seed"] * 7919 + 1
+    best, bseq, bkey = 1e9, None, key
+    run = runner(ops, paces)
+    for it in range(OPT["sweeps"]):
+        if it % OPT["again"] == 0 and it:
+            key = []
+            for i in range(n):
+                x = (x * 1103515245 + 12345) % 2147483648
+                key.append(bkey[i] + OPT["jit"] * x / 2147483648.0)
+        for i in loads:
+            key[i] = i - 1e6
+        st, fin = sweep(topo_sort(key, pre, False), pre, zero)
+        for i in loads:
+            st[i] = i - 1e6
+        for i in lands:
+            st[i] = 0.0
+        seq = topo_sort(st, pre, False)
+        t = run(seq)
+        if t < best:
+            best, bseq, bkey = t, seq, st
+        _s, back = sweep(topo_sort([-f for f in fin], suc, True), suc, tail)
+        key = [-f for f in back]
+    return bseq
+
+
+def runner(ops, paces):
+    n = len(ops)
+    tabs = []
+    for gr, pc, hop, own, net in paces:
+        pr = [[(j, ops[j]["lat"] * (net if ops[j]["kind"] == "r" else 1.0) +
+                ((own if ops[j]["eng"] == o["eng"] else hop) if need else 0.0)) for j, need in o["pre"].items()] for o in ops]
+        tabs.append((costs(ops, gr, pc), pr))
+    eng = [o["eng"] for o in ops]
+    dm = [o.get("bytes", 0) / 250e3 for o in ops]
+    lat = [o["lat"] for o in ops]
+
+    def run(sq):
+        total = 0.0
+        for c, pr in tabs:
+            fin = [0.0] * n
+            free = {}
+            dfree = end = 0.0
+            for i in sq:
+                s = free.get(eng[i], 0.0)
+                for j, l in pr[i]:
+                    if fin[j] + l > s:
+                        s = fin[j] + l
+                f = s + c[i]
+                free[eng[i]] = f
+                if dm[i]:
+                    dfree = max(dfree, f) + dm[i]
+                    f = dfree
+                fin[i] = f
+                if f + lat[i] > end:
+                    end = f + lat[i]
+            total += end
+        return total
+    return run
+
+
+def costs(ops, gr, pc):
+    return [(0.06 + o["gn"] * gr * CY) * pc if o.get("gn") else o["cost"] * pc if o["eng"] in "vap" and o["kind"] == "c" else o["cost"]
+            for o in ops]
+
+
 def polish(ops, seq, rounds, paces):
     n = len(ops)
     tabs = []
     for gr, pc, hop, own, net in paces:
-        c = [o["cost"] * pc if o["eng"] == "p" else 0.07 + o["gn"] * gr * CY if o.get("gn") else o["cost"] for o in ops]
+        c = costs(ops, gr, pc)
         pr = [[(j, ops[j]["lat"] * (net if ops[j]["kind"] == "r" else 1.0) +
                 ((own if ops[j]["eng"] == o["eng"] else hop) if need else 0.0)) for j, need in o["pre"].items()] for o in ops]
         tabs.append((c, pr))
@@ -804,7 +967,7 @@ def polish(ops, seq, rounds, paces):
     return seq
 
 
-PACES = [(1.56, 1.0, 0.27, 0.09, 1.0), (1.3, 1.1, 0.33, 0.12, 1.3), (1.9, 0.9, 0.18, 0.07, 1.0)]
+PACES = [(1.56, 0.85, 0.4, 0.12, 1.0), (1.3, 1.0, 0.33, 0.12, 1.3), (1.9, 1.1, 0.25, 0.09, 1.0)]
 ORDER = {}
 
 
@@ -815,7 +978,7 @@ def rank_program(g, core, T, topo):
     ops, sent = build(g, T, topo, core, rank)
     depend(ops)
     if len(ops) not in ORDER:
-        ORDER[len(ops)] = polish(ops, order(ops)[0], OPT["rounds"], PACES)
+        ORDER[len(ops)] = polish(ops, justify(ops, PACES), OPT["rounds"], PACES)
     seq = ORDER[len(ops)]
     queue = {"v": g.vector, "a": g.scalar, "p": g.tensor, "g": g, "s": g.sync}
     count = {}

from concourse.mybir import AluOpType, ActivationFunctionType

C = 3072
CP = C + 16
K = 1024
H = 2
KH = K // H
JH = KH // 16
NV, NS = 3, 4
NL = NV * NS
LW = NL * JH
OFF = 2032.0
TOP = OFF + CP
BIG = 8192.0
NF32, NI32, NU16, NF16 = 400, 72, 100, 200

SCRATCH = {
    "G": ("sbuf", [128, CP + C], "bfloat16"), "R": ("sbuf", [128, C], "bfloat16"), "LN": ("sbuf", [128, C], "float32"),
    "NX": ("sbuf", [128, 2 * C], "int32"), "F": ("sbuf", [128, C], "bfloat16"),
    "W": ("sbuf", [128, 2 * K + 16], "bfloat16"), "B0": ("sbuf", [128, K], "bfloat16"), "M0": ("sbuf", [128, 64], "int32"),
    "P1": ("sbuf", [128, 2, 6, 16], "int32"), "P2": ("sbuf", [128, 6, 32], "float32"), "P3": ("sbuf", [128, 6, 32], "float32"),
    "PL": ("sbuf", [128, 192], "uint16"),
    "ci": ("sbuf", [128, 16], "int32"), "cf": ("sbuf", [128, 16], "float32"), "cb": ("sbuf", [128, 16], "bfloat16"),
    "ix": ("sbuf", [128, 144], "float32"), "ig": ("sbuf", [128, 128], "float32"),
    "t0": ("sbuf", [128, 128], "float32"), "t1": ("sbuf", [128, 128], "float32"), "t2": ("sbuf", [128, 128], "float32"),
    "t3": ("sbuf", [128, 128], "float32"), "t4": ("sbuf", [128, 128], "float32"), "t5": ("sbuf", [128, 128], "float32"),
    "EZ": ("sbuf", [128, 144], "bfloat16"), "ER": ("sbuf", [128, 144], "float16"), "EP": ("sbuf", [128, 144], "float16"),
    "IB": ("sbuf", [128, 128], "bfloat16"), "IH": ("sbuf", [128, 128], "float16"), "NH": ("sbuf", [128, 128], "float16"),
    "I5": ("sbuf", [128, 128], "float16"), "IP": ("sbuf", [128, 128], "float16"), "I8": ("sbuf", [128, 128], "float16"),
    "IK": ("sbuf", [128, 128], "float16"),
    "M1": ("sbuf", [128, 128], "bfloat16"), "M2": ("sbuf", [128, 128], "bfloat16"), "M3": ("sbuf", [128, 128], "bfloat16"),
    "L0": ("sbuf", [128, H * NS * JH], "float16"),
    "PLC": ("sbuf", [128, LW], "float16"), "COFF": ("sbuf", [128, LW], "float16"), "CEMP": ("sbuf", [128, LW], "float16"),
    "KI": ("sbuf", [128, 64], "float32"), "KJ": ("sbuf", [128, 64], "float32"),
    "BI": ("sbuf", [128, 24], "float32"), "BO": ("sbuf", [128, 24], "uint16"),
    "oh": ("sbuf", [128, JH], "float16"), "mh": ("sbuf", [128, JH], "float16"),
    "lf": ("sbuf", [128, NF32 * JH], "float32"), "li": ("sbuf", [128, NI32 * JH], "int32"),
    "lu": ("sbuf", [128, NU16 * JH], "uint16"), "lh": ("sbuf", [128, NF16 * JH], "float16"),
    "Q": ("sbuf", [128, K], "float16"), "S1": ("sbuf", [128, K], "bfloat16"), "S2": ("sbuf", [128, K], "bfloat16"),
    "XG": ("sbuf", [128, K], "float32"), "PN": ("sbuf", [128, K], "float16"),
    "GG": ("sbuf", [128, K], "float16"), "Y": ("sbuf", [128, K], "float16"),
    "BA": ("sbuf", [128, K], "float16"), "BB": ("sbuf", [128, K], "float16"), "BC": ("sbuf", [128, K], "float16"),
    "XS": ("sbuf", [128, K], "float16"),
    "MA": ("sbuf", [128, H * LW], "float16"), "MB": ("sbuf", [128, H * LW], "float16"), "MD": ("sbuf", [128, H * LW], "float16"),
    "U": ("sbuf", [128, H * LW], "float16"), "RR": ("sbuf", [128, H * LW], "float16"), "U2": ("sbuf", [128, H * LW], "float16"),
    "SB": ("sbuf", [128, 2 * K], "float16"), "LB": ("sbuf", [128, 2 * K], "float16"),
    "SG": ("sbuf", [128, 2 * K], "float16"), "LG": ("sbuf", [128, 2 * K], "float16"),
    "SJ": ("sbuf", [128, 2 * H * 4 * JH], "float16"), "LJ": ("sbuf", [128, 2 * H * 4 * JH], "float16"),
    "LM": ("sbuf", [128, 2 * H * JH], "uint16"),
    "SL": ("sbuf", [128, 2 * H * LW], "float16"), "LL": ("sbuf", [128, 2 * H * LW], "float16"),
    "OB": ("sbuf", [128, K], "float32"), "OL": ("sbuf", [128, NL, 64], "float32"),
    "OM": ("sbuf", [128, 64], "float32"), "OC": ("sbuf", [128, 64], "float32"),
}
for _h in range(H):
    for _n in ("PP", "PB", "PG", "PS"):
        SCRATCH["%s%d" % (_n, _h)] = ("psum", [128, 512], "float32")

NDMA = 44
SEMAPHORES = ["cv", "ca", "cp", "cg", "sent"] + ["d%d" % i for i in range(NDMA)] + ["r%d" % i for i in range(10 * H)]

ALU = AluOpType
ACT = ActivationFunctionType
CY = 0.001
PCY = 0.0005
HOP = 0.3
OWN = 0.08
OPT = {"xm": "p", "bv": "a", "s2": "a", "mk": "v", "lu": "v", "cen": "v", "gu": "g", "fb": "v", "late": 6, "np": 2, "pf": True, "link": 40e3,
       "split": 2, "lead": 3.0, "lead2": 0.0, "turn": 11, "win": 0.3, "lam": 30.0, "hold": 13.0, "seed": 1790, "jit": 1.0,
       "rounds": 20000, "pace": (1.56, 0.95, 0.35, 0.12, 1.1), "sweeps": 600, "again": 6}


def build(g, T, topo, core, rank):
    ops = []
    cur = [None, 0]
    cores = list(T.cores)
    nxt = cores[(rank + 1) % len(cores)]
    rid, pid, _se = topo.addr(nxt)
    emask = topo.mask(core, nxt)
    neng = len(topo.engines(cores[(rank - 1) % len(cores)], core))
    nsend = len(topo.engines(core, nxt))
    V, A, PE = g.vector, g.scalar, g.tensor

    def way(name, i):
        return OPT[name][i % len(OPT[name])]

    def add(eng, fn, cost, r=(), w=(), x=(), kind="c", lat=0.0, sem=None, cnt=0):
        ops.append({"eng": eng, "fn": fn, "cost": cost, "r": list(r), "w": list(w), "x": list(x), "kind": kind,
                    "lat": lat, "sem": sem, "cnt": cnt, "h": cur[0], "i": cur[1]})

    used = {"lf": 0, "li": 0, "lu": 0, "lh": 0}

    def slot(pool):
        i = used[pool]
        used[pool] += 1
        return (T[pool][:, i * JH:(i + 1) * JH], "%s%d" % (pool, i), pool, i * JH)

    def pair(a):
        return T[a[2]][:, a[3]:a[3] + 2 * JH]

    def tt(out, a, b, op, n=JH, f=2.0, x=()):
        add("v", lambda: V.tensor_tensor(out[0], a[0], b[0], op), max(64, n * f) * CY, [a[1], b[1]], [out[1]], x)

    def ts(out, a, s1, o0, s2=None, o1=None, n=JH, f=1.0, x=(), r=()):
        if o1 is None:
            fn = lambda: V.tensor_scalar(out[0], a[0], s1, None, o0)
        else:
            fn = lambda: V.tensor_scalar(out[0], a[0], s1, s2, o0, o1)
        add("v", fn, max(64, n * f) * CY, [a[1]] + list(r), [out[1]], x)

    def cp(out, a, n=JH):
        add("v", lambda: V.tensor_copy(out[0], a[0]), max(64, n) * CY, [a[1]], [out[1]])

    def gtt(out, win, off, b, op, n):
        add("v", lambda: V.tensor_tensor(out[0], win[0].indirect(off[0]), b[0], op), 0.06 + 1.56 * n * CY,
            list(win[1]) + [off[1], b[1]], [out[1]])
        ops[-1]["gn"] = n

    def act(out, a, func, bias=0.0, scale=1.0, n=JH, x=(), r=(), more=0.0):
        add("a", lambda: A.activation(out[0], a[0], func, bias=bias, scale=scale), max(64, n) * CY + 0.02 + more,
            [a[1]] + list(r), [out[1]], x)

    def gact(out, win, off, func, bias, scale, n):
        add("a", lambda: A.activation(out[0], win[0].indirect(off[0]), func, bias=bias, scale=scale), 0.08 + 1.56 * n * CY,
            list(win[1]) + [off[1]], [out[1]])
        ops[-1]["gn"] = n

    def mm(items, r, w, bank, alone=False, cont=False, keep=False):
        def fn():
            last = None
            for i, (o, l, rh, _n) in enumerate(items):
                if alone:
                    last = PE.matmul(o, l, rh, True, True)
                else:
                    last = PE.matmul(o, l, rh, (i == 0) and not cont, i == len(items) - 1 and not keep)
            return last
        add("p", fn, sum(max(64, it[3]) for it in items) * PCY + 0.05, r, w, [bank])

    ndma = [0]

    def dma(q, out, in_, r, w, nbytes):
        s = "d%d" % ndma[0]
        ndma[0] += 1
        e = {"s": g.sync, "a": g.scalar}[q]
        add(q, lambda: e.dma_start(out, in_), 0.06, r, w, kind="d", lat=2.0, sem=s, cnt=16)
        ops[-1]["bytes"] = nbytes

    def gop(fn, n, w):
        add("g", fn, 0.13 + 2 * n * CY, [], w)

    NFP = 2
    fw = C // NFP
    dma("a", T.M0[:], T.m0[:], [], ["M0"], 128 * 256)
    for gr in range(8):
        q, hh = gr // 2, gr % 2
        if gr == 1:
            dma("s", T.G[:, 16:16 + fw], T.fm[:, 0:fw], [], ["F0"], 128 * fw * 2)
        dma("as"[hh], T.P1[32 * q:32 * q + 32, hh], T.nx[16 * gr, :], [], ["P1_%d" % gr], C * 4)
    dma("s", T.G[:, 16 + fw:CP], T.fm[:, fw:C], [], ["F1"], 128 * fw * 2)
    for h in range(H):
        dma("a", T.B0[:, h * KH:(h + 1) * KH], T.b0[:, h * KH:(h + 1) * KH], [], ["B0%d" % h], 128 * KH * 2)
    dma("s", T.NX[:, 0:C // 2], T.nx[:, 0:C // 2], [], ["NX0"], 128 * C * 2)
    dma("a", T.NX[:, C // 2:C], T.nx[:, C // 2:C], [], ["NX1"], 128 * C * 2)
    FT = ["F%d" % i for i in range(NFP)]

    gop(lambda: g.iota(T.ci[:, 0:1], [[0, 1]], 0, 1), 1, ["ci0"])
    gop(lambda: g.iota(T.ix[:], [[1, 144]], 0, 0, allow_small_or_imprecise_dtypes=True), 144, ["ix"])
    gop(lambda: g.iota(T.ig[:], [[16, 8], [0, 16]], 0, 0, allow_small_or_imprecise_dtypes=True), 128, ["ig"])
    gop(lambda: g.iota(T.LN[:, 0:LW], [[1, NL], [0, JH]], 1, 0, allow_small_or_imprecise_dtypes=True), LW, ["LN0"])
    gop(lambda: g.iota(T.KI[:], [[16, 64]], 0, 0, allow_small_or_imprecise_dtypes=True), 64, ["KI"])
    gop(lambda: g.iota(T.BI[:], [[0, 12], [16, 2]], 0, 0, allow_small_or_imprecise_dtypes=True), 24, ["BI"])
    if "s" in OPT["xm"]:
        gop(lambda: g.iota(T.NX[:, C:2 * C], [[0, C]], 0, 0), C, ["NXz"])
    for gr in range(8 if "s" in OPT["xm"] else 0):
        dma("s", T.NX[16 * gr:16 * gr + 1, C:2 * C], T.nx[16 * gr:16 * gr + 1, :], ["NXz"], ["NXp%d" % gr], C * 4)
    dma("s", T.W[:, 0:2 * K], T.wl[:], ["NX0", "NX1"], ["W"], 128 * 2 * K * 2)

    def ci(i):
        return (T.ci[:, i:i + 1], "ci%d" % i)

    def cf(i):
        return (T.cf[:, i:i + 1], "cf%d" % i)

    def whole(name):
        return (T[name][:], name)

    ts(ci(1), ci(0), 15, ALU.bitwise_and)
    ts(ci(2), ci(0), 112, ALU.bitwise_and)
    cp(cf(0), ci(0))
    cp(cf(1), ci(1))
    cp(cf(2), ci(2))
    ts(cf(3), cf(2), 15.0, ALU.add)
    ts(cf(4), cf(1), 0.0, ALU.is_gt, 3.0 * BIG, ALU.mult)
    ts(cf(5), cf(4), -BIG, ALU.add)
    ts(cf(6), cf(1), 15.0, ALU.is_equal)
    ts(cf(7), cf(6), -1000.0, ALU.mult)
    ts(cf(8), cf(6), 32768.0, ALU.mult, 2.0, ALU.add)
    thr = (T.cb[:, 0:1], "cb0")
    cp(thr, cf(8))
    nthr = (T.cb[:, 1:2], "cb1")
    ts(nthr, cf(8), -1.0, ALU.mult)
    ts(cf(9), cf(1), 0.0, ALU.is_equal)
    ixs = (T.ix[:, 0:128], "ix")
    ts(whole("EZ"), whole("ix"), cf(3)[0], ALU.is_equal, cf(5)[0], ALU.mult, n=144, r=["cf3", "cf5"])
    ts(whole("t0"), whole("ig"), cf(2)[0], ALU.is_equal, n=128, r=["cf2"])
    ts(whole("t1"), ixs, cf(0)[0], ALU.is_equal, n=128, r=["cf0"])
    ts(whole("t2"), ixs, cf(0)[0], ALU.is_gt, n=128, r=["cf0"])
    ts(whole("t3"), whole("t1"), 32.0, ALU.mult, -2.0, ALU.add, n=128)
    ts(whole("t4"), whole("t2"), -28.0, ALU.mult, n=128)
    tt(whole("t3"), whole("t3"), whole("t4"), ALU.add, n=128)
    tt(whole("M1"), whole("t3"), whole("t0"), ALU.mult, n=128)
    tt(whole("t4"), whole("t1"), whole("t2"), ALU.subtract, n=128)
    ts(whole("t2"), whole("t4"), 2.0, ALU.mult, cf(6)[0], ALU.subtract, n=128, r=["cf6"])
    tt(whole("M2"), whole("t2"), whole("t0"), ALU.mult, n=128)
    if "a" in OPT["s2"]:
        tt(whole("t5"), whole("ig"), ixs, ALU.subtract, n=128)
        ts(whole("t5"), whole("t5"), cf(6)[0], ALU.mult, n=128, r=["cf6"])
        tt(whole("t5"), whole("t5"), whole("t4"), ALU.add, n=128)
        tt(whole("M3"), whole("t5"), whole("t0"), ALU.mult, n=128)
    ts(whole("ER"), whole("ix"), cf(3)[0], ALU.is_equal, 4096.0, ALU.mult, n=144, r=["cf3"])
    ts(whole("EP"), whole("ix"), cf(3)[0], ALU.is_equal, cf(9)[0], ALU.mult, n=144, r=["cf3", "cf9"])
    cp(whole("IB"), whole("t1"), 128)
    cp(whole("IH"), whole("t1"), 128)
    for name, val in (("NH", -1.0), ("I5", TOP), ("IP", -1.0 * CP), ("I8", BIG), ("IK", OFF + 1.0)):
        ts(whole(name), whole("IH"), val, ALU.mult, n=128, f=0.5)
    cp(whole("PLC"), (T.LN[:, 0:LW], "LN0"), LW)
    ts(whole("COFF"), whole("PLC"), 0.0, ALU.mult, OFF, ALU.add, n=LW, f=0.5)
    ts(whole("CEMP"), whole("PLC"), 0.0, ALU.mult, -OFF - 1.0, ALU.add, n=LW, f=0.5)
    ts(whole("KJ"), whole("KI"), cf(1)[0], ALU.add, n=64, r=["cf1"])
    ts(whole("BO"), whole("BI"), cf(1)[0], ALU.add, n=24, r=["cf1"])
    ts(whole("oh"), (T.PLC[:, 0:JH], "PLC"), 1.0, ALU.mult)
    ts(whole("mh"), (T.PLC[:, 0:JH], "PLC"), -1.0, ALU.mult)
    add("v", lambda: V.memset(T.G[:, 0:16], 0.0), 64 * CY, [], ["Gz"])
    add("v", lambda: V.memset(T.W[:, 2 * K:2 * K + 16], 0.0), 64 * CY, [], ["Wz"])
    for v in range(2):
        for h in range(H):
            o = (v * H + h) * LW
            wv = NS * (v + 1)
            cp((T.LL[:, o + wv * JH:o + LW], "LX%de" % (v * H + h)), (T.CEMP[:, 0:(NL - wv) * JH], "CEMP"), 128)

    NRP = 4
    rw = C // NRP
    for i in range(NRP):
        act((T.LN[:, i * rw:(i + 1) * rw], "LN%d" % i), (T.G[:, 16 + i * rw:16 + (i + 1) * rw], "F%d" % (i * NFP // NRP)), ACT.Ln,
            bias=0.05, n=rw, more=1.3 if i == 0 else 0.0, r=["LN%d" % (i - 1)] if i else [])
    for i in range(NRP):
        act((T.R[:, i * rw:(i + 1) * rw], "R%d" % i), (T.LN[:, i * rw:(i + 1) * rw], "LN%d" % i), ACT.Exp, scale=-1.0, n=rw,
            more=1.5 if i == 0 else 0.0, r=["LN%d" % (NRP - 1)] + (["R%d" % (i - 1)] if i else []))
    for hh in range(2):
        add("v", lambda hh=hh: V.tensor_copy(T.P2[:, :, 16 * hh:16 * hh + 16], T.P1[:, hh]), 96 * CY,
            ["P1_%d" % (2 * q + hh) for q in range(4)], ["P2_%d" % hh])
    for b in range(6):
        add("v", lambda b=b: V.transpose(T.P3[:, b, :], T.P2[:, b, :]), 64 * CY, ["P2_0", "P2_1"], ["P3_%d" % b])
        cp((T.PL[:, b::6], "PL%d" % b), (T.P3[:, b, :], "P3_%d" % b))
    NDP = 6
    dw = C // NDP
    for i in range(NDP):
        add("g", lambda i=i: g.affine_select(T.F[:, i * dw:(i + 1) * dw], T.G[:, 16 + i * dw:16 + (i + 1) * dw], [[0, dw]], ALU.is_ge, 0.0, 0, 0),
            0.17 + 2 * dw * CY, ["F%d" % (i * NFP // NDP)], ["FC%d" % i])
        add("v", lambda i=i: V.tensor_tensor(T.G[:, CP + i * dw:CP + (i + 1) * dw],
                                             T.G[:, 16:CP].indirect(T.PL[:, i * dw // 16:(i + 1) * dw // 16]),
                                             T.F[:, i * dw:(i + 1) * dw], ALU.subtract),
            0.06 + 1.56 * dw * CY, FT + ["FC%d" % i] + ["PL%d" % b for b in range(6)], ["GD%d" % i])
        ops[-1]["gn"] = dw
    winF = (T.G[:, 16:CP], FT)
    winR = (T.R[:], ["R%d" % i for i in range(NRP)])
    winG0 = (T.G[:, 0:CP], FT + ["Gz"])
    winG = (T.G[:], FT + ["Gz"] + ["GD%d" % i for i in range(NDP)])
    winX = (T.NX[:, 0:C], ["NX0", "NX1"])
    winX2 = (T.NX[:], ["NX0", "NX1"] + ["NXp%d" % i for i in range(8)])
    winW = (T.W[:], ["W", "Wz"])

    def big(name, h, w=KH):
        return (T[name][:, h * KH:h * KH + w], "%s%d" % (name, h))

    def wide(name, h, blocks):
        return (T[name][:, h * LW:h * LW + blocks * JH], "%s%d" % (name, h))

    def spread(bank, col, src, blocks, less=False):
        items = [(T[bank][:, col + s * JH:col + (s + 1) * JH], T.IH[:], src[0], JH) for s in range(blocks)]
        if less:
            items = [(T[bank][:, col:col + blocks * JH], T.NH[:], T.PLC[:, 0:blocks * JH], blocks * JH)] + items
        mm(items, ["IH", "NH", "PLC", src[1]], [bank + "w"], bank, alone=not less)

    def mask(h, c1, blocks, name, how):
        ps = "PP%d" % h
        mk = wide(name, h, blocks)
        n = blocks * JH
        pw = (T[ps][:, 0:n], ps + "w")
        spread(ps, 0, c1, blocks, how != "v")
        if how == "v":
            tt(mk, pw, (T.PLC[:, 0:n], "PLC"), ALU.is_equal, n=n, f=1.0, x=[ps])
        else:
            md = wide("MD", h, blocks)
            act(md, pw, ACT.Abs, n=n, x=[ps])
            if how == "a":
                act(mk, md, ACT.Relu, bias=1.0, scale=-1.0, n=n)
            else:
                ts(mk, md, 0.5, ALU.is_lt, n=n, f=0.5)
        return mk

    def first(h):
        st = {}
        m0 = (T.M0[:, h * JH:(h + 1) * JH], "M0")
        st["m16"] = slot("lu")
        cp(st["m16"], m0)
        st["m"] = slot("lf")
        ts(st["m"], m0, float(CP), ALU.add)
        st["B"] = big("B0", h)
        st["L"] = ("L0", h * NS * JH, "L0%d" % h)
        cp((T.L0[:, (h * NS + 1) * JH:(h + 1) * NS * JH], "L0%de" % h), (T.CEMP[:, 0:(NS - 1) * JH], "CEMP"), 64)
        return st

    def arrive(v, h, old):
        st = {"low": True}
        k = (v - 1) * H + h
        st["m16"] = (T.LM[:, k * JH:(k + 1) * JH], "LM%d" % k, "LM", k * JH)
        st["m"] = slot("lf")
        ts(st["m"], st["m16"], float(CP), ALU.add)

        def part(i):
            o = (4 * k + i) * JH
            return (T.LJ[:, o:o + JH], "LJ%d" % k, "LJ", o)
        st["c1"], st["n1"], st["t"] = part(1), part(2), part(3)
        o3 = part(0)
        st["wall"] = o3
        if v > 1:
            d = slot("lf")
            tt(d, o3, old["wall"], ALU.is_equal)
            ez = slot("lf")
            act(ez, d, ACT.Copy, scale=2.0 * K)
            o4 = slot("lf")
            tt(o4, o3, ez, ALU.max)
            o3 = o4
        o2, o16 = slot("lf"), slot("lu")
        tt(o2, o3, (T.KJ[:, h * JH:(h + 1) * JH], "KJ"), ALU.add)
        ts(o16, o2, 2.0 * K, ALU.min)
        bs = big("BB", h)
        lb = (T.LB[:, k * KH:(k + 1) * KH], "LB%d" % k)
        lg = (T.LG[:, k * KH:(k + 1) * KH], "LG%d" % k)
        st["raw"] = big("XS", h)
        if OPT["late"] >= 5:
            npc = OPT["np"]
            pw = KH // npc
            if OPT["late"] == 6:
                gact(bs, winW, o16, ACT.Copy, 0.0, 1.0, KH)
            for a in range(npc):
                ra = (T.XS[:, h * KH + a * pw:h * KH + (a + 1) * pw], "XS%d_%d" % (h, a))
                la = (T.LB[:, k * KH + a * pw:k * KH + (a + 1) * pw], "LB%d_%d" % (k, a))
                if OPT["late"] == 6:
                    tt(ra, (T.BB[:, h * KH + a * pw:h * KH + (a + 1) * pw], bs[1]), la, ALU.subtract, n=pw, f=1.0)
                else:
                    gtt(ra, winW, (T.lu[:, o16[3] + a * pw // 16:o16[3] + (a + 1) * pw // 16], o16[1]), la, ALU.subtract, pw)
            st["cut"] = npc
            st["raw"] = (st["raw"][0], "XS%d_0" % h)
        elif OPT["late"] == 3:
            tt(bs, lb, lg, ALU.add, n=KH, f=1.0)
            gtt(st["raw"], winW, o16, bs, ALU.subtract, KH)
        else:
            gtt(bs, winW, o16, lb, ALU.subtract, KH)
            tt(st["raw"], bs, lg, ALU.subtract, n=KH, f=1.0)
        st["B"] = big("BA", h)
        ts(st["B"], st["raw"], -1.0, ALU.mult, -255.5, ALU.max, n=KH, f=0.5, r=["XS%d_%d" % (h, a) for a in range(st.get("cut", 0))])
        st["L"] = ("LL", k * LW, "LX%d" % k)
        st["M"] = mask(h, st["c1"], NS * v, "MA", way("mk", NS * v))
        return st

    def send(k, part, src, dst, r, w, nbytes):
        s = "r%d" % (5 * k + part)
        add("g", lambda: g.remote_dma(dst, src, T.sem[s], T.sem.sent, pid, rid, emask), 0.6, r, ["fly" + w], kind="s")
        add("x", None, nbytes / OPT["link"], ["fly" + w], [w], kind="r", lat=2.5, sem=s, cnt=neng)

    def step(i, h, st):
        v_, s = divmod(i, NS)
        leave = s == NS - 1 and i < NL - 1
        ahead = s == NS - 2 and v_ < NV - 1 and OPT["late"] < 5
        fetch = leave and OPT["pf"]
        last = i == NL - 1
        par = i > 0 and way("xm", i) == "p"
        low = TOP if st.get("low") else 0.0
        pp, pb, pg, ps = "PP%d" % h, "PB%d" % h, "PG%d" % h, "PS%d" % h
        k_ = v_ * H + h

        def spart(j):
            o = (4 * k_ + j) * JH
            return (T.SJ[:, o:o + JH], "SJ%d_%d" % (k_, j), "SJ", o)
        nw = {"wall": st.get("wall"), "L": st["L"]}
        B, m, m16 = st["B"], st["m"], st["m16"]
        s1, s2, qq = big("S1", h), big("S2", h), big("Q", h)
        pbw = (T[pb][:], pb + "w")
        m2 = "M2"
        if i == 0:
            gtt(s1, winF, m16, B, ALU.is_gt, KH)
            ts(qq, B, 0.5, ALU.mult, cf(7)[0], ALU.add, n=KH, f=0.5, r=["cf7"])
            gtt(s2, winF, m16, qq, ALU.is_gt, KH)
        else:
            q2 = qq[1] + "b"
            if st.get("cut", 1) > 1:
                pw = KH // 2
                for a in range(2):
                    o = h * KH + a * pw
                    gtt((T.Q[:, o:o + pw], q2 if a else qq[1]), winR, (T.LM[:, m16[3] + a * pw // 16:m16[3] + (a + 1) * pw // 16], m16[1]),
                        (T.XS[:, o:o + pw], "XS%d_%d" % (h, a)), ALU.mult, pw)
            else:
                gtt(qq, winR, m16, st.get("raw", B), ALU.mult, KH)
                ops[-1]["w"].append(q2)
            up = "raw" in st
            ts(s1, qq, 1.0 if up else -1.0, ALU.is_lt if up else ALU.is_gt, n=KH, f=0.5, r=[q2])
            if way("s2", i) == "v":
                th = thr if up else nthr
                ts(s2, qq, th[0], ALU.is_lt if up else ALU.is_gt, n=KH, f=0.5, r=[th[1], q2])
            else:
                act(s2, qq, ACT.Sign, bias=cf(8)[0], scale=-1.0 if up else 1.0, n=KH, r=["cf8", q2])
                m2 = "M3"
        if par:
            t16, pn = slot("lu"), big("PN", h)
            ts(t16, st["t"], low - CP, ALU.add)
            gact(pn, winX, t16, ACT.Identity, -OFF, 1.0, KH)
            pr = (T[pg][:, LW:LW + JH], pg + "p")
            mm([(pr[0], T.I8[:], T.mh[:], JH)] +
               [(pr[0], T.EP[:, 15 - r:143 - r], T.PN[:, h * KH + r:(h + 1) * KH:16], JH) for r in range(16)],
               ["I8", "mh", "EP", pn[1]], [pr[1]], pg, keep=True)
        if fetch:
            lbuf, lo, ltok = st["L"]
            ru, nh = wide("U2", h, i - 1), slot("lh")
            mn_ = st["M"][1]
            tt(ru, (T[lbuf][:, lo:lo + (i - 1) * JH], ltok), (T[mn_[:2]][:, h * LW + JH:h * LW + i * JH], mn_), ALU.mult, n=(i - 1) * JH, f=1.0)
            ts(nh, st["c1"], 1.5, ALU.is_lt, -1.0, ALU.mult)
            tm = (T[pb][:, 0:JH], pb + "w")
            mm([(tm[0], T.I8[:], T.mh[:], JH), (tm[0], T.I5[:], nh[0], JH)] +
               [(tm[0], T.IH[:], T.U2[:, h * LW + s_ * JH:h * LW + (s_ + 1) * JH], JH) for s_ in range(i - 1)],
               ["I8", "I5", "IH", "mh", nh[1], ru[1]], [tm[1]], pb, keep=True)
        if last:
            mk = mask(h, st["n1"], NL, "MB" if st["M"][1].startswith("MA") else "MA", way("mk", i))
        z = (T[ps][:, 0:JH], ps + "z")
        base = i > 0 and not low
        mm(([(z[0], T.I5[:], T.oh[:], JH)] if base else []) +
           [(z[0], T.EZ[:, 15 - r:143 - r], T.S1[:, h * KH + r:(h + 1) * KH:16], JH) for r in range(16)],
           ["I5", "oh", "EZ", s1[1]], [z[1]], ps)
        mm([(T[pp][:], T.M1[:], s1[0], KH), (T[pp][:], T[m2][:], s2[0], KH)], ["M1", m2, s1[1], s2[1]], [pp + "w"], pp)
        b, nok = slot("lh"), slot("lh")
        x, ix16, ig16 = slot("lf"), m16, slot("lu")
        if i > 0:
            v = slot("lf")
            tt(v, st["t"], z, ALU.subtract, f=1.0, x=[ps])
            if not par:
                ix, ix16 = slot("lf"), slot("lu")
                tt(ix, v, m, ALU.max)
                ts(ix16, ix, -1.0 * CP, ALU.add)
        ts(nok, z, TOP if base else 0.0, ALU.not_equal, BIG, ALU.mult, x=[ps])
        tt(x, m, nok, ALU.subtract)
        if i > 0:
            ig = slot("lf")
            tt(ig, v, x, ALU.max)
            ts(ig16, ig, -1.0 * C, ALU.add)
            if way("fb", i) == "v":
                ts(b, v, CP + C - 0.5, ALU.is_gt)
            else:
                sg = slot("lf")
                act(sg, v, ACT.Sign, bias=0.5 - CP - C)
                act(b, sg, ACT.Relu)
        else:
            ts(ig16, x, -1.0 * C, ALU.add)
        ys = []
        pw = KH // (1 if par else OPT["split"])
        for a in range(0, KH, pw):
            xa = (T.XG[:, h * KH + a:h * KH + a + pw], "XG%d_%d" % (h, a))
            ya = (T.Y[:, h * KH + a:h * KH + a + pw], "Y%d_%d" % (h, a))
            ox = ix16[3] + a // 16
            gact(xa, winX if par or i == 0 else winX2, (T[ix16[2]][:, ox:ox + pw // 16], ix16[1]), ACT.Identity, -0.375, 1.0 / 4096, pw)
            if par:
                ops[-1]["w"] += ["XG%d_%d" % (h, KH // 2)]
            tt(ya, (T[pp][:, a:a + pw], pp + "w"), xa, ALU.min, n=pw, f=1.0, x=[pp])
            if par:
                ops[-1]["r"] += ["XG%d_%d" % (h, KH // 2)]
                ops[-1]["w"] += ["Y%d_%d" % (h, KH // 2)]
                ys.append("Y%d_%d" % (h, KH // 2))
            ys.append(ya[1])
        gg = big("GG", h)
        if leave and OPT["late"] >= 5:
            pw = KH // OPT["np"]
            for a in range(OPT["np"]):
                o = k_ * KH + a * pw
                sb = (T.SB[:, o:o + pw], "SB%d_%d" % (k_, a))
                gtt(sb, winG, (T.lu[:, ig16[3] + a * pw // 16:ig16[3] + (a + 1) * pw // 16], ig16[1]),
                    (T[B[1][:2]][:, h * KH + a * pw:h * KH + (a + 1) * pw], B[1]), ALU.add, pw)
                send(k_, 4 * a, sb[0], T.LB[:, o:o + pw], [sb[1]], "LB%d_%d" % (k_, a), 128 * pw * 2)
        elif leave:
            sg_ = (T.SG[:, k_ * KH:(k_ + 1) * KH], "SG%d" % k_)
            gact(sg_, winG, ig16, ACT.Copy, 0.0, 1.0, KH)
            send(k_, 4, sg_[0], T.LG[:, k_ * KH:(k_ + 1) * KH], [sg_[1]], "LG%d" % k_, 128 * KH * 2)
        else:
            if ahead:
                nb = (T.SB[:, k_ * KH:(k_ + 1) * KH], "SB%d" % k_)
            else:
                nb = big("BC" if B[1].startswith("BA") else "BA", h)
            nw["B"] = nb
            how = way("bv", i) if 0 < i < NL - 1 else "a"
            if how == "g":
                gtt(nb, winG, ig16, B, ALU.add, KH)
            else:
                gact(gg, winG0 if i == 0 else winG, ig16, ACT.Copy, 0.0, -1.0 if i == 0 else 1.0, KH)
            if how == "v":
                tt(nb, B, gg, ALU.add, n=KH, f=1.0)
            elif how == "a":
                one = "IB" if i == 0 else "IH"
                mm([(pbw[0], T[one][:], B[0], KH)], [one, B[1]], [pbw[1]], pb, keep=True)
                mm([(pbw[0], T.IH[:], gg[0], KH)], ["IH", gg[1], pbw[1]], [pbw[1]], pb, cont=True)
                if last:
                    ob = big("OB", h)
                    act(ob, pbw, ACT.Identity, bias=-0.5, scale=-1.0, n=KH, x=[pb])
                    dma("s", T.yb[:, h * KH:(h + 1) * KH], ob[0], [ob[1]], [], 128 * KH * 4)
                elif i == 0:
                    act(nb, pbw, ACT.Identity, bias=-0.5, scale=-1.0, n=KH, x=[pb])
                else:
                    act(nb, pbw, ACT.Copy, n=KH, x=[pb])
            if ahead:
                send(k_, 0, nb[0], T.LB[:, k_ * KH:(k_ + 1) * KH], [nb[1]], "LB%d" % k_, 128 * KH * 2)
        c1, n1 = (spart(1), spart(2)) if leave else (slot("lh"), slot("lh"))
        nw["c1"], nw["n1"] = c1, n1
        lbuf, lo, ltok = st["L"]
        lsb = (T[lbuf][:, lo:lo + (i + 1) * JH], ltok)
        if i == 0:
            act(c1, nok, ACT.Relu, bias=1.0, scale=-1.0)
            act(n1, c1, ACT.Identity, bias=1.0)
            act(lsb, c1, ACT.Identity, bias=-OFF - 1.0, scale=OFF + 1.0)
            nw["M"], nw["t"] = c1, x
        else:
            cb, nk = slot("lh"), slot("lh")
            add("v", lambda: V.tensor_tensor(pair(cb), pair(st["c1"]), pair(b), ALU.subtract), 64 * CY,
                [st["c1"][1], st["n1"][1], b[1], nok[1]], [cb[1], nk[1]])
            tt(c1, cb, nk, ALU.max)
            if last:
                act((T.OC[:, h * JH:(h + 1) * JH], "OC%d" % h), c1, ACT.Identity, bias=-1.0)
            else:
                ok, has = slot("lh"), slot("lh")
                act(ok, nok, ACT.Relu, bias=1.0, scale=-1.0)
                tt(n1, st["n1"], ok, ALU.add)
                if not fetch:
                    act(has, c1, ACT.Sign)
            mb, bb, tb = slot("lf"), slot("lf"), slot("lf")
            tt(mb, b, m, ALU.mult)
            if par:
                act(bb, b, ACT.Identity, bias=low - TOP, scale=-BIG)
            else:
                act(bb, b, ACT.Identity, bias=low - CP, scale=BIG)
            tt(tb, st["t"], bb, ALU.add)
            mo = st["M"]
            if not last:
                mk = mask(h, c1, i + 1, "MB" if mo[1].startswith("MA") else "MA", way("mk", i))
            nw["M"] = mk
        L = pg + "w"
        n_ = (i + 1) * JH

        def put(vn):
            u = wide("U", h, i)
            if way("gu", i) == "g":
                gtt(u, (vn[0], [vn[1]]), (T.BO[:, 0:2 * i], "BO"), mo, ALU.mult, i * JH)
            else:
                spread(pp, 0, vn, i)
                tt(u, (T[pp][:, 0:i * JH], pp + "w"), mo, ALU.mult, n=i * JH, f=1.0, x=[pp])
            return u

        def log(vn):
            u = put(vn)
            lw = T[pg][:, 0:n_]
            mm([(lw, T.IH[:], lsb[0], n_)], ["IH", ltok, ltok + "e"], [L], pg, keep=True)
            mm([(T[pg][:, 0:i * JH], T.IH[:], u[0], i * JH)], ["IH", u[1], L], [L], pg, cont=True)
            rr = wide("RR", h, i + 1)
            tt(rr, (lw, L), mk, ALU.mult, n=n_, f=1.0, x=[pg])
            return u, rr

        def take(u, rr):
            if not fetch:
                tsum = (T[pg][:, LW + JH:LW + 2 * JH], pg + "t")
                mm([(tsum[0], T.I5[:], has[0], JH)] +
                   [(tsum[0], T.IH[:], T.RR[:, h * LW + s_ * JH:h * LW + (s_ + 1) * JH], JH) for s_ in range(i + 1)],
                   ["IH", "I5", rr[1], has[1]], [tsum[1]], pg)
                t = slot("lf")
                tt(t, tsum, x, ALU.max, f=1.0, x=[pg])
                nw["t"] = t
            lw = T[pg][:, 0:n_]
            lx = (T.SL[:, k_ * LW:k_ * LW + n_], "SL%d" % k_) if leave else lsb
            if way("lu", i) == "v":
                tt(lx, (lw, L), rr, ALU.subtract, n=n_, f=1.0, x=[pg])
            else:
                mm([(lw, T.IH[:], lsb[0], n_), (T[pg][:, 0:i * JH], T.IH[:], u[0], i * JH), (lw, T.NH[:], rr[0], n_)],
                   ["IH", "NH", ltok, ltok + "e", u[1], rr[1]], [L], pg)
                act(lx, (lw, L), ACT.Copy, n=n_, x=[pg])
            if leave:
                if not fetch:
                    act(spart(3), t, ACT.Identity, bias=-TOP)
                    wall(t, 0.0)
                send(k_, 2, lx[0], T.LL[:, k_ * LW:k_ * LW + n_], [lx[1]], "LX%d" % k_, 128 * n_ * 2)

        def wall(t, up):
            ti, j_, nz = slot("li"), slot("li"), slot("lf")
            ts(ti, t, up, ALU.add, float(K), ALU.mult)
            ts(j_, ti, K, ALU.bitwise_and)
            act(nz, c1, ACT.Relu, bias=2.0 * K, scale=-2.0 * K)
            tt(spart(0), j_, nz, ALU.max)
            o = 4 * k_ * JH
            send(k_, 3, T.SJ[:, o:o + 4 * JH], T.LJ[:, o:o + 4 * JH], [spart(j)[1] for j in range(4)], "LJ%d" % k_, 128 * 4 * JH * 2)

        if fetch:
            mm([(tm[0], T.I8[:], b[0], JH)], ["I8", b[1], tm[1]], [tm[1]], pb, cont=True)
            okb, xc, t2, t3 = slot("lf"), slot("lf"), slot("lf"), slot("lf")
            act(okb, nok, ACT.Relu, bias=BIG, scale=-1.0)
            act(xc, x, ACT.Identity, bias=-TOP)
            tt(t2, tb, okb, ALU.subtract)
            tt(t3, t2, xc, ALU.max)
            tt(spart(3), tm, t3, ALU.max, f=1.0, x=[pb])
            wall(spart(3), TOP)
        if par:
            mm([(pr[0], T.I8[:], b[0], JH)], ["I8", b[1], pr[1]], [pr[1]], pg, cont=True)
            vn = slot("lf" if way("gu", i) == "g" else "lh")
            tt(vn, pr, tb, ALU.max, f=1.0, x=[pg])
            if last:
                mc = slot("lf")
                ts(mc, x, -TOP, ALU.add, -OFF - 1.0, ALU.max)
                u = put(vn)
                u2 = wide("U2", h, NL)
                gtt(u2, (mc[0], [mc[1]]), whole("BO"), mk, ALU.mult, LW)
                lw = T[pg][:, 0:LW]
                mm([(lw, T.IH[:], lsb[0], LW), (lw, T.IH[:], T.COFF[:], LW), (lw, T.IK[:], mk[0], LW)],
                   ["IH", "IK", "COFF", ltok, ltok + "e", mk[1]], [L], pg, keep=True)
                mm([(T[pg][:, 0:i * JH], T.IH[:], u[0], i * JH), (lw, T.IH[:], u2[0], LW)], ["IH", u[1], u2[1], L], [L], pg, cont=True)
                act((T.OL[:, :, h * JH:(h + 1) * JH], "OL%d" % h), (lw, L), ACT.Copy, n=LW, x=[pg])
            else:
                u, rr = log(vn)
        rs = (T[ps][:, JH:2 * JH], ps + "r")
        mm(([(rs[0], T.IP[:], b[0], JH)] if i > 0 else []) +
           [(rs[0], T.ER[:, 15 - r:143 - r], T.Y[:, h * KH + r:(h + 1) * KH:16], JH) for r in range(16)],
           ["ER", "IP"] + ys + ([b[1]] if i > 0 else []), [rs[1]], ps)
        ri, r_ = slot("li"), slot("li")
        ts(ri, rs, 16777216.0 - BIG + CP - 2560.0, ALU.add, x=[ps])
        ts(r_, ri, 8191, ALU.bitwise_and)
        if i == 0:
            mn = r_
        else:
            mn = slot("lf")
            tt(mn, r_, mb, ALU.max)
        nw["m"] = mn
        if last:
            ts((T.OM[:, h * JH:(h + 1) * JH], "OM%d" % h), mn, -1.0 * CP, ALU.add)
            return nw
        nw["m16"] = slot("lu")
        ts(nw["m16"], mn, -1.0 * CP, ALU.add)
        if leave:
            send(k_, 1, nw["m16"][0], T.LM[:, k_ * JH:(k_ + 1) * JH], [nw["m16"][1]], "LM%d" % k_, 128 * JH * 2)
        if i > 0 and not par:
            vn, vc = slot("lf"), slot("lf" if way("gu", i) == "g" else "lh")
            tt(vn, r_, tb, ALU.min)
            if way("cen", i) == "v":
                ts(vc, vn, -OFF, ALU.add)
            else:
                act(vc, vn, ACT.Identity, bias=-OFF)
            u, rr = log(vc)
        if i > 0:
            take(u, rr)
        return nw

    sts = []
    for h in range(H):
        cur[0] = h
        sts.append(first(h))
    for i in range(NL):
        for h in range(H):
            cur[0], cur[1] = h, i
            if i > 0 and i % NS == 0:
                sts[h] = arrive(i // NS, h, sts[h])
            sts[h] = step(i, h, sts[h])
    dma("s", T.ym[:], T.OM[:], ["OM0", "OM1"], [], 128 * 256)
    dma("a", T.yc[:], T.OC[:], ["OC0", "OC1"], [], 128 * 256)
    dma("s", T.yl[:, 0:384], T.OL[:, 0:6], ["OL0", "OL1"], [], 128 * 384 * 4)
    dma("a", T.yl[:, 384:768], T.OL[:, 6:12], ["OL0", "OL1"], [], 128 * 384 * 4)
    return ops, nsend * len([op for op in ops if op["kind"] == "s"])


def depend(ops):
    lastw, readers, lastx = {}, {}, {}
    for i, op in enumerate(ops):
        pre = {}

        def edge(j, data):
            if j == i:
                return
            pj = ops[j]
            need = pj["eng"] != op["eng"] or pj["kind"] in ("d", "r") or (data and op["eng"] != "p")
            if pj["kind"] == "s":
                need = False
            pre[j] = pre.get(j, False) or need
        for n in op["r"]:
            if n in lastw:
                edge(lastw[n], True)
        for n in op["w"]:
            if n in lastw:
                edge(lastw[n], True)
            for j in readers.get(n, []):
                edge(j, True)
        for n in op["x"]:
            if n in lastx:
                edge(lastx[n], False)
            lastx[n] = i
        for n in op["r"]:
            readers.setdefault(n, []).append(i)
        for n in op["w"]:
            lastw[n] = i
            readers[n] = []
        op["pre"] = pre


def order(ops):
    n = len(ops)
    succ = [[] for _ in range(n)]
    for i, op in enumerate(ops):
        for j in op["pre"]:
            succ[j].append(i)

    def gap(j, i):
        if not ops[i]["pre"][j]:
            return ops[j]["lat"]
        return ops[j]["lat"] + (OWN if ops[j]["eng"] == ops[i]["eng"] else HOP)
    prio = [0.0] * n
    for i in range(n - 1, -1, -1):
        d = ops[i].get("bytes", 0) / 250e3
        prio[i] = ops[i]["cost"] + d + max([ops[i]["lat"]] + [gap(i, s) + prio[s] for s in succ[i]])
    x = OPT["seed"] * 7919 + 1
    for i in range(n):
        x = (x * 1103515245 + 12345) % 2147483648
        prio[i] += OPT["jit"] * x / 2147483648.0
        if ops[i]["h"] == 0:
            prio[i] += OPT["lead"] if ops[i]["i"] < OPT["turn"] else OPT["lead2"]
    left = [len(op["pre"]) for op in ops]
    rdy = [0.0] * n
    for i in range(n):
        if ops[i]["w"] == ["XG1_0"]:
            rdy[i] = OPT["hold"]
            break
    ready = [i for i in range(n) if left[i] == 0]
    free = {}
    dfree = [0.0]
    seq = []
    end = 0.0
    while ready:
        st = [max(rdy[i], free.get(ops[i]["eng"], 0.0)) for i in ready]
        t0 = min(st)
        e0 = ops[ready[st.index(t0)]]["eng"]
        cand = [i for i, s in zip(ready, st) if ops[i]["eng"] == e0 and s <= t0 + OPT["win"]]
        if ops[cand[0]]["kind"] == "d" and not ops[cand[0]]["r"]:
            i = min(cand)
        else:
            i = max(cand, key=lambda q: prio[q] - OPT["lam"] * max(0.0, rdy[q] - t0))
        s = max(rdy[i], free.get(e0, 0.0))
        f = s + ops[i]["cost"]
        free[e0] = f
        if ops[i]["kind"] == "d":
            dfree[0] = max(dfree[0], f) + ops[i]["bytes"] / 250e3
            f = dfree[0]
        ops[i]["t"] = (s, f)
        end = max(end, f + ops[i]["lat"])
        ready.remove(i)
        seq.append(i)
        for q in succ[i]:
            rdy[q] = max(rdy[q], f + gap(i, q))
            left[q] -= 1
            if left[q] == 0:
                ready.append(q)
    return seq, end


def clear(a, b, s, d):
    lo, hi = 0, len(b)
    while lo < hi:
        mid = (lo + hi) // 2
        if b[mid] <= s:
            lo = mid + 1
        else:
            hi = mid
    while lo < len(a) and a[lo] < s + d - 1e-9:
        s = max(s, b[lo])
        lo += 1
    return s, lo


def justify(ops, paces):
    n = len(ops)
    gr, pc, hop, own, net = OPT["pace"]
    c = costs(ops, gr, pc)
    res = ["D" if o["kind"] == "d" else o["eng"] for o in ops]
    dur = [c[i] + o.get("bytes", 0) / 250e3 for i, o in enumerate(ops)]
    pre = [[(j, ops[j]["lat"] * (net if ops[j]["kind"] == "r" else 1.0) + ((own if ops[j]["eng"] == o["eng"] else hop) if need else 0.0))
            for j, need in o["pre"].items()] for o in ops]
    suc = [[] for _ in range(n)]
    for i in range(n):
        for j, l in pre[i]:
            suc[j].append((i, l))
    tail = [o["lat"] if o["kind"] == "d" else 0.0 for o in ops]

    def sweep(seq, edges, first):
        st, fin, span = [0.0] * n, [0.0] * n, {}
        for i in seq:
            s = first[i]
            for j, l in edges[i]:
                if fin[j] + l > s:
                    s = fin[j] + l
            if dur[i] > 0:
                a, b = span.setdefault(res[i], ([], []))
                s, k = clear(a, b, s, dur[i])
                a.insert(k, s)
                b.insert(k, s + dur[i])
            st[i], fin[i] = s, s + dur[i]
        return st, fin

    def topo_sort(key, edges, back):
        k2 = list(key)
        for i in (range(n - 1, -1, -1) if back else range(n)):
            for j, _l in edges[i]:
                if k2[j] >= k2[i]:
                    k2[i] = k2[j] + 1e-7
        return sorted(range(n), key=lambda i: k2[i])
    far = [0.0] * n
    for i in range(n - 1, -1, -1):
        far[i] = dur[i] + max([tail[i]] + [l + far[s] for s, l in suc[i]])
    key = [-far[i] - (OPT["lead"] if ops[i]["h"] == 0 else 0.0) for i in range(n)]
    zero = [0.0] * n
    loads = [i for i, o in enumerate(ops) if o["kind"] == "d" and not o["pre"]]
    lands = [i for i, o in enumerate(ops) if o["kind"] == "r"]
    x = OPT["seed"] * 7919 + 1
    best, bseq, bkey = 1e9, None, key
    run = runner(ops, paces)
    for it in range(OPT["sweeps"]):
        if it % OPT["again"] == 0 and it:
            key = []
            for i in range(n):
                x = (x * 1103515245 + 12345) % 2147483648
                key.append(bkey[i] + OPT["jit"] * x / 2147483648.0)
        for i in loads:
            key[i] = i - 1e6
        st, fin = sweep(topo_sort(key, pre, False), pre, zero)
        for i in loads:
            st[i] = i - 1e6
        for i in lands:
            st[i] = 0.0
        seq = topo_sort(st, pre, False)
        t = run(seq)
        if t < best:
            best, bseq, bkey = t, seq, st
        _s, back = sweep(topo_sort([-f for f in fin], suc, True), suc, tail)
        key = [-f for f in back]
    return bseq


def runner(ops, paces):
    n = len(ops)
    tabs = []
    for gr, pc, hop, own, net in paces:
        pr = [[(j, ops[j]["lat"] * (net if ops[j]["kind"] == "r" else 1.0) +
                ((own if ops[j]["eng"] == o["eng"] else hop) if need else 0.0)) for j, need in o["pre"].items()] for o in ops]
        tabs.append((costs(ops, gr, pc), pr))
    eng = [o["eng"] for o in ops]
    dm = [o.get("bytes", 0) / 250e3 for o in ops]
    lat = [o["lat"] for o in ops]

    def run(sq):
        total = 0.0
        for c, pr in tabs:
            fin = [0.0] * n
            free = {}
            dfree = end = 0.0
            for i in sq:
                s = free.get(eng[i], 0.0)
                for j, l in pr[i]:
                    if fin[j] + l > s:
                        s = fin[j] + l
                f = s + c[i]
                free[eng[i]] = f
                if dm[i]:
                    dfree = max(dfree, f) + dm[i]
                    f = dfree
                fin[i] = f
                if f + lat[i] > end:
                    end = f + lat[i]
            total += end
        return total
    return run


def costs(ops, gr, pc):
    return [(0.06 + o["gn"] * gr * CY) * pc if o.get("gn") else o["cost"] * pc if o["eng"] in "vap" and o["kind"] == "c" else o["cost"]
            for o in ops]


def polish(ops, seq, rounds, paces):
    n = len(ops)
    tabs = []
    for gr, pc, hop, own, net in paces:
        c = costs(ops, gr, pc)
        pr = [[(j, ops[j]["lat"] * (net if ops[j]["kind"] == "r" else 1.0) +
                ((own if ops[j]["eng"] == o["eng"] else hop) if need else 0.0)) for j, need in o["pre"].items()] for o in ops]
        tabs.append((c, pr))
    eng = [o["eng"] for o in ops]
    dm = [o.get("bytes", 0) / 250e3 for o in ops]
    lat = [o["lat"] for o in ops]

    def run(sq, tab, trace=False):
        c, pr = tab
        fin = [0.0] * n
        why = [-1] * n
        free = {}
        dfree = 0.0
        end, last = 0.0, -1
        for i in sq:
            s, w = free.get(eng[i], (0.0, -1))
            if w >= 0:
                w = -2 - w
            for j, l in pr[i]:
                t = fin[j] + l
                if t > s:
                    s, w = t, j
            f = s + c[i]
            free[eng[i]] = (f, i)
            if dm[i]:
                dfree = max(dfree, f) + dm[i]
                f = dfree
            fin[i] = f
            why[i] = w
            if f + lat[i] > end:
                end, last = f + lat[i], i
        if not trace:
            return end
        pairs = []
        while last != -1:
            w = why[last]
            if w <= -2:
                w = -2 - w
                if w not in ops[last]["pre"] and not dm[w]:
                    pairs.append((w, last))
            last = w
        return pairs
    best = sum(run(seq, t) for t in tabs)
    x = 1
    pairs = []
    for _ in range(rounds):
        x = (x * 1103515245 + 12345) % 2147483648
        if not pairs:
            pairs = run(seq, tabs[(x >> 8) % len(tabs)], True)
            if not pairs:
                continue
        a, b = pairs.pop((x >> 8) % len(pairs))
        pa, pb = seq.index(a), seq.index(b)
        if pa > pb:
            continue
        need = {b}
        for q in range(pb - 1, pa - 1, -1):
            k = seq[q]
            if any(k in ops[m]["pre"] for m in need) or (eng[k] != eng[a] and any(eng[m] == eng[k] for m in need)):
                need.add(k)
        if a in need:
            continue
        mid = seq[pa:pb + 1]
        new = seq[:pa] + [k for k in mid if k in need] + [k for k in mid if k not in need] + seq[pb + 1:]
        t = sum(run(new, tb) for tb in tabs)
        if t <= best + 1e-9:
            if t < best - 1e-9:
                pairs = []
            best, seq = t, new
    return seq


PACES = [(1.56, 0.85, 0.4, 0.12, 1.0), (1.3, 1.0, 0.33, 0.12, 1.3), (1.9, 1.1, 0.25, 0.09, 1.0)]
ORDER = {}


def rank_program(g, core, T, topo):
    rank = T.rank_of(core)
    if rank is None:
        return
    ops, sent = build(g, T, topo, core, rank)
    depend(ops)
    if len(ops) not in ORDER:
        ORDER[len(ops)] = polish(ops, justify(ops, PACES), OPT["rounds"], PACES)
    seq = ORDER[len(ops)]
    queue = {"v": g.vector, "a": g.scalar, "p": g.tensor, "g": g, "s": g.sync}
    count = {}
    for i in seq:
        op = ops[i]
        if op["kind"] == "c":
            op["sem"] = "c" + op["eng"]
            count[op["sem"]] = count.get(op["sem"], 0) + 1
            op["cnt"] = count[op["sem"]]
        elif op["kind"] in ("d", "r"):
            count[op["sem"]] = op["cnt"]
    seen = {}
    for i in seq:
        op = ops[i]
        if op["kind"] == "r":
            continue
        q = queue[op["eng"]]
        want = {}
        for j, need in op["pre"].items():
            if need:
                want[ops[j]["sem"]] = max(want.get(ops[j]["sem"], 0), ops[j]["cnt"])
        for s, c in want.items():
            if seen.get((op["eng"], s), 0) < c:
                q.wait_ge(T.sem[s], c)
                seen[(op["eng"], s)] = c
        ins = op["fn"]()
        if op["kind"] == "c":
            ins.then_inc(T.sem[op["sem"]], 1)
        elif op["kind"] == "d":
            ins.then_inc(T.sem[op["sem"]], 16)
    count["sent"] = sent
    for s, c in count.items():
        if max([seen.get((e, s), 0) for e in queue]) < c:
            g.wait_ge(T.sem[s], c)
